import numpy as np
import ml_dtypes


def mxq(x, axis, fmt="e4m3"):
    dtype, down = {"e4m3": (ml_dtypes.float8_e4m3fn, 7), "e5m2": (ml_dtypes.float8_e5m2, 14)}[fmt]
    v = np.moveaxis(np.asarray(x, np.float32).astype(ml_dtypes.bfloat16).astype(np.float64), axis, -1)
    blocks = v.reshape(v.shape[:-1] + (-1, 32))
    amax = np.abs(blocks).max(-1, keepdims=True)
    byte = np.maximum(np.where(amax > 0, np.frexp(amax)[1] - 1 + 127, 0) - down, 1)
    scale = np.exp2(byte - 127.0)
    codes = (blocks / scale).astype(np.float32).astype(dtype).astype(np.float64)
    return np.moveaxis((codes * scale).reshape(v.shape), -1, axis)


WIDE = False


def mx_kscale(k):
    if not WIDE:
        return np.ones(k)
    levels = np.array([24, -24, 12, -12, 0])
    if k % 512:
        return np.exp2(np.random.permutation(np.resize(levels, k // 32))).repeat(32)
    a = np.empty((k // 512, 16))
    for p in range(k // 512):
        a[p, :8] = np.random.permutation(np.resize(levels, 8))
        for g in range(8):
            far = levels[np.abs(levels - a[p, g]) >= 10]
            a[p, g + 8] = far[np.random.randint(len(far))]
    return np.exp2(a.ravel()).repeat(32)


def f64(x):
    return np.asarray(x).astype(np.float64)


def striped(idx):
    return np.tile(idx.reshape(-1, 16).T, (8, 1)).astype(np.uint16)


def unstriped(offs):
    return offs[:16].T.reshape(-1).astype(np.int64)


E2M1 = np.array([0.0, 0.5, 1.0, 1.5, 2.0, 3.0, 4.0, 6.0, -0.0, -0.5, -1.0, -1.5, -2.0, -3.0, -4.0, -6.0])


def pack_weight(w, fmt):
    k, n = w.shape
    w = f64(np.asarray(w, np.float32).astype(ml_dtypes.bfloat16)).reshape(k // 32, 32, n)
    amax = np.abs(w).max(1)
    if fmt == "e4m3":
        byte = np.frexp(amax)[1] - 1 + 127 - 7
    else:
        mant, ex = np.frexp(amax / 6.0)
        byte = np.where(mant > 0.5, ex, ex - 1) + 127
    byte = np.clip(np.where(amax > 0, byte, 1), 1, 254)
    scaled = (w * np.exp2(127.0 - byte)[:, None, :]).reshape(k, n).astype(np.float32)
    by_word = np.ascontiguousarray(scaled.reshape(k // 512, 128, 4, n).transpose(0, 1, 3, 2))
    if fmt == "e4m3":
        words = by_word.astype(ml_dtypes.float8_e4m3fn).view(np.uint8)
    else:
        c = by_word.astype(ml_dtypes.float4_e2m1fn).view(np.uint8) & 0xF
        words = (c[..., 0::2] | (c[..., 1::2] << 4)).reshape(k // 512, 128, 2 * n)
    return np.ascontiguousarray(words), np.ascontiguousarray(byte.astype(np.uint8).reshape(k // 512, 16, n))


def unpack_weight(words, scales, fmt):
    g, _, n = scales.shape
    words = np.ascontiguousarray(words).reshape(g, 128, n, -1)
    if fmt == "e4m3":
        vals = words.view(ml_dtypes.float8_e4m3fn).astype(np.float64)
    else:
        nib = np.empty((g, 128, n, 4), np.uint8)
        nib[..., 0::2] = words & 0xF
        nib[..., 1::2] = words >> 4
        vals = E2M1[nib]
    vals = vals * np.repeat(np.exp2(scales.astype(np.float64) - 127.0), 8, axis=1)[..., None]
    return vals.transpose(0, 1, 3, 2).reshape(g * 512, n)


def sigm(f):
    return 1.0 / (1.0 + np.exp(-np.maximum(f, -700.0)))


K, L, R, N, T, J = 512, 512, 512, 256, 4096, 2048


def setup_inputs():
    n = np.random.standard_normal
    s = mx_kscale(K)[:, None]
    s2 = mx_kscale(L)[:, None]
    u = mx_kscale(R)[:, None]
    p_tab = pack_weight(n((K, T)) * s, "e4m3")
    p_tab2 = pack_weight(n((L, T)) * s2, "e4m3")
    p_wer = pack_weight(n((K, R)) / np.sqrt(K) / s * u.T, "e2m1")
    p_wei = pack_weight(n((K, R)) / np.sqrt(K) / s * u.T, "e2m1")
    p_wrr = pack_weight(n((L, R)) / np.sqrt(L) / s2, "e4m3")
    p_wri = pack_weight(n((L, R)) / np.sqrt(L) / s2, "e4m3")
    p_nr = pack_weight(n((R, N)) / np.sqrt(R) / u, "e2m1")
    p_ni = pack_weight(n((R, N)) / np.sqrt(R) / u, "e2m1")
    return {
        "tab_words": p_tab[0],
        "tab_scales": p_tab[1],
        "tab2_words": p_tab2[0],
        "tab2_scales": p_tab2[1],
        "wer_words": p_wer[0],
        "wer_scales": p_wer[1],
        "wei_words": p_wei[0],
        "wei_scales": p_wei[1],
        "wrr_words": p_wrr[0],
        "wrr_scales": p_wrr[1],
        "wri_words": p_wri[0],
        "wri_scales": p_wri[1],
        "nr_words": p_nr[0],
        "nr_scales": p_nr[1],
        "ni_words": p_ni[0],
        "ni_scales": p_ni[1],
        "offs": striped(np.random.permutation(T)[:J]),
        "offs2": striped(np.random.permutation(T)[:J]),
    }


def reference(tab_words, tab_scales, tab2_words, tab2_scales, wer_words, wer_scales, wei_words, wei_scales, wrr_words, wrr_scales, wri_words, wri_scales, nr_words, nr_scales, ni_words, ni_scales, offs, offs2):
    idx = unstriped(offs)
    idx2 = unstriped(offs2)
    tab_ = unpack_weight(tab_words, tab_scales, "e4m3")[:, idx]
    tab2_ = unpack_weight(tab2_words, tab2_scales, "e4m3")[:, idx2]
    wer_ = unpack_weight(wer_words, wer_scales, "e2m1")
    aer = wer_.T @ tab_
    wei_ = unpack_weight(wei_words, wei_scales, "e2m1")
    aei = wei_.T @ tab_
    wrr_ = unpack_weight(wrr_words, wrr_scales, "e4m3")
    arr = wrr_.T @ tab2_
    wri_ = unpack_weight(wri_words, wri_scales, "e4m3")
    ari = wri_.T @ tab2_
    hr = aer * arr - aei * ari
    hi = aer * ari + aei * arr
    hr_ = mxq(hr, 0, "e4m3")
    hi_ = mxq(hi, 0, "e4m3")
    nr_ = unpack_weight(nr_words, nr_scales, "e2m1")
    ni_ = unpack_weight(ni_words, ni_scales, "e2m1")
    y = nr_.T @ hr_ + ni_.T @ hi_
    return sigm(y)

@@ -1,0 +1,214 @@
+from contextlib import ExitStack
+
+import concourse.mybir as mybir
+from concourse.masks import make_identity
+
+K, L, R, N, T, J = 512, 512, 512, 256, 4096, 2048
+FLOPS = 5368709120
+
+F32 = mybir.dt.float32
+BF16 = mybir.dt.bfloat16
+I32 = mybir.dt.int32
+U32 = mybir.dt.uint32
+U16 = mybir.dt.uint16
+U8 = mybir.dt.uint8
+FP8X4 = mybir.dt.float8_e4m3fn_x4
+FP4X4 = mybir.dt.float4_e2m1fn_x4
+MULT = mybir.AluOpType.mult
+SIGMOID = mybir.ActivationFunctionType.Sigmoid
+
+P = 128
+PACK = 4
+CHUNK = 512
+TILE = 128
+CHUNKS = J // CHUNK
+TILES = J // TILE
+TILES_PER_CHUNK = CHUNK // TILE
+TABLE_PIECES = 4
+POOL_TILES = ()
+SCORE_GROUPS = ((0, 4), (4, 4), (8, 4), (12, 1), (13, 1), (14, 1), (15, 1))
+TURN_LAG = 1
+SCORE_LAG = 3
+
+
+def tile_list_ckg_sig_kernel(
+    tc, tab_words, tab_scales, tab2_words, tab2_scales, wer_words, wer_scales, wei_words, wei_scales,
+    wrr_words, wrr_scales, wri_words, wri_scales, nr_words, nr_scales, ni_words, ni_scales, offs, offs2, out,
+):
+    nc = tc.nc
+    with ExitStack() as ctx:
+        keep = ctx.enter_context(tc.tile_pool(name="keep", bufs=1))
+        ring = ctx.enter_context(tc.tile_pool(name="ring", bufs=2))
+        psum = ctx.enter_context(tc.psum_pool(name="psum", bufs=2))
+
+        list_e = keep.tile([P, J // 16], U16, name="list_e")
+        list_r = keep.tile([P, J // 16], U16, name="list_r")
+        tab_e = keep.tile([P, T], I32, name="tab_e", align_bytes=64)
+        tab_r = keep.tile([P, T], I32, name="tab_r", align_bytes=64)
+        tabs_e = keep.tile([P, T // 4], I32, name="tabs_e", align_bytes=64)
+        tabs_r = keep.tile([P, T // 4], I32, name="tabs_r", align_bytes=64)
+        planes = keep.tile([P, (4 * R + 2 * N) // 4], I32, name="planes", align_bytes=64)
+        ident = keep.tile([P, P], F32, name="ident", align_bytes=64)
+
+        nc.vector.memset(tabs_r[:], 0)
+        nc.vector.memset(planes[:], 0)
+        nc.vector.memset(tabs_e[:], 0)
+        make_identity(nc, ident[:])
+
+        def plane_loads(plane, scales):
+            rows = scales[0].bitcast(I32)
+            return [(plane[r:P:32, :], rows[r:16:4, :]) for r in range(4)]
+
+        def table_loads(table, words):
+            flat = words[0].rearrange("p t i -> p (t i)").bitcast(I32)
+            step = T // TABLE_PIECES
+            return [(table[:, c * step : (c + 1) * step], flat[:, c * step : (c + 1) * step]) for c in range(TABLE_PIECES)]
+
+        def weight(name, flat_words, scales, first, columns):
+            codes = keep.tile([P, flat_words.shape[1]], U8, name=name, align_bytes=64)
+            plane = planes[:, first // 4 : (first + columns) // 4]
+            return codes, plane.bitcast(U8), (codes[:].bitcast(I32), flat_words.bitcast(I32)), plane_loads(plane, scales)
+
+        wrr = weight("wrr", wrr_words[0].rearrange("p r i -> p (r i)"), wrr_scales, 0, R)
+        wri = weight("wri", wri_words[0].rearrange("p r i -> p (r i)"), wri_scales, R, R)
+        wer = weight("wer", wer_words[0], wer_scales, 2 * R, R)
+        wei = weight("wei", wei_words[0], wei_scales, 3 * R, R)
+        nr = weight("nr", nr_words[0], nr_scales, 4 * R, N)
+        ni = weight("ni", ni_words[0], ni_scales, 4 * R + N, N)
+
+        def weave(big, small):
+            each = -(-len(small) // len(big))
+            order = []
+            for n, piece in enumerate(big):
+                order.append(piece)
+                order.extend(small[n * each : (n + 1) * each])
+            return order
+
+        loads = [(list_r[:], offs2)] + plane_loads(tabs_r, tab2_scales)
+        loads += weave(table_loads(tab_r, tab2_words), wrr[3] + wri[3] + [(list_e[:], offs), wrr[2], wri[2]])
+        loads += weave(table_loads(tab_e, tab_words), plane_loads(tabs_e, tab_scales) + wer[3] + wei[3])
+        loads += [wer[2], wei[2], nr[2], ni[2]] + nr[3] + ni[3]
+        for dst, src in loads:
+            nc.sync.dma_start(out=dst, in_=src)
+
+        def gather(name, window, offsets, c, dtype):
+            picked = keep.tile([P, CHUNK], dtype, name=name + str(c), align_bytes=64)
+            columns = slice(c * CHUNK // 16, (c + 1) * CHUNK // 16)
+            nc.vector.tensor_copy(picked[:], window[:].bitcast(dtype).indirect(offsets[:, columns]))
+            return picked
+
+        sources = (
+            ("scales_r", tabs_r, list_r, U8), ("codes_r", tab_r, list_r, U32),
+            ("scales_e", tabs_e, list_e, U8), ("codes_e", tab_e, list_e, U32),
+        )
+        picked = {}
+
+        def gather_part(c, k):
+            name, window, offsets, dtype = sources[k]
+            picked[name, c] = gather(name, window, offsets, c, dtype)
+
+        def project(tag, bufs, side, i, w, fmt):
+            c, k = divmod(i, TILES_PER_CHUNK)
+            cols = slice(k * TILE, (k + 1) * TILE)
+            acc = psum.tile([P, R], F32, name=tag, tag=tag, bufs=bufs)
+            nc.tensor.matmul_mx(
+                out=acc[:], lhsT=picked["codes_" + side, c][:, cols].bitcast(FP8X4),
+                lhsT_scale=picked["scales_" + side, c][:, cols],
+                rhs=w[0][:].bitcast(fmt), rhs_scale=w[1], start=True, stop=True,
+            )
+            return acc[:].rearrange("p (m t) -> p t m", t=PACK)
+
+        def relation(i):
+            rel = ring.tile([P, 2, PACK, TILE], F32, name="rel", bufs=16, align_bytes=64)
+            nc.scalar.copy(rel[:, 0], project("rel_acc", 2, "r", i, wrr, FP8X4))
+            nc.scalar.copy(rel[:, 1], project("rel_acc", 2, "r", i, wri, FP8X4))
+            return rel
+
+        def products(i, rel):
+            prod = ring.tile([P, 4, PACK, TILE], F32, name="prod", bufs=3, align_bytes=64)
+            aer = project("ent_acc", 3, "e", i, wer, FP4X4)
+            aei = project("ent_acc", 3, "e", i, wei, FP4X4)
+            if i in POOL_TILES:
+                ent = ring.tile([P, PACK, TILE], F32, name="ent", bufs=2, align_bytes=64)
+                nc.scalar.copy(ent[:], aer)
+                nc.gpsimd.tensor_tensor(prod[:, 0], ent[:], rel[:, 0], MULT)
+                nc.gpsimd.tensor_tensor(prod[:, 2], ent[:], rel[:, 1], MULT)
+                nc.vector.scalar_tensor_tensor(prod[:, 1], aei, -1.0, rel[:, 1], MULT, MULT)
+                nc.vector.tensor_tensor(prod[:, 3], aei, rel[:, 0], MULT)
+            elif i == TILES - 1:
+                nc.vector.tensor_tensor(prod[:, 0], aer, rel[:, 0], MULT)
+                nc.vector.scalar_tensor_tensor(prod[:, 1], aei, -1.0, rel[:, 1], MULT, MULT)
+                nc.vector.tensor_tensor(prod[:, 2], aer, rel[:, 1], MULT)
+                nc.vector.tensor_tensor(prod[:, 3], aei, rel[:, 0], MULT)
+            else:
+                nc.vector.tensor_tensor(prod[:, 0], aer, rel[:, 0], MULT)
+                nc.vector.tensor_tensor(prod[:, 2], aer, rel[:, 1], MULT)
+                nc.vector.scalar_tensor_tensor(prod[:, 1], aei, -1.0, rel[:, 1], MULT, MULT)
+                nc.vector.tensor_tensor(prod[:, 3], aei, rel[:, 0], MULT)
+            return prod
+
+        group_of = {}
+        for first, count in SCORE_GROUPS:
+            for i in range(first, first + count):
+                group_of[i] = (first, count)
+        h_bf = {}
+
+        def turn(i, prod):
+            first, count = group_of[i]
+            if i == first:
+                h_bf[first] = ring.tile([P, 2, count * TILE, PACK], BF16, name="h_bf", bufs=3, align_bytes=64)
+            k = i - first
+            for part in range(2):
+                acc = psum.tile([P, PACK, TILE], F32, name="h_acc", tag="h_acc", bufs=2)
+                for t in range(PACK):
+                    for term in range(2):
+                        nc.tensor.matmul(
+                            acc[:, t, :], lhsT=prod[:, 2 * part + term, t, :], rhs=ident[:],
+                            start=(term == 0), stop=(term == 1), is_transpose=True,
+                        )
+                nc.scalar.copy(h_bf[first][:, part, k * TILE : (k + 1) * TILE, :], acc[:].rearrange("p t n -> p n t"))
+
+        def score(first, count):
+            width = count * TILE
+            h_codes = ring.tile([P, 2 * width], U32, name="h_codes", bufs=2, align_bytes=64)
+            h_scales = ring.tile([P, 2 * width], U8, name="h_scales", bufs=2, align_bytes=64)
+            nc.vector.quantize_mx(
+                out=h_codes[:].bitcast(FP8X4), scales=h_scales[:], in_=h_bf[first][:].rearrange("p h n t -> p (h n t)"),
+            )
+            per_bank = min(2, CHUNK // width)
+            for bank in range(2 // per_bank):
+                acc = psum.tile([P, per_bank, width], F32, name="y_acc", tag="y_acc", bufs=1)
+                for slot in range(per_bank):
+                    half = bank * per_bank + slot
+                    for part, w in enumerate((nr, ni)):
+                        cols = slice(part * width, (part + 1) * width)
+                        nc.tensor.matmul_mx(
+                            out=acc[:, slot, :], lhsT=w[0][:, 2 * P * half : 2 * P * (half + 1)].bitcast(FP4X4),
+                            lhsT_scale=w[1][:, P * half : P * (half + 1)],
+                            rhs=h_codes[:, cols].bitcast(FP8X4), rhs_scale=h_scales[:, cols],
+                            start=(part == 0), stop=(part == 1),
+                        )
+                result = ring.tile([P, per_bank, width], F32, name="result", bufs=4)
+                nc.scalar.activation(result[:], acc[:], SIGMOID)
+                rows = out[P * bank * per_bank : P * (bank + 1) * per_bank, first * TILE : first * TILE + width]
+                nc.sync.dma_start(out=rows.rearrange("(h p) n -> p h n", p=P), in_=result[:])
+
+        for k in range(4):
+            gather_part(0, k)
+        rels = {}
+        prods = {}
+        for step in range(TILES + SCORE_LAG + 1):
+            c, k = divmod(step, TILES_PER_CHUNK)
+            if c + 1 < CHUNKS:
+                gather_part(c + 1, k)
+            if step == 0:
+                rels[0] = relation(0)
+            if step < TILES:
+                prods[step] = products(step, rels[step])
+            if step + 1 < TILES:
+                rels[step + 1] = relation(step + 1)
+            if 0 <= step - TURN_LAG < TILES:
+                turn(step - TURN_LAG, prods[step - TURN_LAG])
+            for first, count in SCORE_GROUPS:
+                if first + count - 1 == step - SCORE_LAG:
+                    score(first, count)

@@ -47,11 +47,8 @@ def tile_list_ckg_sig_kernel(
         tab_r = keep.tile([P, T], I32, name="tab_r", align_bytes=64)
         tabs_e = keep.tile([P, T // 4], I32, name="tabs_e", align_bytes=64)
         tabs_r = keep.tile([P, T // 4], I32, name="tabs_r", align_bytes=64)
-        planes = keep.tile([P, (4 * R + 2 * N) // 4], I32, name="planes", align_bytes=64)
         ident = keep.tile([P, P], F32, name="ident", align_bytes=64)
 
-        nc.vector.memset(tabs_r[:], 0)
-        nc.vector.memset(planes[:], 0)
         nc.vector.memset(tabs_e[:], 0)
         make_identity(nc, ident[:])
 
@@ -59,40 +56,46 @@ def tile_list_ckg_sig_kernel(
             rows = scales[0].bitcast(I32)
             return [(plane[r:P:32, :], rows[r:16:4, :]) for r in range(4)]
 
+        def spread_loads(plane, scales):
+            rows = scales[0].bitcast(I32)
+            width = rows.shape[1]
+            return [
+                (plane[32 * q : 32 * (q + 1), :], rows[4 * q : 4 * (q + 1), :].unsqueeze(0).broadcast_to([8, 4, width]))
+                for q in range(4)
+            ]
+
         def table_loads(table, words):
             flat = words[0].rearrange("p t i -> p (t i)").bitcast(I32)
             step = T // TABLE_PIECES
             return [(table[:, c * step : (c + 1) * step], flat[:, c * step : (c + 1) * step]) for c in range(TABLE_PIECES)]
 
-        def weight(name, flat_words, scales, first, columns):
+        def weight(name, flat_words, scales, first, columns, scale_loads):
             codes = keep.tile([P, flat_words.shape[1]], U8, name=name, align_bytes=64)
-            plane = planes[:, first // 4 : (first + columns) // 4]
-            return codes, plane.bitcast(U8), (codes[:].bitcast(I32), flat_words.bitcast(I32)), plane_loads(plane, scales)
+            plane = keep.tile([P, columns // 4], I32, name=name + "_plane", align_bytes=64)[:]
+            if first:
+                nc.vector.memset(plane, 0)
+            return codes, plane.bitcast(U8), (codes[:].bitcast(I32), flat_words.bitcast(I32)), scale_loads(plane, scales)
 
-        wrr = weight("wrr", wrr_words[0].rearrange("p r i -> p (r i)"), wrr_scales, 0, R)
-        wri = weight("wri", wri_words[0].rearrange("p r i -> p (r i)"), wri_scales, R, R)
-        wer = weight("wer", wer_words[0], wer_scales, 2 * R, R)
-        wei = weight("wei", wei_words[0], wei_scales, 3 * R, R)
-        nr = weight("nr", nr_words[0], nr_scales, 4 * R, N)
-        ni = weight("ni", ni_words[0], ni_scales, 4 * R + N, N)
+        wrr = weight("wrr", wrr_words[0].rearrange("p r i -> p (r i)"), wrr_scales, 0, R, spread_loads)
+        wri = weight("wri", wri_words[0].rearrange("p r i -> p (r i)"), wri_scales, 0, R, spread_loads)
+        wer = weight("wer", wer_words[0], wer_scales, 2 * R, R, plane_loads)
+        wei = weight("wei", wei_words[0], wei_scales, 3 * R, R, plane_loads)
+        nr = weight("nr", nr_words[0], nr_scales, 4 * R, N, plane_loads)
+        ni = weight("ni", ni_words[0], ni_scales, 4 * R + N, N, plane_loads)
 
-        def weave(big, small):
-            each = -(-len(small) // len(big))
-            order = []
-            for n, piece in enumerate(big):
-                order.append(piece)
-                order.extend(small[n * each : (n + 1) * each])
-            return order
-
-        loads = [(list_r[:], offs2)] + plane_loads(tabs_r, tab2_scales)
-        loads += weave(table_loads(tab_r, tab2_words), wrr[3] + wri[3] + [(list_e[:], offs), wrr[2], wri[2]])
-        loads += weave(table_loads(tab_e, tab_words), plane_loads(tabs_e, tab_scales) + wer[3] + wei[3])
-        loads += [wer[2], wei[2], nr[2], ni[2]] + nr[3] + ni[3]
+        words_r = table_loads(tab_r, tab2_words)
+        words_e = table_loads(tab_e, tab_words)
+        plane_e = plane_loads(tabs_e, tab_scales)
+        loads = [(list_r[:], offs2)] + spread_loads(tabs_r, tab2_scales) + words_r[:2] + [wrr[2]]
+        loads += [wri[2]] + wrr[3] + words_r[2:] + [(list_e[:], offs)]
+        loads += wri[3] + plane_e[:1] + words_e[:2] + plane_e[1:2]
+        loads += plane_e[2:] + [wer[2], wei[2]] + wer[3][:1] + words_e[2:] + wer[3][1:]
+        loads += wei[3] + [nr[2], ni[2]] + nr[3] + ni[3]
         for dst, src in loads:
             nc.sync.dma_start(out=dst, in_=src)
 
         def gather(name, window, offsets, c, dtype):
-            picked = keep.tile([P, CHUNK], dtype, name=name + str(c), align_bytes=64)
+            picked = ring.tile([P, CHUNK], dtype, name=name, bufs=(2 if name in ("scales_e", "codes_e") else 4), align_bytes=64)
             columns = slice(c * CHUNK // 16, (c + 1) * CHUNK // 16)
             nc.vector.tensor_copy(picked[:], window[:].bitcast(dtype).indirect(offsets[:, columns]))
             return picked
@@ -119,7 +122,7 @@ def tile_list_ckg_sig_kernel(
             return acc[:].rearrange("p (m t) -> p t m", t=PACK)
 
         def relation(i):
-            rel = ring.tile([P, 2, PACK, TILE], F32, name="rel", bufs=16, align_bytes=64)
+            rel = ring.tile([P, 2, PACK, TILE], F32, name="rel", bufs=6, align_bytes=64)
             nc.scalar.copy(rel[:, 0], project("rel_acc", 2, "r", i, wrr, FP8X4))
             nc.scalar.copy(rel[:, 1], project("rel_acc", 2, "r", i, wri, FP8X4))
             return rel

@@ -49,50 +49,55 @@ def tile_list_ckg_sig_kernel(
         tabs_r = keep.tile([P, T // 4], I32, name="tabs_r", align_bytes=64)
         ident = keep.tile([P, P], F32, name="ident", align_bytes=64)
 
-        nc.vector.memset(tabs_e[:], 0)
+        nc.gpsimd.memset(tabs_r[:], 0)
         make_identity(nc, ident[:])
 
         def plane_loads(plane, scales):
             rows = scales[0].bitcast(I32)
             return [(plane[r:P:32, :], rows[r:16:4, :]) for r in range(4)]
 
-        def spread_loads(plane, scales):
-            rows = scales[0].bitcast(I32)
-            width = rows.shape[1]
-            return [
-                (plane[32 * q : 32 * (q + 1), :], rows[4 * q : 4 * (q + 1), :].unsqueeze(0).broadcast_to([8, 4, width]))
-                for q in range(4)
-            ]
-
         def table_loads(table, words):
             flat = words[0].rearrange("p t i -> p (t i)").bitcast(I32)
             step = T // TABLE_PIECES
             return [(table[:, c * step : (c + 1) * step], flat[:, c * step : (c + 1) * step]) for c in range(TABLE_PIECES)]
 
-        def weight(name, flat_words, scales, first, columns, scale_loads):
+        def weight(name, flat_words, scales, columns):
             codes = keep.tile([P, flat_words.shape[1]], U8, name=name, align_bytes=64)
-            plane = keep.tile([P, columns // 4], I32, name=name + "_plane", align_bytes=64)[:]
-            if first:
-                nc.vector.memset(plane, 0)
-            return codes, plane.bitcast(U8), (codes[:].bitcast(I32), flat_words.bitcast(I32)), scale_loads(plane, scales)
+            plane = keep.tile([P, columns // 4], I32, name=name + "_plane", align_bytes=64)
+            nc.vector.memset(plane[:], 0)
+            return codes[:], plane[:].bitcast(U8), (codes[:].bitcast(I32), flat_words.bitcast(I32)), plane_loads(plane, scales)
 
-        wrr = weight("wrr", wrr_words[0].rearrange("p r i -> p (r i)"), wrr_scales, 0, R, spread_loads)
-        wri = weight("wri", wri_words[0].rearrange("p r i -> p (r i)"), wri_scales, 0, R, spread_loads)
-        wer = weight("wer", wer_words[0], wer_scales, 2 * R, R, plane_loads)
-        wei = weight("wei", wei_words[0], wei_scales, 3 * R, R, plane_loads)
-        nr = weight("nr", nr_words[0], nr_scales, 4 * R, N, plane_loads)
-        ni = weight("ni", ni_words[0], ni_scales, 4 * R + N, N, plane_loads)
+        wrr = weight("wrr", wrr_words[0].rearrange("p r i -> p (r i)"), wrr_scales, R)
+        wri = weight("wri", wri_words[0].rearrange("p r i -> p (r i)"), wri_scales, R)
+        wer = weight("wer", wer_words[0], wer_scales, R)
+        wei = weight("wei", wei_words[0], wei_scales, R)
+        nc.vector.memset(tabs_e[:], 0)
+        nr = weight("nr", nr_words[0], nr_scales, N)
+        ni = weight("ni", ni_words[0], ni_scales, N)
 
         words_r = table_loads(tab_r, tab2_words)
         words_e = table_loads(tab_e, tab_words)
         plane_e = plane_loads(tabs_e, tab_scales)
-        loads = [(list_r[:], offs2)] + spread_loads(tabs_r, tab2_scales) + words_r[:2] + [wrr[2]]
-        loads += [wri[2]] + wrr[3] + words_r[2:] + [(list_e[:], offs)]
-        loads += wri[3] + plane_e[:1] + words_e[:2] + plane_e[1:2]
-        loads += plane_e[2:] + [wer[2], wei[2]] + wer[3][:1] + words_e[2:] + wer[3][1:]
+        loads = [wrr[2], wri[2], (list_r[:], offs2), wer[2], wei[2]] + plane_loads(tabs_r, tab2_scales)
+        loads += words_r[:2] + wrr[3] + words_r[2:] + wri[3] + [(list_e[:], offs)]
+        loads += plane_e[:1] + words_e[:2] + plane_e[1:] + wer[3][:3] + words_e[2:] + wer[3][3:]
         loads += wei[3] + [nr[2], ni[2]] + nr[3] + ni[3]
         for dst, src in loads:
             nc.sync.dma_start(out=dst, in_=src)
+
+        def reorder(name, source, dtype):
+            ordered = keep.tile([P, PACK, R // PACK], dtype, name=name, align_bytes=64)
+            nc.vector.tensor_copy(ordered[:], source.bitcast(dtype).rearrange("p (m t) -> p t m", t=PACK))
+            return ordered[:].rearrange("p t m -> p (t m)")
+
+        wrr_codes = reorder("wrr_codes", wrr[0], I32)
+        wri_codes = reorder("wri_codes", wri[0], I32)
+        wer_codes = reorder("wer_codes", wer[0], U16)
+        wei_codes = reorder("wei_codes", wei[0], U16)
+        wrr = (wrr_codes, reorder("wrr_order", wrr[1], U8))
+        wri = (wri_codes, reorder("wri_order", wri[1], U8))
+        wer = (wer_codes, reorder("wer_order", wer[1], U8))
+        wei = (wei_codes, reorder("wei_order", wei[1], U8))
 
         def gather(name, window, offsets, c, dtype):
             picked = ring.tile([P, CHUNK], dtype, name=name, bufs=(2 if name in ("scales_e", "codes_e") else 4), align_bytes=64)
@@ -117,36 +122,35 @@ def tile_list_ckg_sig_kernel(
             nc.tensor.matmul_mx(
                 out=acc[:], lhsT=picked["codes_" + side, c][:, cols].bitcast(FP8X4),
                 lhsT_scale=picked["scales_" + side, c][:, cols],
-                rhs=w[0][:].bitcast(fmt), rhs_scale=w[1], start=True, stop=True,
+                rhs=w[0].bitcast(fmt), rhs_scale=w[1], start=True, stop=True,
             )
-            return acc[:].rearrange("p (m t) -> p t m", t=PACK)
+            return acc[:]
 
         def relation(i):
-            rel = ring.tile([P, 2, PACK, TILE], F32, name="rel", bufs=6, align_bytes=64)
+            rel = ring.tile([P, 2, R], F32, name="rel", bufs=6, align_bytes=64)
             nc.scalar.copy(rel[:, 0], project("rel_acc", 2, "r", i, wrr, FP8X4))
             nc.scalar.copy(rel[:, 1], project("rel_acc", 2, "r", i, wri, FP8X4))
             return rel
 
         def products(i, rel):
-            prod = ring.tile([P, 4, PACK, TILE], F32, name="prod", bufs=3, align_bytes=64)
+            prod = ring.tile([P, 4, R], F32, name="prod", bufs=4, align_bytes=64)
             aer = project("ent_acc", 3, "e", i, wer, FP4X4)
             aei = project("ent_acc", 3, "e", i, wei, FP4X4)
             if i in POOL_TILES:
-                ent = ring.tile([P, PACK, TILE], F32, name="ent", bufs=2, align_bytes=64)
+                ent = ring.tile([P, R], F32, name="ent", bufs=2, align_bytes=64)
                 nc.scalar.copy(ent[:], aer)
                 nc.gpsimd.tensor_tensor(prod[:, 0], ent[:], rel[:, 0], MULT)
-                nc.gpsimd.tensor_tensor(prod[:, 2], ent[:], rel[:, 1], MULT)
-                nc.vector.scalar_tensor_tensor(prod[:, 1], aei, -1.0, rel[:, 1], MULT, MULT)
+                nc.gpsimd.tensor_tensor(prod[:, 1], ent[:], rel[:, 1], MULT)
+                nc.vector.scalar_tensor_tensor(prod[:, 2], aei, -1.0, rel[:, 1], MULT, MULT)
                 nc.vector.tensor_tensor(prod[:, 3], aei, rel[:, 0], MULT)
             elif i == TILES - 1:
                 nc.vector.tensor_tensor(prod[:, 0], aer, rel[:, 0], MULT)
-                nc.vector.scalar_tensor_tensor(prod[:, 1], aei, -1.0, rel[:, 1], MULT, MULT)
-                nc.vector.tensor_tensor(prod[:, 2], aer, rel[:, 1], MULT)
+                nc.vector.scalar_tensor_tensor(prod[:, 2], aei, -1.0, rel[:, 1], MULT, MULT)
+                nc.vector.tensor_tensor(prod[:, 1], aer, rel[:, 1], MULT)
                 nc.vector.tensor_tensor(prod[:, 3], aei, rel[:, 0], MULT)
             else:
-                nc.vector.tensor_tensor(prod[:, 0], aer, rel[:, 0], MULT)
-                nc.vector.tensor_tensor(prod[:, 2], aer, rel[:, 1], MULT)
-                nc.vector.scalar_tensor_tensor(prod[:, 1], aei, -1.0, rel[:, 1], MULT, MULT)
+                nc.vector.tensor_tensor(prod[:, 0:2], aer.unsqueeze(1).broadcast_to([P, 2, R]), rel[:], MULT)
+                nc.vector.scalar_tensor_tensor(prod[:, 2], aei, -1.0, rel[:, 1], MULT, MULT)
                 nc.vector.tensor_tensor(prod[:, 3], aei, rel[:, 0], MULT)
             return prod
 
@@ -166,7 +170,7 @@ def tile_list_ckg_sig_kernel(
                 for t in range(PACK):
                     for term in range(2):
                         nc.tensor.matmul(
-                            acc[:, t, :], lhsT=prod[:, 2 * part + term, t, :], rhs=ident[:],
+                            acc[:, t, :], lhsT=prod[:, part + 2 * term, t * P : (t + 1) * P], rhs=ident[:],
                             start=(term == 0), stop=(term == 1), is_transpose=True,
                         )
                 nc.scalar.copy(h_bf[first][:, part, k * TILE : (k + 1) * TILE, :], acc[:].rearrange("p t n -> p n t"))

@@ -24,7 +24,7 @@ TILE = 128
 CHUNKS = J // CHUNK
 TILES = J // TILE
 TILES_PER_CHUNK = CHUNK // TILE
-TABLE_PIECES = 4
+TABLE_PIECES = 1
 POOL_TILES = ()
 SCORE_GROUPS = ((0, 4), (4, 4), (8, 4), (12, 1), (13, 1), (14, 1), (15, 1))
 TURN_LAG = 1
@@ -69,19 +69,16 @@ def tile_list_ckg_sig_kernel(
 
         wrr = weight("wrr", wrr_words[0].rearrange("p r i -> p (r i)"), wrr_scales, R)
         wri = weight("wri", wri_words[0].rearrange("p r i -> p (r i)"), wri_scales, R)
+        nc.vector.memset(tabs_e[:], 0)
         wer = weight("wer", wer_words[0], wer_scales, R)
         wei = weight("wei", wei_words[0], wei_scales, R)
-        nc.vector.memset(tabs_e[:], 0)
         nr = weight("nr", nr_words[0], nr_scales, N)
         ni = weight("ni", ni_words[0], ni_scales, N)
 
-        words_r = table_loads(tab_r, tab2_words)
-        words_e = table_loads(tab_e, tab_words)
-        plane_e = plane_loads(tabs_e, tab_scales)
-        loads = [wrr[2], wri[2], (list_r[:], offs2), wer[2], wei[2]] + plane_loads(tabs_r, tab2_scales)
-        loads += words_r[:2] + wrr[3] + words_r[2:] + wri[3] + [(list_e[:], offs)]
-        loads += plane_e[:1] + words_e[:2] + plane_e[1:] + wer[3][:3] + words_e[2:] + wer[3][3:]
-        loads += wei[3] + [nr[2], ni[2]] + nr[3] + ni[3]
+        loads = [(list_r[:], offs2), wrr[2], wri[2], wer[2], wei[2], (list_e[:], offs)]
+        loads += plane_loads(tabs_r, tab2_scales) + wrr[3] + wri[3] + plane_loads(tabs_e, tab_scales)
+        loads += wer[3][:1] + table_loads(tab_r, tab2_words) + table_loads(tab_e, tab_words) + wer[3][1:] + wei[3]
+        loads += [nr[2], ni[2]] + nr[3] + ni[3]
         for dst, src in loads:
             nc.sync.dma_start(out=dst, in_=src)
 
@@ -127,7 +124,7 @@ def tile_list_ckg_sig_kernel(
             return acc[:]
 
         def relation(i):
-            rel = ring.tile([P, 2, R], F32, name="rel", bufs=6, align_bytes=64)
+            rel = ring.tile([P, 2, R], F32, name="rel", bufs=4, align_bytes=64)
             nc.scalar.copy(rel[:, 0], project("rel_acc", 2, "r", i, wrr, FP8X4))
             nc.scalar.copy(rel[:, 1], project("rel_acc", 2, "r", i, wri, FP8X4))
             return rel

@@ -15,6 +15,8 @@ U8 = mybir.dt.uint8
 FP8X4 = mybir.dt.float8_e4m3fn_x4
 FP4X4 = mybir.dt.float4_e2m1fn_x4
 MULT = mybir.AluOpType.mult
+ADD = mybir.AluOpType.add
+SUBTRACT = mybir.AluOpType.subtract
 SIGMOID = mybir.ActivationFunctionType.Sigmoid
 
 P = 128
@@ -25,10 +27,14 @@ CHUNKS = J // CHUNK
 TILES = J // TILE
 TILES_PER_CHUNK = CHUNK // TILE
 TABLE_PIECES = 1
-POOL_TILES = ()
+POOL_TILES = (2, 4)
+SUM_TILES = (1, 10, 14, 15)
+VECTOR_SUM_TILES = (15,)
+POOL_LAG = 1
+RELATION_AHEAD = 2
 SCORE_GROUPS = ((0, 4), (4, 4), (8, 4), (12, 1), (13, 1), (14, 1), (15, 1))
 TURN_LAG = 1
-SCORE_LAG = 3
+SCORE_LAG = 4
 
 
 def tile_list_ckg_sig_kernel(
@@ -116,6 +122,16 @@ def tile_list_ckg_sig_kernel(
             c, k = divmod(i, TILES_PER_CHUNK)
             cols = slice(k * TILE, (k + 1) * TILE)
             acc = psum.tile([P, R], F32, name=tag, tag=tag, bufs=bufs)
+            if i in SUM_TILES:
+                slots = acc[:].rearrange("p (t n) -> p t n", t=PACK)
+                for t in range(PACK):
+                    nc.tensor.matmul_mx(
+                        out=slots[:, t, :], lhsT=w[0][:, t * P : (t + 1) * P].bitcast(fmt),
+                        lhsT_scale=w[1][:, t * P : (t + 1) * P],
+                        rhs=picked["codes_" + side, c][:, cols].bitcast(FP8X4),
+                        rhs_scale=picked["scales_" + side, c][:, cols], start=True, stop=True,
+                    )
+                return slots.rearrange("p t n -> p n t")
             nc.tensor.matmul_mx(
                 out=acc[:], lhsT=picked["codes_" + side, c][:, cols].bitcast(FP8X4),
                 lhsT_scale=picked["scales_" + side, c][:, cols],
@@ -124,16 +140,27 @@ def tile_list_ckg_sig_kernel(
             return acc[:]
 
         def relation(i):
-            rel = ring.tile([P, 2, R], F32, name="rel", bufs=4, align_bytes=64)
-            nc.scalar.copy(rel[:, 0], project("rel_acc", 2, "r", i, wrr, FP8X4))
-            nc.scalar.copy(rel[:, 1], project("rel_acc", 2, "r", i, wri, FP8X4))
+            rel = ring.tile([P, 2, R], F32, name="rel", bufs=3, align_bytes=64)
+            for part, w in enumerate((wrr, wri)):
+                acc = project("rel_acc", 2, "r", i, w, FP8X4)
+                if i in SUM_TILES:
+                    nc.scalar.copy(rel[:, part].rearrange("p (n t) -> p n t", t=PACK), acc)
+                else:
+                    nc.scalar.copy(rel[:, part], acc)
             return rel
 
         def products(i, rel):
-            prod = ring.tile([P, 4, R], F32, name="prod", bufs=4, align_bytes=64)
-            aer = project("ent_acc", 3, "e", i, wer, FP4X4)
-            aei = project("ent_acc", 3, "e", i, wei, FP4X4)
-            if i in POOL_TILES:
+            prod = ring.tile([P, 4, R], F32, name="prod", bufs=5, align_bytes=64)
+            aer = project("ent_acc", 4, "e", i, wer, FP4X4)
+            aei = project("ent_acc", 4, "e", i, wei, FP4X4)
+            if i in SUM_TILES:
+                both = rel[:].rearrange("p h (n t) -> p h n t", t=PACK)
+                for pair, ent_acc in enumerate((aer, aei)):
+                    nc.vector.tensor_tensor(
+                        prod[:, 2 * pair : 2 * pair + 2].rearrange("p h (n t) -> p h n t", t=PACK),
+                        ent_acc.unsqueeze(1).broadcast_to([P, 2, TILE, PACK]), both, MULT,
+                    )
+            elif i in POOL_TILES:
                 ent = ring.tile([P, R], F32, name="ent", bufs=2, align_bytes=64)
                 nc.scalar.copy(ent[:], aer)
                 nc.gpsimd.tensor_tensor(prod[:, 0], ent[:], rel[:, 0], MULT)
@@ -159,9 +186,16 @@ def tile_list_ckg_sig_kernel(
 
         def turn(i, prod):
             first, count = group_of[i]
-            if i == first:
-                h_bf[first] = ring.tile([P, 2, count * TILE, PACK], BF16, name="h_bf", bufs=3, align_bytes=64)
+            if first not in h_bf:
+                h_bf[first] = ring.tile([P, 2, count * TILE, PACK], BF16, name="h_bf", bufs=4, align_bytes=64)
             k = i - first
+            if i in SUM_TILES:
+                flat = h_bf[first][:].rearrange("p h n t -> p h (n t)")
+                span = slice(k * R, (k + 1) * R)
+                engine = nc.vector if i in VECTOR_SUM_TILES else nc.gpsimd
+                engine.tensor_tensor(flat[:, 0, span], prod[:, 0], prod[:, 3], SUBTRACT)
+                engine.tensor_tensor(flat[:, 1, span], prod[:, 1], prod[:, 2], ADD)
+                return
             for part in range(2):
                 acc = psum.tile([P, PACK, TILE], F32, name="h_acc", tag="h_acc", bufs=2)
                 for t in range(PACK):
@@ -181,7 +215,7 @@ def tile_list_ckg_sig_kernel(
             )
             per_bank = min(2, CHUNK // width)
             for bank in range(2 // per_bank):
-                acc = psum.tile([P, per_bank, width], F32, name="y_acc", tag="y_acc", bufs=1)
+                acc = psum.tile([P, per_bank, width], F32, name="y_acc", tag="h_acc", bufs=2)
                 for slot in range(per_bank):
                     half = bank * per_bank + slot
                     for part, w in enumerate((nr, ni)):
@@ -206,13 +240,15 @@ def tile_list_ckg_sig_kernel(
             if c + 1 < CHUNKS:
                 gather_part(c + 1, k)
             if step == 0:
-                rels[0] = relation(0)
+                for j in range(RELATION_AHEAD):
+                    rels[j] = relation(j)
             if step < TILES:
                 prods[step] = products(step, rels[step])
-            if step + 1 < TILES:
-                rels[step + 1] = relation(step + 1)
-            if 0 <= step - TURN_LAG < TILES:
-                turn(step - TURN_LAG, prods[step - TURN_LAG])
+            if step + RELATION_AHEAD < TILES:
+                rels[step + RELATION_AHEAD] = relation(step + RELATION_AHEAD)
+            for i in range(TILES):
+                if i + (POOL_LAG if i in POOL_TILES else TURN_LAG) == step:
+                    turn(i, prods[i])
             for first, count in SCORE_GROUPS:
                 if first + count - 1 == step - SCORE_LAG:
                     score(first, count)

@@ -26,15 +26,17 @@ TILE = 128
 CHUNKS = J // CHUNK
 TILES = J // TILE
 TILES_PER_CHUNK = CHUNK // TILE
-TABLE_PIECES = 1
-POOL_TILES = (2, 4)
-SUM_TILES = (1, 10, 14, 15)
-VECTOR_SUM_TILES = (15,)
-POOL_LAG = 1
-RELATION_AHEAD = 2
-SCORE_GROUPS = ((0, 4), (4, 4), (8, 4), (12, 1), (13, 1), (14, 1), (15, 1))
+TABLE_PIECES = 4
+POOL_TILES = (1, 4, 6, 9, 11, 13)
+SUM_TILES = (2, 5, 7, 10, 12)
+POOL_LAG = 2
 TURN_LAG = 1
-SCORE_LAG = 4
+RELATION_AHEAD = 5
+SCORE_GROUPS = ((0, 4), (4, 4), (8, 4), (12, 2), (14, 1), (15, 1))
+SCORE_LAG = 3
+TABLE_ROW = 8
+WEIGHT_ROW = 4
+GATHERS_AT = {2: (("codes_r", 2),), 3: (("scales_e", 2), ("codes_e", 2)), 7: (("scales_e", 3), ("codes_e", 3))}
 
 
 def tile_list_ckg_sig_kernel(
@@ -44,8 +46,22 @@ def tile_list_ckg_sig_kernel(
     nc = tc.nc
     with ExitStack() as ctx:
         keep = ctx.enter_context(tc.tile_pool(name="keep", bufs=1))
-        ring = ctx.enter_context(tc.tile_pool(name="ring", bufs=2))
-        psum = ctx.enter_context(tc.psum_pool(name="psum", bufs=2))
+        psum = ctx.enter_context(tc.psum_pool(name="psum", bufs=1))
+
+        held = {}
+        used = {}
+
+        def take(name, pool, shape, dtype, depth):
+            if name not in held:
+                held[name] = [pool.tile(shape, dtype, name="%s_%d" % (name, n), align_bytes=64) for n in range(depth)]
+            used[name] = used.get(name, -1) + 1
+            return held[name][used[name] % depth]
+
+        def bank(name):
+            if name not in held:
+                held[name] = [psum.tile([P, R], F32, name="%s_%d" % (name, n)) for n in range(4)]
+            used[name] = used.get(name, -1) + 1
+            return held[name][used[name] % 4]
 
         list_e = keep.tile([P, J // 16], U16, name="list_e")
         list_r = keep.tile([P, J // 16], U16, name="list_r")
@@ -54,128 +70,122 @@ def tile_list_ckg_sig_kernel(
         tabs_e = keep.tile([P, T // 4], I32, name="tabs_e", align_bytes=64)
         tabs_r = keep.tile([P, T // 4], I32, name="tabs_r", align_bytes=64)
         ident = keep.tile([P, P], F32, name="ident", align_bytes=64)
+        warm = keep.tile([P, 2], F32, name="warm")
 
-        nc.gpsimd.memset(tabs_r[:], 0)
-        make_identity(nc, ident[:])
+        nc.gpsimd.memset(warm[:, 0:1], 0.0)
+        nc.gpsimd.memset(tabs_r[:, : T // 8], 0)
+        nc.vector.memset(tabs_r[:, T // 8 :], 0)
+        nc.scalar.activation(warm[:, 1:2], warm[:, 0:1], SIGMOID)
 
-        def plane_loads(plane, scales):
+        def plane_loads(plane, scales, row):
             rows = scales[0].bitcast(I32)
-            return [(plane[r:P:32, :], rows[r:16:4, :]) for r in range(4)]
+            return [(plane[row + r : P : 32, :], rows[r:16:4, :]) for r in range(4)]
 
         def table_loads(table, words):
             flat = words[0].rearrange("p t i -> p (t i)").bitcast(I32)
             step = T // TABLE_PIECES
             return [(table[:, c * step : (c + 1) * step], flat[:, c * step : (c + 1) * step]) for c in range(TABLE_PIECES)]
 
-        def weight(name, flat_words, scales, columns):
+        def weight(name, flat_words, scales, columns, row):
             codes = keep.tile([P, flat_words.shape[1]], U8, name=name, align_bytes=64)
             plane = keep.tile([P, columns // 4], I32, name=name + "_plane", align_bytes=64)
             nc.vector.memset(plane[:], 0)
-            return codes[:], plane[:].bitcast(U8), (codes[:].bitcast(I32), flat_words.bitcast(I32)), plane_loads(plane, scales)
+            return (
+                codes[:], plane[:].bitcast(U8)[row:P, :], (codes[:].bitcast(I32), flat_words.bitcast(I32)),
+                plane_loads(plane, scales, row),
+            )
 
-        wrr = weight("wrr", wrr_words[0].rearrange("p r i -> p (r i)"), wrr_scales, R)
-        wri = weight("wri", wri_words[0].rearrange("p r i -> p (r i)"), wri_scales, R)
+        wrr = weight("wrr", wrr_words[0].rearrange("p r i -> p (r i)"), wrr_scales, R, WEIGHT_ROW)
+        wri = weight("wri", wri_words[0].rearrange("p r i -> p (r i)"), wri_scales, R, WEIGHT_ROW)
         nc.vector.memset(tabs_e[:], 0)
-        wer = weight("wer", wer_words[0], wer_scales, R)
-        wei = weight("wei", wei_words[0], wei_scales, R)
-        nr = weight("nr", nr_words[0], nr_scales, N)
-        ni = weight("ni", ni_words[0], ni_scales, N)
+        wer = weight("wer", wer_words[0], wer_scales, R, 0)
+        wei = weight("wei", wei_words[0], wei_scales, R, 0)
+        nr = weight("nr", nr_words[0], nr_scales, N, 0)
+        ni = weight("ni", ni_words[0], ni_scales, N, 0)
+        make_identity(nc, ident[:])
 
-        loads = [(list_r[:], offs2), wrr[2], wri[2], wer[2], wei[2], (list_e[:], offs)]
-        loads += plane_loads(tabs_r, tab2_scales) + wrr[3] + wri[3] + plane_loads(tabs_e, tab_scales)
-        loads += wer[3][:1] + table_loads(tab_r, tab2_words) + table_loads(tab_e, tab_words) + wer[3][1:] + wei[3]
-        loads += [nr[2], ni[2]] + nr[3] + ni[3]
+        big_r = table_loads(tab_r, tab2_words)
+        big_e = table_loads(tab_e, tab_words)
+        loads = [(list_r[:], offs2), (list_e[:], offs)] + plane_loads(tabs_r, tab2_scales, TABLE_ROW) + [wrr[2], wri[2]]
+        loads += big_r[:2] + wrr[3] + wri[3][:2]
+        loads += big_r[2:] + wri[3][2:] + plane_loads(tabs_e, tab_scales, 0)
+        loads += big_e[:2] + [wer[2], wei[2]] + wer[3]
+        loads += big_e[2:3] + wei[3] + big_e[3:] + [nr[2], ni[2]] + nr[3] + ni[3]
         for dst, src in loads:
             nc.sync.dma_start(out=dst, in_=src)
 
-        def reorder(name, source, dtype):
-            ordered = keep.tile([P, PACK, R // PACK], dtype, name=name, align_bytes=64)
-            nc.vector.tensor_copy(ordered[:], source.bitcast(dtype).rearrange("p (m t) -> p t m", t=PACK))
-            return ordered[:].rearrange("p t m -> p (t m)")
-
-        wrr_codes = reorder("wrr_codes", wrr[0], I32)
-        wri_codes = reorder("wri_codes", wri[0], I32)
-        wer_codes = reorder("wer_codes", wer[0], U16)
-        wei_codes = reorder("wei_codes", wei[0], U16)
-        wrr = (wrr_codes, reorder("wrr_order", wrr[1], U8))
-        wri = (wri_codes, reorder("wri_order", wri[1], U8))
-        wer = (wer_codes, reorder("wer_order", wer[1], U8))
-        wei = (wei_codes, reorder("wei_order", wei[1], U8))
-
-        def gather(name, window, offsets, c, dtype):
-            picked = ring.tile([P, CHUNK], dtype, name=name, bufs=(2 if name in ("scales_e", "codes_e") else 4), align_bytes=64)
-            columns = slice(c * CHUNK // 16, (c + 1) * CHUNK // 16)
-            nc.vector.tensor_copy(picked[:], window[:].bitcast(dtype).indirect(offsets[:, columns]))
-            return picked
-
-        sources = (
-            ("scales_r", tabs_r, list_r, U8), ("codes_r", tab_r, list_r, U32),
-            ("scales_e", tabs_e, list_e, U8), ("codes_e", tab_e, list_e, U32),
-        )
+        sources = {
+            "scales_r": (tabs_r, list_r, U8, 4), "codes_r": (tab_r, list_r, U32, 1),
+            "scales_e": (tabs_e, list_e, U8, 2), "codes_e": (tab_e, list_e, U32, 2),
+        }
         picked = {}
 
-        def gather_part(c, k):
-            name, window, offsets, dtype = sources[k]
-            picked[name, c] = gather(name, window, offsets, c, dtype)
+        def gather(name, c):
+            window, offsets, dtype, bufs = sources[name]
+            chunks = 2 if (name, c) == ("codes_r", 2) else 1
+            tag = "codes_r_first" if (name, c) == ("codes_r", 0) else name
+            wide = 2 if tag == "codes_r" else 1
+            taken = take(tag, keep, [P, wide * CHUNK], dtype, bufs)[:, : chunks * CHUNK]
+            columns = slice(c * CHUNK // 16, (c + chunks) * CHUNK // 16)
+            nc.vector.tensor_copy(taken, window[:].bitcast(dtype).indirect(offsets[:, columns]))
+            for n in range(chunks):
+                picked[name, c + n] = taken[:, n * CHUNK : (n + 1) * CHUNK]
 
-        def project(tag, bufs, side, i, w, fmt):
+        def dealt(flat, i):
+            if i in SUM_TILES:
+                return flat.rearrange("p (u m e) -> p u m e", u=2, e=2)
+            return flat.rearrange("p (t m) -> p t m", t=PACK)
+
+        def project(tag, side, i, w, fmt, row):
             c, k = divmod(i, TILES_PER_CHUNK)
             cols = slice(k * TILE, (k + 1) * TILE)
-            acc = psum.tile([P, R], F32, name=tag, tag=tag, bufs=bufs)
-            if i in SUM_TILES:
-                slots = acc[:].rearrange("p (t n) -> p t n", t=PACK)
-                for t in range(PACK):
-                    nc.tensor.matmul_mx(
-                        out=slots[:, t, :], lhsT=w[0][:, t * P : (t + 1) * P].bitcast(fmt),
-                        lhsT_scale=w[1][:, t * P : (t + 1) * P],
-                        rhs=picked["codes_" + side, c][:, cols].bitcast(FP8X4),
-                        rhs_scale=picked["scales_" + side, c][:, cols], start=True, stop=True,
-                    )
-                return slots.rearrange("p t n -> p n t")
+            acc = bank(tag)
             nc.tensor.matmul_mx(
                 out=acc[:], lhsT=picked["codes_" + side, c][:, cols].bitcast(FP8X4),
-                lhsT_scale=picked["scales_" + side, c][:, cols],
+                lhsT_scale=picked["scales_" + side, c][row:P, cols],
                 rhs=w[0].bitcast(fmt), rhs_scale=w[1], start=True, stop=True,
             )
-            return acc[:]
+            if i in SUM_TILES:
+                return acc[:].rearrange("p (m u e) -> p u m e", u=2, e=2)
+            return acc[:].rearrange("p (m t) -> p t m", t=PACK)
 
         def relation(i):
-            rel = ring.tile([P, 2, R], F32, name="rel", bufs=3, align_bytes=64)
+            rel = take("rel", keep, [P, 2, R], F32, RELATION_AHEAD + 1)
             for part, w in enumerate((wrr, wri)):
-                acc = project("rel_acc", 2, "r", i, w, FP8X4)
-                if i in SUM_TILES:
-                    nc.scalar.copy(rel[:, part].rearrange("p (n t) -> p n t", t=PACK), acc)
-                else:
-                    nc.scalar.copy(rel[:, part], acc)
+                nc.scalar.copy(dealt(rel[:, part], i), project("for_scalar", "r", i, w, FP8X4, TABLE_ROW))
             return rel
 
-        def products(i, rel):
-            prod = ring.tile([P, 4, R], F32, name="prod", bufs=5, align_bytes=64)
-            aer = project("ent_acc", 4, "e", i, wer, FP4X4)
-            aei = project("ent_acc", 4, "e", i, wei, FP4X4)
+        def entity(i):
+            return project("for_vector", "e", i, wer, FP4X4, 0), project("for_vector", "e", i, wei, FP4X4, 0)
+
+        def products(i, rel, aer, aei):
+            prod = take("prod", keep, [P, 4, R], F32, 5)
+            arr, ari = dealt(rel[:, 0], i), dealt(rel[:, 1], i)
+            term = [dealt(prod[:, n], i) for n in range(4)]
             if i in SUM_TILES:
-                both = rel[:].rearrange("p h (n t) -> p h n t", t=PACK)
-                for pair, ent_acc in enumerate((aer, aei)):
-                    nc.vector.tensor_tensor(
-                        prod[:, 2 * pair : 2 * pair + 2].rearrange("p h (n t) -> p h n t", t=PACK),
-                        ent_acc.unsqueeze(1).broadcast_to([P, 2, TILE, PACK]), both, MULT,
-                    )
-            elif i in POOL_TILES:
-                ent = ring.tile([P, R], F32, name="ent", bufs=2, align_bytes=64)
-                nc.scalar.copy(ent[:], aer)
+                nc.vector.tensor_tensor(term[0], aer, arr, MULT)
+                nc.vector.tensor_tensor(term[2], aei, ari, MULT)
+                nc.vector.tensor_tensor(term[1], aer, ari, MULT)
+                nc.vector.tensor_tensor(term[3], aei, arr, MULT)
+                return prod
+            if i in POOL_TILES:
+                ent = take("ent", keep, [P, R], F32, 2)
+                nc.scalar.copy(dealt(ent[:], i), aer)
                 nc.gpsimd.tensor_tensor(prod[:, 0], ent[:], rel[:, 0], MULT)
                 nc.gpsimd.tensor_tensor(prod[:, 1], ent[:], rel[:, 1], MULT)
-                nc.vector.scalar_tensor_tensor(prod[:, 2], aei, -1.0, rel[:, 1], MULT, MULT)
-                nc.vector.tensor_tensor(prod[:, 3], aei, rel[:, 0], MULT)
+                nc.vector.scalar_tensor_tensor(term[2], aei, -1.0, ari, MULT, MULT)
             elif i == TILES - 1:
-                nc.vector.tensor_tensor(prod[:, 0], aer, rel[:, 0], MULT)
-                nc.vector.scalar_tensor_tensor(prod[:, 2], aei, -1.0, rel[:, 1], MULT, MULT)
-                nc.vector.tensor_tensor(prod[:, 1], aer, rel[:, 1], MULT)
-                nc.vector.tensor_tensor(prod[:, 3], aei, rel[:, 0], MULT)
+                nc.vector.tensor_tensor(term[0], aer, arr, MULT)
+                nc.vector.scalar_tensor_tensor(term[2], aei, -1.0, ari, MULT, MULT)
+                nc.vector.tensor_tensor(term[1], aer, ari, MULT)
             else:
-                nc.vector.tensor_tensor(prod[:, 0:2], aer.unsqueeze(1).broadcast_to([P, 2, R]), rel[:], MULT)
-                nc.vector.scalar_tensor_tensor(prod[:, 2], aei, -1.0, rel[:, 1], MULT, MULT)
-                nc.vector.tensor_tensor(prod[:, 3], aei, rel[:, 0], MULT)
+                nc.vector.tensor_tensor(
+                    prod[:, 0:2].rearrange("p h (t m) -> p h t m", t=PACK),
+                    aer.unsqueeze(1).broadcast_to([P, 2, PACK, TILE]),
+                    rel[:].rearrange("p h (t m) -> p h t m", t=PACK), MULT,
+                )
+                nc.vector.scalar_tensor_tensor(term[2], aei, -1.0, ari, MULT, MULT)
+            nc.vector.tensor_tensor(term[3], aei, arr, MULT)
             return prod
 
         group_of = {}
@@ -187,67 +197,79 @@ def tile_list_ckg_sig_kernel(
         def turn(i, prod):
             first, count = group_of[i]
             if first not in h_bf:
-                h_bf[first] = ring.tile([P, 2, count * TILE, PACK], BF16, name="h_bf", bufs=4, align_bytes=64)
-            k = i - first
+                h_bf[first] = keep.tile([P, 2, count * TILE, PACK], BF16, name="h_bf_%d" % first, align_bytes=64)
+            tokens = slice((i - first) * TILE, (i - first + 1) * TILE)
             if i in SUM_TILES:
-                flat = h_bf[first][:].rearrange("p h n t -> p h (n t)")
-                span = slice(k * R, (k + 1) * R)
-                engine = nc.vector if i in VECTOR_SUM_TILES else nc.gpsimd
-                engine.tensor_tensor(flat[:, 0, span], prod[:, 0], prod[:, 3], SUBTRACT)
-                engine.tensor_tensor(flat[:, 1, span], prod[:, 1], prod[:, 2], ADD)
+                rounded = take("rounded", keep, [P, 2, R], BF16, 2)
+                nc.gpsimd.tensor_tensor(rounded[:, 0], prod[:, 0], prod[:, 2], SUBTRACT)
+                nc.gpsimd.tensor_tensor(rounded[:, 1], prod[:, 1], prod[:, 3], ADD)
+                pairs = rounded[:].rearrange("p h r -> p (h r)").bitcast(F32)
+                acc = bank("for_scalar")[:].rearrange("p (t n) -> p t n", t=PACK)
+                for slot in range(PACK):
+                    nc.tensor.matmul(
+                        acc[:, slot, :], lhsT=pairs[:, slot * P : (slot + 1) * P], rhs=ident[:],
+                        start=True, stop=True, is_transpose=True,
+                    )
+                nc.scalar.copy(h_bf[first][:, :, tokens, :].bitcast(F32), acc.rearrange("p (h u) n -> p h n u", u=2))
                 return
             for part in range(2):
-                acc = psum.tile([P, PACK, TILE], F32, name="h_acc", tag="h_acc", bufs=2)
+                acc = bank("for_scalar")[:].rearrange("p (t n) -> p t n", t=PACK)
                 for t in range(PACK):
                     for term in range(2):
                         nc.tensor.matmul(
                             acc[:, t, :], lhsT=prod[:, part + 2 * term, t * P : (t + 1) * P], rhs=ident[:],
                             start=(term == 0), stop=(term == 1), is_transpose=True,
                         )
-                nc.scalar.copy(h_bf[first][:, part, k * TILE : (k + 1) * TILE, :], acc[:].rearrange("p t n -> p n t"))
+                nc.scalar.copy(h_bf[first][:, part, tokens, :], acc.rearrange("p t n -> p n t"))
 
         def score(first, count):
             width = count * TILE
-            h_codes = ring.tile([P, 2 * width], U32, name="h_codes", bufs=2, align_bytes=64)
-            h_scales = ring.tile([P, 2 * width], U8, name="h_scales", bufs=2, align_bytes=64)
+            h_codes = keep.tile([P, 2 * width], U32, name="h_codes_%d" % first, align_bytes=64)
+            h_scales = keep.tile([P, 2 * width], U8, name="h_scales_%d" % first, align_bytes=64)
             nc.vector.quantize_mx(
                 out=h_codes[:].bitcast(FP8X4), scales=h_scales[:], in_=h_bf[first][:].rearrange("p h n t -> p (h n t)"),
             )
             per_bank = min(2, CHUNK // width)
-            for bank in range(2 // per_bank):
-                acc = psum.tile([P, per_bank, width], F32, name="y_acc", tag="h_acc", bufs=2)
+            span = CHUNK if width == CHUNK else TILE
+            for n in range(2 // per_bank):
+                acc = bank("for_scalar")[:, : per_bank * width].rearrange("p (h w) -> p h w", h=per_bank)
                 for slot in range(per_bank):
-                    half = bank * per_bank + slot
-                    for part, w in enumerate((nr, ni)):
-                        cols = slice(part * width, (part + 1) * width)
-                        nc.tensor.matmul_mx(
-                            out=acc[:, slot, :], lhsT=w[0][:, 2 * P * half : 2 * P * (half + 1)].bitcast(FP4X4),
-                            lhsT_scale=w[1][:, P * half : P * (half + 1)],
-                            rhs=h_codes[:, cols].bitcast(FP8X4), rhs_scale=h_scales[:, cols],
-                            start=(part == 0), stop=(part == 1),
-                        )
-                result = ring.tile([P, per_bank, width], F32, name="result", bufs=4)
-                nc.scalar.activation(result[:], acc[:], SIGMOID)
-                rows = out[P * bank * per_bank : P * (bank + 1) * per_bank, first * TILE : first * TILE + width]
+                    half = n * per_bank + slot
+                    for begin in range(0, width, span):
+                        for part, w in enumerate((nr, ni)):
+                            cols = slice(part * width + begin, part * width + begin + span)
+                            nc.tensor.matmul_mx(
+                                out=acc[:, slot, begin : begin + span],
+                                lhsT=w[0][:, 2 * P * half : 2 * P * (half + 1)].bitcast(FP4X4),
+                                lhsT_scale=w[1][:, P * half : P * (half + 1)],
+                                rhs=h_codes[:, cols].bitcast(FP8X4), rhs_scale=h_scales[:, cols],
+                                start=(part == 0), stop=(part == 1),
+                            )
+                result = keep.tile([P, per_bank, width], F32, name="result_%d_%d" % (first, n))
+                nc.scalar.activation(result[:], acc, SIGMOID)
+                rows = out[P * n * per_bank : P * (n + 1) * per_bank, first * TILE : first * TILE + width]
                 nc.sync.dma_start(out=rows.rearrange("(h p) n -> p h n", p=P), in_=result[:])
 
-        for k in range(4):
-            gather_part(0, k)
-        rels = {}
+        for c in range(CHUNKS):
+            gather("scales_r", c)
+        gather("codes_r", 0)
+        gather("codes_r", 1)
+        rels = {j: relation(j) for j in range(RELATION_AHEAD)}
+        for name, c in (("scales_e", 0), ("scales_e", 1), ("codes_e", 0), ("codes_e", 1)):
+            gather(name, c)
+        ents = {0: entity(0)}
         prods = {}
         for step in range(TILES + SCORE_LAG + 1):
-            c, k = divmod(step, TILES_PER_CHUNK)
-            if c + 1 < CHUNKS:
-                gather_part(c + 1, k)
-            if step == 0:
-                for j in range(RELATION_AHEAD):
-                    rels[j] = relation(j)
-            if step < TILES:
-                prods[step] = products(step, rels[step])
+            if step + 1 < TILES:
+                ents[step + 1] = entity(step + 1)
             if step + RELATION_AHEAD < TILES:
                 rels[step + RELATION_AHEAD] = relation(step + RELATION_AHEAD)
+            if step < TILES:
+                prods[step] = products(step, rels[step], *ents[step])
+            for name, c in GATHERS_AT.get(step, ()):
+                gather(name, c)
             for i in range(TILES):
-                if i + (POOL_LAG if i in POOL_TILES else TURN_LAG) == step:
+                if i + (POOL_LAG if i in POOL_TILES + SUM_TILES else TURN_LAG) == step:
                     turn(i, prods[i])
             for first, count in SCORE_GROUPS:
                 if first + count - 1 == step - SCORE_LAG:

@@ -27,16 +27,17 @@ CHUNKS = J // CHUNK
 TILES = J // TILE
 TILES_PER_CHUNK = CHUNK // TILE
 TABLE_PIECES = 4
-POOL_TILES = (1, 4, 6, 9, 11, 13)
-SUM_TILES = (2, 5, 7, 10, 12)
+POOL_TILES = ()
+SUM_TILES = ()
 POOL_LAG = 2
 TURN_LAG = 1
 RELATION_AHEAD = 5
 SCORE_GROUPS = ((0, 4), (4, 4), (8, 4), (12, 2), (14, 1), (15, 1))
+QUANT_LAG = 2
 SCORE_LAG = 3
 TABLE_ROW = 8
 WEIGHT_ROW = 4
-GATHERS_AT = {2: (("codes_r", 2),), 3: (("scales_e", 2), ("codes_e", 2)), 7: (("scales_e", 3), ("codes_e", 3))}
+GATHERS_AT = {2: (("codes_r", 2),), 6: (("codes_e", 2),), 10: (("scales_e", 3), ("codes_e", 3))}
 
 
 def tile_list_ckg_sig_kernel(
@@ -115,17 +116,21 @@ def tile_list_ckg_sig_kernel(
             nc.sync.dma_start(out=dst, in_=src)
 
         sources = {
-            "scales_r": (tabs_r, list_r, U8, 4), "codes_r": (tab_r, list_r, U32, 1),
-            "scales_e": (tabs_e, list_e, U8, 2), "codes_e": (tab_e, list_e, U32, 2),
+            "scales_r": (tabs_r, list_r, U8), "codes_r": (tab_r, list_r, U32),
+            "scales_e": (tabs_e, list_e, U8), "codes_e": (tab_e, list_e, U32),
         }
         picked = {}
+        late_codes = keep.tile([P, 2 * CHUNK], U32, name="late_codes", align_bytes=64)
 
         def gather(name, c):
-            window, offsets, dtype, bufs = sources[name]
+            window, offsets, dtype = sources[name]
             chunks = 2 if (name, c) == ("codes_r", 2) else 1
-            tag = "codes_r_first" if (name, c) == ("codes_r", 0) else name
-            wide = 2 if tag == "codes_r" else 1
-            taken = take(tag, keep, [P, wide * CHUNK], dtype, bufs)[:, : chunks * CHUNK]
+            if name == "codes_r" and c > 0:
+                taken = late_codes[:, : chunks * CHUNK]
+            elif name[-1] == "e" and c >= (3 if name == "scales_e" else 2):
+                taken = picked[name[:-1] + "r", c]
+            else:
+                taken = keep.tile([P, CHUNK], dtype, name="%s_%d" % (name, c), align_bytes=64)[:]
             columns = slice(c * CHUNK // 16, (c + chunks) * CHUNK // 16)
             nc.vector.tensor_copy(taken, window[:].bitcast(dtype).indirect(offsets[:, columns]))
             for n in range(chunks):
@@ -214,21 +219,28 @@ def tile_list_ckg_sig_kernel(
                 return
             for part in range(2):
                 acc = bank("for_scalar")[:].rearrange("p (t n) -> p t n", t=PACK)
-                for t in range(PACK):
-                    for term in range(2):
+                for term in range(2):
+                    for t in range(PACK):
                         nc.tensor.matmul(
                             acc[:, t, :], lhsT=prod[:, part + 2 * term, t * P : (t + 1) * P], rhs=ident[:],
-                            start=(term == 0), stop=(term == 1), is_transpose=True,
+                            start=(term == 0 and t == 0), stop=(term == 1 and t == PACK - 1), is_transpose=True,
                         )
                 nc.scalar.copy(h_bf[first][:, part, tokens, :], acc.rearrange("p t n -> p n t"))
 
-        def score(first, count):
+        packed = {}
+
+        def quantise(first, count):
             width = count * TILE
             h_codes = keep.tile([P, 2 * width], U32, name="h_codes_%d" % first, align_bytes=64)
             h_scales = keep.tile([P, 2 * width], U8, name="h_scales_%d" % first, align_bytes=64)
             nc.vector.quantize_mx(
                 out=h_codes[:].bitcast(FP8X4), scales=h_scales[:], in_=h_bf[first][:].rearrange("p h n t -> p (h n t)"),
             )
+            packed[first] = (h_codes, h_scales)
+
+        def score(first, count):
+            width = count * TILE
+            h_codes, h_scales = packed[first]
             per_bank = min(2, CHUNK // width)
             span = CHUNK if width == CHUNK else TILE
             for n in range(2 // per_bank):
@@ -255,7 +267,7 @@ def tile_list_ckg_sig_kernel(
         gather("codes_r", 0)
         gather("codes_r", 1)
         rels = {j: relation(j) for j in range(RELATION_AHEAD)}
-        for name, c in (("scales_e", 0), ("scales_e", 1), ("codes_e", 0), ("codes_e", 1)):
+        for name, c in (("scales_e", 0), ("scales_e", 1), ("scales_e", 2), ("codes_e", 0), ("codes_e", 1)):
             gather(name, c)
         ents = {0: entity(0)}
         prods = {}
@@ -271,6 +283,9 @@ def tile_list_ckg_sig_kernel(
             for i in range(TILES):
                 if i + (POOL_LAG if i in POOL_TILES + SUM_TILES else TURN_LAG) == step:
                     turn(i, prods[i])
+            for first, count in SCORE_GROUPS:
+                if first + count - 1 == step - QUANT_LAG:
+                    quantise(first, count)
             for first, count in SCORE_GROUPS:
                 if first + count - 1 == step - SCORE_LAG:
                     score(first, count)

@@ -27,17 +27,21 @@ CHUNKS = J // CHUNK
 TILES = J // TILE
 TILES_PER_CHUNK = CHUNK // TILE
 TABLE_PIECES = 4
-POOL_TILES = ()
-SUM_TILES = ()
-POOL_LAG = 2
+POOL_TILES = (1, 4, 7, 10, 13)
+SUM_TILES = (2, 5, 8, 11, 14)
+VECTOR_SUM_TILES = ()
+POOL_LAG = 1
 TURN_LAG = 1
 RELATION_AHEAD = 5
 SCORE_GROUPS = ((0, 4), (4, 4), (8, 4), (12, 2), (14, 1), (15, 1))
-QUANT_LAG = 2
-SCORE_LAG = 3
-TABLE_ROW = 8
+QUANT_LAG = 3
+SCORE_LAG = 4
+TABLE_ROW = 4
 WEIGHT_ROW = 4
-GATHERS_AT = {2: (("codes_r", 2),), 6: (("codes_e", 2),), 10: (("scales_e", 3), ("codes_e", 3))}
+GATHERS_AT = {2: (("codes_r", 2),), 5: (("codes_e", 2),), 9: (("scales_e", 3), ("codes_e", 3))}
+TILE_AFTER = {("scales_e", 3): ("scales_e", 1), ("codes_e", 2): ("codes_e", 0), ("codes_e", 3): ("codes_e", 1)}
+PROD_DEPTH = 5
+ENT_DEPTH = 2
 
 
 def tile_list_ckg_sig_kernel(
@@ -92,7 +96,7 @@ def tile_list_ckg_sig_kernel(
             plane = keep.tile([P, columns // 4], I32, name=name + "_plane", align_bytes=64)
             nc.vector.memset(plane[:], 0)
             return (
-                codes[:], plane[:].bitcast(U8)[row:P, :], (codes[:].bitcast(I32), flat_words.bitcast(I32)),
+                codes[:], plane[:].bitcast(U8), (codes[:].bitcast(I32), flat_words.bitcast(I32)),
                 plane_loads(plane, scales, row),
             )
 
@@ -115,6 +119,19 @@ def tile_list_ckg_sig_kernel(
         for dst, src in loads:
             nc.sync.dma_start(out=dst, in_=src)
 
+        def reorder(name, source, dtype):
+            ordered = keep.tile([P, PACK, R // PACK], dtype, name=name, align_bytes=64)
+            nc.vector.tensor_copy(ordered[:], source.bitcast(dtype).rearrange("p (m t) -> p t m", t=PACK))
+            return ordered[:].rearrange("p t m -> p (t m)")
+
+        def deal(name, w, dtype, row):
+            return reorder(name + "_codes", w[0], dtype), reorder(name + "_order", w[1], U8)[row:P, :]
+
+        wrr = deal("wrr", wrr, I32, WEIGHT_ROW)
+        wri = deal("wri", wri, I32, WEIGHT_ROW)
+        wer = deal("wer", wer, U16, 0)
+        wei = deal("wei", wei, U16, 0)
+
         sources = {
             "scales_r": (tabs_r, list_r, U8), "codes_r": (tab_r, list_r, U32),
             "scales_e": (tabs_e, list_e, U8), "codes_e": (tab_e, list_e, U32),
@@ -127,8 +144,8 @@ def tile_list_ckg_sig_kernel(
             chunks = 2 if (name, c) == ("codes_r", 2) else 1
             if name == "codes_r" and c > 0:
                 taken = late_codes[:, : chunks * CHUNK]
-            elif name[-1] == "e" and c >= (3 if name == "scales_e" else 2):
-                taken = picked[name[:-1] + "r", c]
+            elif (name, c) in TILE_AFTER:
+                taken = picked[TILE_AFTER[name, c]]
             else:
                 taken = keep.tile([P, CHUNK], dtype, name="%s_%d" % (name, c), align_bytes=64)[:]
             columns = slice(c * CHUNK // 16, (c + chunks) * CHUNK // 16)
@@ -136,61 +153,59 @@ def tile_list_ckg_sig_kernel(
             for n in range(chunks):
                 picked[name, c + n] = taken[:, n * CHUNK : (n + 1) * CHUNK]
 
-        def dealt(flat, i):
-            if i in SUM_TILES:
-                return flat.rearrange("p (u m e) -> p u m e", u=2, e=2)
-            return flat.rearrange("p (t m) -> p t m", t=PACK)
+        channel_major = SUM_TILES + VECTOR_SUM_TILES
 
         def project(tag, side, i, w, fmt, row):
             c, k = divmod(i, TILES_PER_CHUNK)
             cols = slice(k * TILE, (k + 1) * TILE)
+            codes = picked["codes_" + side, c][:, cols].bitcast(FP8X4)
             acc = bank(tag)
+            if i in channel_major:
+                slots = acc[:].rearrange("p (t n) -> p t n", t=PACK)
+                for t in range(PACK):
+                    nc.tensor.matmul_mx(
+                        out=slots[:, t, :], lhsT=w[0][:, t * P : (t + 1) * P].bitcast(fmt),
+                        lhsT_scale=w[1][:, t * P : (t + 1) * P],
+                        rhs=codes, rhs_scale=picked["scales_" + side, c][row:P, cols], start=True, stop=True,
+                    )
+                return slots.rearrange("p t n -> p n t")
             nc.tensor.matmul_mx(
-                out=acc[:], lhsT=picked["codes_" + side, c][:, cols].bitcast(FP8X4),
-                lhsT_scale=picked["scales_" + side, c][row:P, cols],
+                out=acc[:], lhsT=codes, lhsT_scale=picked["scales_" + side, c][row:P, cols],
                 rhs=w[0].bitcast(fmt), rhs_scale=w[1], start=True, stop=True,
             )
-            if i in SUM_TILES:
-                return acc[:].rearrange("p (m u e) -> p u m e", u=2, e=2)
-            return acc[:].rearrange("p (m t) -> p t m", t=PACK)
+            return acc[:]
+
+        def shaped(flat, i):
+            return flat.rearrange("p (n t) -> p n t", t=PACK) if i in channel_major else flat
 
         def relation(i):
             rel = take("rel", keep, [P, 2, R], F32, RELATION_AHEAD + 1)
             for part, w in enumerate((wrr, wri)):
-                nc.scalar.copy(dealt(rel[:, part], i), project("for_scalar", "r", i, w, FP8X4, TABLE_ROW))
+                nc.scalar.copy(shaped(rel[:, part], i), project("for_scalar", "r", i, w, FP8X4, TABLE_ROW))
             return rel
 
         def entity(i):
             return project("for_vector", "e", i, wer, FP4X4, 0), project("for_vector", "e", i, wei, FP4X4, 0)
 
         def products(i, rel, aer, aei):
-            prod = take("prod", keep, [P, 4, R], F32, 5)
-            arr, ari = dealt(rel[:, 0], i), dealt(rel[:, 1], i)
-            term = [dealt(prod[:, n], i) for n in range(4)]
-            if i in SUM_TILES:
-                nc.vector.tensor_tensor(term[0], aer, arr, MULT)
-                nc.vector.tensor_tensor(term[2], aei, ari, MULT)
-                nc.vector.tensor_tensor(term[1], aer, ari, MULT)
-                nc.vector.tensor_tensor(term[3], aei, arr, MULT)
+            prod = take("prod", keep, [P, 4, R], F32, PROD_DEPTH)
+            if i in channel_major:
+                for pair, ent_acc in enumerate((aer, aei)):
+                    nc.vector.tensor_tensor(
+                        prod[:, 2 * pair : 2 * pair + 2].rearrange("p h (n t) -> p h n t", t=PACK),
+                        ent_acc.unsqueeze(1).broadcast_to([P, 2, TILE, PACK]),
+                        rel[:].rearrange("p h (n t) -> p h n t", t=PACK), MULT,
+                    )
                 return prod
             if i in POOL_TILES:
-                ent = take("ent", keep, [P, R], F32, 2)
-                nc.scalar.copy(dealt(ent[:], i), aer)
+                ent = take("ent", keep, [P, R], F32, ENT_DEPTH)
+                nc.scalar.copy(ent[:], aer)
                 nc.gpsimd.tensor_tensor(prod[:, 0], ent[:], rel[:, 0], MULT)
                 nc.gpsimd.tensor_tensor(prod[:, 1], ent[:], rel[:, 1], MULT)
-                nc.vector.scalar_tensor_tensor(term[2], aei, -1.0, ari, MULT, MULT)
-            elif i == TILES - 1:
-                nc.vector.tensor_tensor(term[0], aer, arr, MULT)
-                nc.vector.scalar_tensor_tensor(term[2], aei, -1.0, ari, MULT, MULT)
-                nc.vector.tensor_tensor(term[1], aer, ari, MULT)
             else:
-                nc.vector.tensor_tensor(
-                    prod[:, 0:2].rearrange("p h (t m) -> p h t m", t=PACK),
-                    aer.unsqueeze(1).broadcast_to([P, 2, PACK, TILE]),
-                    rel[:].rearrange("p h (t m) -> p h t m", t=PACK), MULT,
-                )
-                nc.vector.scalar_tensor_tensor(term[2], aei, -1.0, ari, MULT, MULT)
-            nc.vector.tensor_tensor(term[3], aei, arr, MULT)
+                nc.vector.tensor_tensor(prod[:, 0:2], aer.unsqueeze(1).broadcast_to([P, 2, R]), rel[:], MULT)
+            nc.vector.scalar_tensor_tensor(prod[:, 2], aei, -1.0, rel[:, 1], MULT, MULT)
+            nc.vector.tensor_tensor(prod[:, 3], aei, rel[:, 0], MULT)
             return prod
 
         group_of = {}
@@ -199,33 +214,27 @@ def tile_list_ckg_sig_kernel(
                 group_of[i] = (first, count)
         h_bf = {}
 
-        def turn(i, prod):
+        def rounded(i):
             first, count = group_of[i]
             if first not in h_bf:
                 h_bf[first] = keep.tile([P, 2, count * TILE, PACK], BF16, name="h_bf_%d" % first, align_bytes=64)
-            tokens = slice((i - first) * TILE, (i - first + 1) * TILE)
-            if i in SUM_TILES:
-                rounded = take("rounded", keep, [P, 2, R], BF16, 2)
-                nc.gpsimd.tensor_tensor(rounded[:, 0], prod[:, 0], prod[:, 2], SUBTRACT)
-                nc.gpsimd.tensor_tensor(rounded[:, 1], prod[:, 1], prod[:, 3], ADD)
-                pairs = rounded[:].rearrange("p h r -> p (h r)").bitcast(F32)
-                acc = bank("for_scalar")[:].rearrange("p (t n) -> p t n", t=PACK)
-                for slot in range(PACK):
+            return h_bf[first][:, :, (i - first) * TILE : (i - first + 1) * TILE, :]
+
+        def add_terms(i, prod):
+            engine = nc.gpsimd if i in SUM_TILES else nc.vector
+            flat = rounded(i).rearrange("p h n t -> p h (n t)")
+            engine.tensor_tensor(flat[:, 0], prod[:, 0], prod[:, 3], SUBTRACT)
+            engine.tensor_tensor(flat[:, 1], prod[:, 1], prod[:, 2], ADD)
+
+        def turn(i, prod, part):
+            acc = bank("for_scalar")[:].rearrange("p (t n) -> p t n", t=PACK)
+            for term in range(2):
+                for t in range(PACK):
                     nc.tensor.matmul(
-                        acc[:, slot, :], lhsT=pairs[:, slot * P : (slot + 1) * P], rhs=ident[:],
-                        start=True, stop=True, is_transpose=True,
+                        acc[:, t, :], lhsT=prod[:, part + 2 * term, t * P : (t + 1) * P], rhs=ident[:],
+                        start=(term == 0 and t == 0), stop=(term == 1 and t == PACK - 1), is_transpose=True,
                     )
-                nc.scalar.copy(h_bf[first][:, :, tokens, :].bitcast(F32), acc.rearrange("p (h u) n -> p h n u", u=2))
-                return
-            for part in range(2):
-                acc = bank("for_scalar")[:].rearrange("p (t n) -> p t n", t=PACK)
-                for term in range(2):
-                    for t in range(PACK):
-                        nc.tensor.matmul(
-                            acc[:, t, :], lhsT=prod[:, part + 2 * term, t * P : (t + 1) * P], rhs=ident[:],
-                            start=(term == 0 and t == 0), stop=(term == 1 and t == PACK - 1), is_transpose=True,
-                        )
-                nc.scalar.copy(h_bf[first][:, part, tokens, :], acc.rearrange("p t n -> p n t"))
+            nc.scalar.copy(rounded(i)[:, part], acc.rearrange("p t n -> p n t"))
 
         packed = {}
 
@@ -272,20 +281,27 @@ def tile_list_ckg_sig_kernel(
         ents = {0: entity(0)}
         prods = {}
         for step in range(TILES + SCORE_LAG + 1):
+            due = [
+                i for i in range(TILES)
+                if i not in channel_major and i + (POOL_LAG if i in POOL_TILES else TURN_LAG) == step
+            ]
+            for i in due:
+                turn(i, prods[i], 0)
             if step + 1 < TILES:
                 ents[step + 1] = entity(step + 1)
             if step + RELATION_AHEAD < TILES:
                 rels[step + RELATION_AHEAD] = relation(step + RELATION_AHEAD)
-            if step < TILES:
-                prods[step] = products(step, rels[step], *ents[step])
-            for name, c in GATHERS_AT.get(step, ()):
-                gather(name, c)
-            for i in range(TILES):
-                if i + (POOL_LAG if i in POOL_TILES + SUM_TILES else TURN_LAG) == step:
-                    turn(i, prods[i])
-            for first, count in SCORE_GROUPS:
-                if first + count - 1 == step - QUANT_LAG:
-                    quantise(first, count)
             for first, count in SCORE_GROUPS:
                 if first + count - 1 == step - SCORE_LAG:
                     score(first, count)
+            for i in due:
+                turn(i, prods[i], 1)
+            if step < TILES:
+                prods[step] = products(step, rels[step], *ents[step])
+            if step in channel_major:
+                add_terms(step, prods[step])
+            for name, c in GATHERS_AT.get(step, ()):
+                gather(name, c)
+            for first, count in SCORE_GROUPS:
+                if first + count - 1 == step - QUANT_LAG:
+                    quantise(first, count)

@@ -26,20 +26,21 @@ TILE = 128
 CHUNKS = J // CHUNK
 TILES = J // TILE
 TILES_PER_CHUNK = CHUNK // TILE
-TABLE_PIECES = 4
+TABLE_PIECES = 1
 POOL_TILES = (1, 4, 7, 10, 13)
 SUM_TILES = (2, 5, 8, 11, 14)
 VECTOR_SUM_TILES = ()
 POOL_LAG = 1
 TURN_LAG = 1
-RELATION_AHEAD = 5
+RELATION_AHEAD = 2
 SCORE_GROUPS = ((0, 4), (4, 4), (8, 4), (12, 2), (14, 1), (15, 1))
 QUANT_LAG = 3
 SCORE_LAG = 4
-TABLE_ROW = 4
-WEIGHT_ROW = 4
-GATHERS_AT = {2: (("codes_r", 2),), 5: (("codes_e", 2),), 9: (("scales_e", 3), ("codes_e", 3))}
-TILE_AFTER = {("scales_e", 3): ("scales_e", 1), ("codes_e", 2): ("codes_e", 0), ("codes_e", 3): ("codes_e", 1)}
+TABLE_ROW = 0
+WRR_ROW = 4
+WRI_ROW = 8
+GATHERS_AT = {3: (("codes_r", 2),), 6: (("codes_e", 2), ("codes_r", 3),), 9: (("scales_e", 3), ("codes_e", 3),)}
+TILE_AFTER = {("codes_r", 2): ("codes_e", 0), ("codes_e", 2): ("codes_r", 1), ("codes_r", 3): ("codes_e", 1), ("scales_e", 3): ("scales_e", 1), ("codes_e", 3): ("codes_r", 2)}
 PROD_DEPTH = 5
 ENT_DEPTH = 2
 
@@ -91,31 +92,34 @@ def tile_list_ckg_sig_kernel(
             step = T // TABLE_PIECES
             return [(table[:, c * step : (c + 1) * step], flat[:, c * step : (c + 1) * step]) for c in range(TABLE_PIECES)]
 
-        def weight(name, flat_words, scales, columns, row):
-            codes = keep.tile([P, flat_words.shape[1]], U8, name=name, align_bytes=64)
+        def zeroed(name, columns):
             plane = keep.tile([P, columns // 4], I32, name=name + "_plane", align_bytes=64)
             nc.vector.memset(plane[:], 0)
+            return plane
+
+        def weight(name, flat_words, scales, plane, row):
+            codes = keep.tile([P, flat_words.shape[1]], U8, name=name, align_bytes=64)
             return (
                 codes[:], plane[:].bitcast(U8), (codes[:].bitcast(I32), flat_words.bitcast(I32)),
                 plane_loads(plane, scales, row),
             )
 
-        wrr = weight("wrr", wrr_words[0].rearrange("p r i -> p (r i)"), wrr_scales, R, WEIGHT_ROW)
-        wri = weight("wri", wri_words[0].rearrange("p r i -> p (r i)"), wri_scales, R, WEIGHT_ROW)
+        shared = zeroed("relation", R)
+        wrr = weight("wrr", wrr_words[0].rearrange("p r i -> p (r i)"), wrr_scales, shared, WRR_ROW)
+        wri = weight("wri", wri_words[0].rearrange("p r i -> p (r i)"), wri_scales, shared, WRI_ROW)
         nc.vector.memset(tabs_e[:], 0)
-        wer = weight("wer", wer_words[0], wer_scales, R, 0)
-        wei = weight("wei", wei_words[0], wei_scales, R, 0)
-        nr = weight("nr", nr_words[0], nr_scales, N, 0)
-        ni = weight("ni", ni_words[0], ni_scales, N, 0)
+        wer = weight("wer", wer_words[0], wer_scales, zeroed("wer", R), 0)
+        wei = weight("wei", wei_words[0], wei_scales, zeroed("wei", R), 0)
+        nr = weight("nr", nr_words[0], nr_scales, zeroed("nr", N), 0)
+        ni = weight("ni", ni_words[0], ni_scales, zeroed("ni", N), 0)
         make_identity(nc, ident[:])
 
         big_r = table_loads(tab_r, tab2_words)
         big_e = table_loads(tab_e, tab_words)
-        loads = [(list_r[:], offs2), (list_e[:], offs)] + plane_loads(tabs_r, tab2_scales, TABLE_ROW) + [wrr[2], wri[2]]
-        loads += big_r[:2] + wrr[3] + wri[3][:2]
-        loads += big_r[2:] + wri[3][2:] + plane_loads(tabs_e, tab_scales, 0)
-        loads += big_e[:2] + [wer[2], wei[2]] + wer[3]
-        loads += big_e[2:3] + wei[3] + big_e[3:] + [nr[2], ni[2]] + nr[3] + ni[3]
+        loads = [(list_r[:], offs2), wer[2], wei[2]] + plane_loads(tabs_r, tab2_scales, TABLE_ROW) + [(list_e[:], offs)]
+        loads += plane_loads(tabs_e, tab_scales, 0) + [wrr[2], wri[2]] + wrr[3] + wri[3] + wer[3][:1]
+        loads += big_r + big_e + wei[3][:3] + wer[3][1:3] + wer[3][3:] + wei[3][3:]
+        loads += [nr[2], ni[2]] + nr[3] + ni[3]
         for dst, src in loads:
             nc.sync.dma_start(out=dst, in_=src)
 
@@ -124,34 +128,26 @@ def tile_list_ckg_sig_kernel(
             nc.vector.tensor_copy(ordered[:], source.bitcast(dtype).rearrange("p (m t) -> p t m", t=PACK))
             return ordered[:].rearrange("p t m -> p (t m)")
 
-        def deal(name, w, dtype, row):
-            return reorder(name + "_codes", w[0], dtype), reorder(name + "_order", w[1], U8)[row:P, :]
-
-        wrr = deal("wrr", wrr, I32, WEIGHT_ROW)
-        wri = deal("wri", wri, I32, WEIGHT_ROW)
-        wer = deal("wer", wer, U16, 0)
-        wei = deal("wei", wei, U16, 0)
+        relation_order = reorder("relation_order", wrr[1], U8)
+        wrr = (reorder("wrr_codes", wrr[0], I32), relation_order[WRR_ROW:P, :])
+        wri = (reorder("wri_codes", wri[0], I32), relation_order[WRI_ROW:P, :])
+        wer = (reorder("wer_codes", wer[0], U16), reorder("wer_order", wer[1], U8))
+        wei = (reorder("wei_codes", wei[0], U16), reorder("wei_order", wei[1], U8))
 
         sources = {
             "scales_r": (tabs_r, list_r, U8), "codes_r": (tab_r, list_r, U32),
             "scales_e": (tabs_e, list_e, U8), "codes_e": (tab_e, list_e, U32),
         }
         picked = {}
-        late_codes = keep.tile([P, 2 * CHUNK], U32, name="late_codes", align_bytes=64)
 
         def gather(name, c):
             window, offsets, dtype = sources[name]
-            chunks = 2 if (name, c) == ("codes_r", 2) else 1
-            if name == "codes_r" and c > 0:
-                taken = late_codes[:, : chunks * CHUNK]
-            elif (name, c) in TILE_AFTER:
-                taken = picked[TILE_AFTER[name, c]]
+            if (name, c) in TILE_AFTER:
+                picked[name, c] = picked[TILE_AFTER[name, c]]
             else:
-                taken = keep.tile([P, CHUNK], dtype, name="%s_%d" % (name, c), align_bytes=64)[:]
-            columns = slice(c * CHUNK // 16, (c + chunks) * CHUNK // 16)
-            nc.vector.tensor_copy(taken, window[:].bitcast(dtype).indirect(offsets[:, columns]))
-            for n in range(chunks):
-                picked[name, c + n] = taken[:, n * CHUNK : (n + 1) * CHUNK]
+                picked[name, c] = keep.tile([P, CHUNK], dtype, name="%s_%d" % (name, c), align_bytes=64)
+            columns = slice(c * CHUNK // 16, (c + 1) * CHUNK // 16)
+            nc.vector.tensor_copy(picked[name, c][:], window[:].bitcast(dtype).indirect(offsets[:, columns]))
 
         channel_major = SUM_TILES + VECTOR_SUM_TILES
 

@@ -39,8 +39,8 @@ SCORE_LAG = 4
 TABLE_ROW = 0
 WRR_ROW = 4
 WRI_ROW = 8
-GATHERS_AT = {3: (("codes_r", 2),), 6: (("codes_e", 2), ("codes_r", 3),), 9: (("scales_e", 3), ("codes_e", 3),)}
-TILE_AFTER = {("codes_r", 2): ("codes_e", 0), ("codes_e", 2): ("codes_r", 1), ("codes_r", 3): ("codes_e", 1), ("scales_e", 3): ("scales_e", 1), ("codes_e", 3): ("codes_r", 2)}
+GATHERS_AT = {3: (("codes_r", 2),), 6: (("codes_e", 2), ("codes_r", 3),), 9: (("codes_e", 3),)}
+TILE_AFTER = {("codes_r", 2): ("codes_e", 0), ("codes_e", 2): ("codes_r", 1), ("codes_r", 3): ("codes_e", 1), ("codes_e", 3): ("codes_r", 2)}
 PROD_DEPTH = 5
 ENT_DEPTH = 2
 
@@ -78,8 +78,8 @@ def tile_list_ckg_sig_kernel(
         ident = keep.tile([P, P], F32, name="ident", align_bytes=64)
         warm = keep.tile([P, 2], F32, name="warm")
 
-        nc.gpsimd.memset(warm[:, 0:1], 0.0)
         nc.gpsimd.memset(tabs_r[:, : T // 8], 0)
+        nc.gpsimd.memset(warm[:, 0:1], 0.0)
         nc.vector.memset(tabs_r[:, T // 8 :], 0)
         nc.scalar.activation(warm[:, 1:2], warm[:, 0:1], SIGMOID)
 
@@ -117,22 +117,25 @@ def tile_list_ckg_sig_kernel(
         big_r = table_loads(tab_r, tab2_words)
         big_e = table_loads(tab_e, tab_words)
         loads = [(list_r[:], offs2), wer[2], wei[2]] + plane_loads(tabs_r, tab2_scales, TABLE_ROW) + [(list_e[:], offs)]
-        loads += plane_loads(tabs_e, tab_scales, 0) + [wrr[2], wri[2]] + wrr[3] + wri[3] + wer[3][:1]
-        loads += big_r + big_e + wei[3][:3] + wer[3][1:3] + wer[3][3:] + wei[3][3:]
+        loads += plane_loads(tabs_e, tab_scales, 0) + [wrr[2], wri[2]] + wrr[3] + wri[3] + wer[3][:2]
+        loads += big_r + wer[3][2:] + wei[3] + big_e
         loads += [nr[2], ni[2]] + nr[3] + ni[3]
         for dst, src in loads:
             nc.sync.dma_start(out=dst, in_=src)
 
-        def reorder(name, source, dtype):
+        def reorder(name, source, dtype, run):
             ordered = keep.tile([P, PACK, R // PACK], dtype, name=name, align_bytes=64)
-            nc.vector.tensor_copy(ordered[:], source.bitcast(dtype).rearrange("p (m t) -> p t m", t=PACK))
+            nc.vector.tensor_copy(
+                ordered[:].rearrange("p t (c i) -> p c t i", i=run),
+                source.bitcast(dtype).rearrange("p (c i t) -> p c t i", i=run, t=PACK),
+            )
             return ordered[:].rearrange("p t m -> p (t m)")
 
-        relation_order = reorder("relation_order", wrr[1], U8)
-        wrr = (reorder("wrr_codes", wrr[0], I32), relation_order[WRR_ROW:P, :])
-        wri = (reorder("wri_codes", wri[0], I32), relation_order[WRI_ROW:P, :])
-        wer = (reorder("wer_codes", wer[0], U16), reorder("wer_order", wer[1], U8))
-        wei = (reorder("wei_codes", wei[0], U16), reorder("wei_order", wei[1], U8))
+        relation_order = reorder("relation_order", wrr[1], U8, 16)
+        wrr = (reorder("wrr_codes", wrr[0], I32, 4), relation_order[WRR_ROW:P, :])
+        wri = (reorder("wri_codes", wri[0], I32, 4), relation_order[WRI_ROW:P, :])
+        wer = (reorder("wer_codes", wer[0], U16, 8), reorder("wer_order", wer[1], U8, 16))
+        wei = (reorder("wei_codes", wei[0], U16, 8), reorder("wei_order", wei[1], U8, 16))
 
         sources = {
             "scales_r": (tabs_r, list_r, U8), "codes_r": (tab_r, list_r, U32),
@@ -140,14 +143,16 @@ def tile_list_ckg_sig_kernel(
         }
         picked = {}
 
-        def gather(name, c):
+        def gather(name, c, chunks=1):
             window, offsets, dtype = sources[name]
             if (name, c) in TILE_AFTER:
-                picked[name, c] = picked[TILE_AFTER[name, c]]
+                taken = picked[TILE_AFTER[name, c]]
             else:
-                picked[name, c] = keep.tile([P, CHUNK], dtype, name="%s_%d" % (name, c), align_bytes=64)
-            columns = slice(c * CHUNK // 16, (c + 1) * CHUNK // 16)
-            nc.vector.tensor_copy(picked[name, c][:], window[:].bitcast(dtype).indirect(offsets[:, columns]))
+                taken = keep.tile([P, chunks * CHUNK], dtype, name="%s_%d" % (name, c), align_bytes=64)[:]
+            columns = slice(c * CHUNK // 16, (c + chunks) * CHUNK // 16)
+            nc.vector.tensor_copy(taken, window[:].bitcast(dtype).indirect(offsets[:, columns]))
+            for n in range(chunks):
+                picked[name, c + n] = taken[:, n * CHUNK : (n + 1) * CHUNK]
 
         channel_major = SUM_TILES + VECTOR_SUM_TILES
 
@@ -267,13 +272,13 @@ def tile_list_ckg_sig_kernel(
                 rows = out[P * n * per_bank : P * (n + 1) * per_bank, first * TILE : first * TILE + width]
                 nc.sync.dma_start(out=rows.rearrange("(h p) n -> p h n", p=P), in_=result[:])
 
-        for c in range(CHUNKS):
-            gather("scales_r", c)
+        gather("scales_r", 0, CHUNKS)
         gather("codes_r", 0)
         gather("codes_r", 1)
         rels = {j: relation(j) for j in range(RELATION_AHEAD)}
-        for name, c in (("scales_e", 0), ("scales_e", 1), ("scales_e", 2), ("codes_e", 0), ("codes_e", 1)):
-            gather(name, c)
+        gather("scales_e", 0, CHUNKS)
+        gather("codes_e", 0)
+        gather("codes_e", 1)
         ents = {0: entity(0)}
         prods = {}
         for step in range(TILES + SCORE_LAG + 1):

@@ -39,8 +39,8 @@ SCORE_LAG = 4
 TABLE_ROW = 0
 WRR_ROW = 4
 WRI_ROW = 8
-GATHERS_AT = {3: (("codes_r", 2),), 6: (("codes_e", 2), ("codes_r", 3),), 9: (("codes_e", 3),)}
-TILE_AFTER = {("codes_r", 2): ("codes_e", 0), ("codes_e", 2): ("codes_r", 1), ("codes_r", 3): ("codes_e", 1), ("codes_e", 3): ("codes_r", 2)}
+GATHERS_AT = {3: (("codes_r", 3),), 6: (("codes_e", 2),), 9: (("codes_e", 3),)}
+TILE_AFTER = {("codes_r", 3): ("codes_e", 0), ("codes_e", 2): ("codes_r", 1), ("codes_e", 3): ("codes_e", 1)}
 PROD_DEPTH = 5
 ENT_DEPTH = 2
 
@@ -123,19 +123,19 @@ def tile_list_ckg_sig_kernel(
         for dst, src in loads:
             nc.sync.dma_start(out=dst, in_=src)
 
-        def reorder(name, source, dtype, run):
+        def reorder(name, source, dtype, run, engine):
             ordered = keep.tile([P, PACK, R // PACK], dtype, name=name, align_bytes=64)
-            nc.vector.tensor_copy(
+            engine.tensor_copy(
                 ordered[:].rearrange("p t (c i) -> p c t i", i=run),
                 source.bitcast(dtype).rearrange("p (c i t) -> p c t i", i=run, t=PACK),
             )
             return ordered[:].rearrange("p t m -> p (t m)")
 
-        relation_order = reorder("relation_order", wrr[1], U8, 16)
-        wrr = (reorder("wrr_codes", wrr[0], I32, 4), relation_order[WRR_ROW:P, :])
-        wri = (reorder("wri_codes", wri[0], I32, 4), relation_order[WRI_ROW:P, :])
-        wer = (reorder("wer_codes", wer[0], U16, 8), reorder("wer_order", wer[1], U8, 16))
-        wei = (reorder("wei_codes", wei[0], U16, 8), reorder("wei_order", wei[1], U8, 16))
+        relation_order = reorder("relation_order", wrr[1], U8, 16, nc.gpsimd)
+        wrr = (reorder("wrr_codes", wrr[0], I32, 4, nc.gpsimd), relation_order[WRR_ROW:P, :])
+        wri = (reorder("wri_codes", wri[0], I32, 4, nc.gpsimd), relation_order[WRI_ROW:P, :])
+        wer = (reorder("wer_codes", wer[0], U16, 8, nc.vector), reorder("wer_order", wer[1], U8, 16, nc.gpsimd))
+        wei = (reorder("wei_codes", wei[0], U16, 8, nc.vector), reorder("wei_order", wei[1], U8, 16, nc.gpsimd))
 
         sources = {
             "scales_r": (tabs_r, list_r, U8), "codes_r": (tab_r, list_r, U32),
@@ -275,6 +275,7 @@ def tile_list_ckg_sig_kernel(
         gather("scales_r", 0, CHUNKS)
         gather("codes_r", 0)
         gather("codes_r", 1)
+        gather("codes_r", 2)
         rels = {j: relation(j) for j in range(RELATION_AHEAD)}
         gather("scales_e", 0, CHUNKS)
         gather("codes_e", 0)

@@ -3,7 +3,7 @@ from contextlib import ExitStack
 import concourse.mybir as mybir
 from concourse.masks import make_identity
 
-K, L, R, N, T, J = 512, 512, 512, 256, 4096, 2048
+R, N, T, J = 512, 256, 4096, 2048
 FLOPS = 5368709120
 
 F32 = mybir.dt.float32
@@ -21,28 +21,28 @@ SIGMOID = mybir.ActivationFunctionType.Sigmoid
 
 P = 128
 PACK = 4
+LINE = 16
 CHUNK = 512
 TILE = 128
 CHUNKS = J // CHUNK
 TILES = J // TILE
 TILES_PER_CHUNK = CHUNK // TILE
-TABLE_PIECES = 1
-POOL_TILES = (1, 4, 7, 10, 13)
-SUM_TILES = (2, 5, 8, 11, 14)
-VECTOR_SUM_TILES = ()
-POOL_LAG = 1
-TURN_LAG = 1
+
+POOL_PRODUCT_TILES = tuple(range(1, TILES, 3))
+POOL_SUM_TILES = tuple(range(2, TILES, 3))
+
 RELATION_AHEAD = 2
+PRODUCT_DEPTH = 5
+AER_DEPTH = 2
+BANKS = 4
+
 SCORE_GROUPS = ((0, 4), (4, 4), (8, 4), (12, 2), (14, 1), (15, 1))
-QUANT_LAG = 3
-SCORE_LAG = 4
-TABLE_ROW = 0
+QUANTISE_STEPS = POOL_SUM_TILES[-3:] + (TILES, TILES + 1, TILES + 2)
+LATE_GATHER_STEPS = {3: 2, 9: 3}
+
 WRR_ROW = 4
 WRI_ROW = 8
-GATHERS_AT = {3: (("codes_r", 3),), 6: (("codes_e", 2),), 9: (("codes_e", 3),)}
-TILE_AFTER = {("codes_r", 3): ("codes_e", 0), ("codes_e", 2): ("codes_r", 1), ("codes_e", 3): ("codes_e", 1)}
-PROD_DEPTH = 5
-ENT_DEPTH = 2
+WER_ROWS_AHEAD = 2
 
 
 def tile_list_ckg_sig_kernel(
@@ -54,76 +54,75 @@ def tile_list_ckg_sig_kernel(
         keep = ctx.enter_context(tc.tile_pool(name="keep", bufs=1))
         psum = ctx.enter_context(tc.psum_pool(name="psum", bufs=1))
 
-        held = {}
-        used = {}
+        rings = {}
+        uses = {}
 
-        def take(name, pool, shape, dtype, depth):
-            if name not in held:
-                held[name] = [pool.tile(shape, dtype, name="%s_%d" % (name, n), align_bytes=64) for n in range(depth)]
-            used[name] = used.get(name, -1) + 1
-            return held[name][used[name] % depth]
+        def next_of(name, depth, make):
+            if name not in rings:
+                rings[name] = [make("%s_%d" % (name, n)) for n in range(depth)]
+            uses[name] = uses.get(name, -1) + 1
+            return rings[name][uses[name] % depth]
+
+        def ring_tile(name, shape, depth):
+            return next_of(name, depth, lambda label: keep.tile(shape, F32, name=label, align_bytes=64))
 
         def bank(name):
-            if name not in held:
-                held[name] = [psum.tile([P, R], F32, name="%s_%d" % (name, n)) for n in range(4)]
-            used[name] = used.get(name, -1) + 1
-            return held[name][used[name] % 4]
+            return next_of(name, BANKS, lambda label: psum.tile([P, CHUNK], F32, name=label))
 
         list_e = keep.tile([P, J // 16], U16, name="list_e")
         list_r = keep.tile([P, J // 16], U16, name="list_r")
-        tab_e = keep.tile([P, T], I32, name="tab_e", align_bytes=64)
-        tab_r = keep.tile([P, T], I32, name="tab_r", align_bytes=64)
-        tabs_e = keep.tile([P, T // 4], I32, name="tabs_e", align_bytes=64)
-        tabs_r = keep.tile([P, T // 4], I32, name="tabs_r", align_bytes=64)
+        words_e = keep.tile([P, T], I32, name="words_e", align_bytes=64)
+        words_r = keep.tile([P, T], I32, name="words_r", align_bytes=64)
+        plane_e = keep.tile([P, T // 4], I32, name="plane_e", align_bytes=64)
+        plane_r = keep.tile([P, T // 4], I32, name="plane_r", align_bytes=64)
         ident = keep.tile([P, P], F32, name="ident", align_bytes=64)
         warm = keep.tile([P, 2], F32, name="warm")
 
-        nc.gpsimd.memset(tabs_r[:, : T // 8], 0)
+        nc.gpsimd.memset(plane_r[:, : T // 8], 0)
         nc.gpsimd.memset(warm[:, 0:1], 0.0)
-        nc.vector.memset(tabs_r[:, T // 8 :], 0)
+        nc.vector.memset(plane_r[:, T // 8 :], 0)
         nc.scalar.activation(warm[:, 1:2], warm[:, 0:1], SIGMOID)
 
-        def plane_loads(plane, scales, row):
+        def row_loads(plane, scales, first_row):
             rows = scales[0].bitcast(I32)
-            return [(plane[row + r : P : 32, :], rows[r:16:4, :]) for r in range(4)]
+            return [(plane[first_row + s : P : 32, :], rows[s:16:4, :]) for s in range(4)]
 
-        def table_loads(table, words):
-            flat = words[0].rearrange("p t i -> p (t i)").bitcast(I32)
-            step = T // TABLE_PIECES
-            return [(table[:, c * step : (c + 1) * step], flat[:, c * step : (c + 1) * step]) for c in range(TABLE_PIECES)]
+        def flat_words(words):
+            return words[0].rearrange("p c i -> p (c i)")
 
-        def zeroed(name, columns):
+        def zeroed_plane(name, columns):
             plane = keep.tile([P, columns // 4], I32, name=name + "_plane", align_bytes=64)
             nc.vector.memset(plane[:], 0)
             return plane
 
-        def weight(name, flat_words, scales, plane, row):
-            codes = keep.tile([P, flat_words.shape[1]], U8, name=name, align_bytes=64)
-            return (
-                codes[:], plane[:].bitcast(U8), (codes[:].bitcast(I32), flat_words.bitcast(I32)),
-                plane_loads(plane, scales, row),
-            )
+        def weight(name, words, scales, plane, first_row):
+            codes = keep.tile([P, words.shape[1]], U8, name=name, align_bytes=64)
+            return {
+                "codes": codes[:], "plane": plane[:].bitcast(U8),
+                "load": (codes[:].bitcast(I32), words.bitcast(I32)), "rows": row_loads(plane, scales, first_row),
+            }
 
-        shared = zeroed("relation", R)
-        wrr = weight("wrr", wrr_words[0].rearrange("p r i -> p (r i)"), wrr_scales, shared, WRR_ROW)
-        wri = weight("wri", wri_words[0].rearrange("p r i -> p (r i)"), wri_scales, shared, WRI_ROW)
-        nc.vector.memset(tabs_e[:], 0)
-        wer = weight("wer", wer_words[0], wer_scales, zeroed("wer", R), 0)
-        wei = weight("wei", wei_words[0], wei_scales, zeroed("wei", R), 0)
-        nr = weight("nr", nr_words[0], nr_scales, zeroed("nr", N), 0)
-        ni = weight("ni", ni_words[0], ni_scales, zeroed("ni", N), 0)
+        relation_plane = zeroed_plane("relation", R)
+        wrr = weight("wrr", flat_words(wrr_words), wrr_scales, relation_plane, WRR_ROW)
+        wri = weight("wri", flat_words(wri_words), wri_scales, relation_plane, WRI_ROW)
+        nc.vector.memset(plane_e[:], 0)
+        wer = weight("wer", wer_words[0], wer_scales, zeroed_plane("wer", R), 0)
+        wei = weight("wei", wei_words[0], wei_scales, zeroed_plane("wei", R), 0)
+        nr = weight("nr", nr_words[0], nr_scales, zeroed_plane("nr", N), 0)
+        ni = weight("ni", ni_words[0], ni_scales, zeroed_plane("ni", N), 0)
         make_identity(nc, ident[:])
 
-        big_r = table_loads(tab_r, tab2_words)
-        big_e = table_loads(tab_e, tab_words)
-        loads = [(list_r[:], offs2), wer[2], wei[2]] + plane_loads(tabs_r, tab2_scales, TABLE_ROW) + [(list_e[:], offs)]
-        loads += plane_loads(tabs_e, tab_scales, 0) + [wrr[2], wri[2]] + wrr[3] + wri[3] + wer[3][:2]
-        loads += big_r + wer[3][2:] + wei[3] + big_e
-        loads += [nr[2], ni[2]] + nr[3] + ni[3]
+        loads = [(list_r[:], offs2), wer["load"], wei["load"]] + row_loads(plane_r, tab2_scales, 0)
+        loads += [(list_e[:], offs)] + row_loads(plane_e, tab_scales, 0) + [wrr["load"], wri["load"]]
+        loads += wrr["rows"] + wri["rows"] + wer["rows"][:WER_ROWS_AHEAD]
+        loads += [(words_r[:], flat_words(tab2_words).bitcast(I32))] + wer["rows"][WER_ROWS_AHEAD:] + wei["rows"]
+        loads += [(words_e[:], flat_words(tab_words).bitcast(I32))]
+        loads += [nr["load"], ni["load"]] + nr["rows"] + ni["rows"]
         for dst, src in loads:
             nc.sync.dma_start(out=dst, in_=src)
 
-        def reorder(name, source, dtype, run, engine):
+        def reorder(name, source, dtype, size, engine):
+            run = LINE // size
             ordered = keep.tile([P, PACK, R // PACK], dtype, name=name, align_bytes=64)
             engine.tensor_copy(
                 ordered[:].rearrange("p t (c i) -> p c t i", i=run),
@@ -131,101 +130,97 @@ def tile_list_ckg_sig_kernel(
             )
             return ordered[:].rearrange("p t m -> p (t m)")
 
-        relation_order = reorder("relation_order", wrr[1], U8, 16, nc.gpsimd)
-        wrr = (reorder("wrr_codes", wrr[0], I32, 4, nc.gpsimd), relation_order[WRR_ROW:P, :])
-        wri = (reorder("wri_codes", wri[0], I32, 4, nc.gpsimd), relation_order[WRI_ROW:P, :])
-        wer = (reorder("wer_codes", wer[0], U16, 8, nc.vector), reorder("wer_order", wer[1], U8, 16, nc.gpsimd))
-        wei = (reorder("wei_codes", wei[0], U16, 8, nc.vector), reorder("wei_order", wei[1], U8, 16, nc.gpsimd))
+        relation_slots = reorder("relation_slots", wrr["plane"], U8, 1, nc.gpsimd)
+        slots_wrr = (reorder("wrr_slots", wrr["codes"], I32, 4, nc.gpsimd), relation_slots[WRR_ROW:P, :])
+        slots_wri = (reorder("wri_slots", wri["codes"], I32, 4, nc.gpsimd), relation_slots[WRI_ROW:P, :])
+        slots_wer = (
+            reorder("wer_slots", wer["codes"], U16, 2, nc.vector), reorder("wer_scales", wer["plane"], U8, 1, nc.gpsimd),
+        )
+        slots_wei = (
+            reorder("wei_slots", wei["codes"], U16, 2, nc.vector), reorder("wei_scales", wei["plane"], U8, 1, nc.gpsimd),
+        )
 
         sources = {
-            "scales_r": (tabs_r, list_r, U8), "codes_r": (tab_r, list_r, U32),
-            "scales_e": (tabs_e, list_e, U8), "codes_e": (tab_e, list_e, U32),
+            "scales_r": (plane_r, list_r, U8), "codes_r": (words_r, list_r, U32),
+            "scales_e": (plane_e, list_e, U8), "codes_e": (words_e, list_e, U32),
         }
         picked = {}
 
-        def gather(name, c, chunks=1):
+        def gather(name, chunk, count, into=None):
             window, offsets, dtype = sources[name]
-            if (name, c) in TILE_AFTER:
-                taken = picked[TILE_AFTER[name, c]]
-            else:
-                taken = keep.tile([P, chunks * CHUNK], dtype, name="%s_%d" % (name, c), align_bytes=64)[:]
-            columns = slice(c * CHUNK // 16, (c + chunks) * CHUNK // 16)
-            nc.vector.tensor_copy(taken, window[:].bitcast(dtype).indirect(offsets[:, columns]))
-            for n in range(chunks):
-                picked[name, c + n] = taken[:, n * CHUNK : (n + 1) * CHUNK]
+            if into is None:
+                into = keep.tile([P, count * CHUNK], dtype, name="%s_%d" % (name, chunk), align_bytes=64)[:]
+            columns = slice(chunk * CHUNK // 16, (chunk + count) * CHUNK // 16)
+            nc.vector.tensor_copy(into, window[:].bitcast(dtype).indirect(offsets[:, columns]))
+            for n in range(count):
+                picked[name, chunk + n] = into[:, n * CHUNK : (n + 1) * CHUNK]
 
-        channel_major = SUM_TILES + VECTOR_SUM_TILES
-
-        def project(tag, side, i, w, fmt, row):
-            c, k = divmod(i, TILES_PER_CHUNK)
-            cols = slice(k * TILE, (k + 1) * TILE)
-            codes = picked["codes_" + side, c][:, cols].bitcast(FP8X4)
-            acc = bank(tag)
-            if i in channel_major:
-                slots = acc[:].rearrange("p (t n) -> p t n", t=PACK)
+        def project(ring, side, i, slots, fmt):
+            chunk, place = divmod(i, TILES_PER_CHUNK)
+            tokens = slice(place * TILE, (place + 1) * TILE)
+            codes = picked["codes_" + side, chunk][:, tokens].bitcast(FP8X4)
+            scales = picked["scales_" + side, chunk][:, tokens]
+            acc = bank(ring)
+            if i in POOL_SUM_TILES:
+                by_slot = acc[:].rearrange("p (t n) -> p t n", t=PACK)
                 for t in range(PACK):
                     nc.tensor.matmul_mx(
-                        out=slots[:, t, :], lhsT=w[0][:, t * P : (t + 1) * P].bitcast(fmt),
-                        lhsT_scale=w[1][:, t * P : (t + 1) * P],
-                        rhs=codes, rhs_scale=picked["scales_" + side, c][row:P, cols], start=True, stop=True,
+                        out=by_slot[:, t, :], lhsT=slots[0][:, t * P : (t + 1) * P].bitcast(fmt),
+                        lhsT_scale=slots[1][:, t * P : (t + 1) * P],
+                        rhs=codes, rhs_scale=scales, start=True, stop=True,
                     )
-                return slots.rearrange("p t n -> p n t")
+                return by_slot.rearrange("p t n -> p n t")
             nc.tensor.matmul_mx(
-                out=acc[:], lhsT=codes, lhsT_scale=picked["scales_" + side, c][row:P, cols],
-                rhs=w[0].bitcast(fmt), rhs_scale=w[1], start=True, stop=True,
+                out=acc[:], lhsT=codes, lhsT_scale=scales,
+                rhs=slots[0].bitcast(fmt), rhs_scale=slots[1], start=True, stop=True,
             )
             return acc[:]
 
-        def shaped(flat, i):
-            return flat.rearrange("p (n t) -> p n t", t=PACK) if i in channel_major else flat
-
         def relation(i):
-            rel = take("rel", keep, [P, 2, R], F32, RELATION_AHEAD + 1)
-            for part, w in enumerate((wrr, wri)):
-                nc.scalar.copy(shaped(rel[:, part], i), project("for_scalar", "r", i, w, FP8X4, TABLE_ROW))
+            rel = ring_tile("rel", [P, 2, R], RELATION_AHEAD + 1)
+            for part, slots in enumerate((slots_wrr, slots_wri)):
+                target = rel[:, part]
+                if i in POOL_SUM_TILES:
+                    target = target.rearrange("p (n t) -> p n t", t=PACK)
+                nc.scalar.copy(target, project("for_scalar", "r", i, slots, FP8X4))
             return rel
 
         def entity(i):
-            return project("for_vector", "e", i, wer, FP4X4, 0), project("for_vector", "e", i, wei, FP4X4, 0)
+            return project("entity", "e", i, slots_wer, FP4X4), project("entity", "e", i, slots_wei, FP4X4)
 
         def products(i, rel, aer, aei):
-            prod = take("prod", keep, [P, 4, R], F32, PROD_DEPTH)
-            if i in channel_major:
-                for pair, ent_acc in enumerate((aer, aei)):
+            prod = ring_tile("prod", [P, 4, R], PRODUCT_DEPTH)
+            if i in POOL_SUM_TILES:
+                for pair, acc in enumerate((aer, aei)):
                     nc.vector.tensor_tensor(
                         prod[:, 2 * pair : 2 * pair + 2].rearrange("p h (n t) -> p h n t", t=PACK),
-                        ent_acc.unsqueeze(1).broadcast_to([P, 2, TILE, PACK]),
+                        acc.unsqueeze(1).broadcast_to([P, 2, TILE, PACK]),
                         rel[:].rearrange("p h (n t) -> p h n t", t=PACK), MULT,
                     )
                 return prod
-            if i in POOL_TILES:
-                ent = take("ent", keep, [P, R], F32, ENT_DEPTH)
-                nc.scalar.copy(ent[:], aer)
-                nc.gpsimd.tensor_tensor(prod[:, 0], ent[:], rel[:, 0], MULT)
-                nc.gpsimd.tensor_tensor(prod[:, 1], ent[:], rel[:, 1], MULT)
+            if i in POOL_PRODUCT_TILES:
+                aer_copy = ring_tile("aer_copy", [P, R], AER_DEPTH)
+                nc.scalar.copy(aer_copy[:], aer)
+                nc.gpsimd.tensor_tensor(prod[:, 0], aer_copy[:], rel[:, 0], MULT)
+                nc.gpsimd.tensor_tensor(prod[:, 1], aer_copy[:], rel[:, 1], MULT)
             else:
                 nc.vector.tensor_tensor(prod[:, 0:2], aer.unsqueeze(1).broadcast_to([P, 2, R]), rel[:], MULT)
             nc.vector.scalar_tensor_tensor(prod[:, 2], aei, -1.0, rel[:, 1], MULT, MULT)
             nc.vector.tensor_tensor(prod[:, 3], aei, rel[:, 0], MULT)
             return prod
 
-        group_of = {}
-        for first, count in SCORE_GROUPS:
-            for i in range(first, first + count):
-                group_of[i] = (first, count)
-        h_bf = {}
+        h_rounded = {}
 
         def rounded(i):
-            first, count = group_of[i]
-            if first not in h_bf:
-                h_bf[first] = keep.tile([P, 2, count * TILE, PACK], BF16, name="h_bf_%d" % first, align_bytes=64)
-            return h_bf[first][:, :, (i - first) * TILE : (i - first + 1) * TILE, :]
+            first, count = [group for group in SCORE_GROUPS if group[0] <= i][-1]
+            if first not in h_rounded:
+                h_rounded[first] = keep.tile([P, 2, count * TILE, PACK], BF16, name="h_%d" % first, align_bytes=64)
+            return h_rounded[first][:, :, (i - first) * TILE : (i - first + 1) * TILE, :]
 
         def add_terms(i, prod):
-            engine = nc.gpsimd if i in SUM_TILES else nc.vector
             flat = rounded(i).rearrange("p h n t -> p h (n t)")
-            engine.tensor_tensor(flat[:, 0], prod[:, 0], prod[:, 3], SUBTRACT)
-            engine.tensor_tensor(flat[:, 1], prod[:, 1], prod[:, 2], ADD)
+            nc.gpsimd.tensor_tensor(flat[:, 0], prod[:, 0], prod[:, 3], SUBTRACT)
+            nc.gpsimd.tensor_tensor(flat[:, 1], prod[:, 1], prod[:, 2], ADD)
 
         def turn(i, prod, part):
             acc = bank("for_scalar")[:].rearrange("p (t n) -> p t n", t=PACK)
@@ -237,34 +232,35 @@ def tile_list_ckg_sig_kernel(
                     )
             nc.scalar.copy(rounded(i)[:, part], acc.rearrange("p t n -> p n t"))
 
-        packed = {}
+        h_packed = {}
 
         def quantise(first, count):
             width = count * TILE
             h_codes = keep.tile([P, 2 * width], U32, name="h_codes_%d" % first, align_bytes=64)
             h_scales = keep.tile([P, 2 * width], U8, name="h_scales_%d" % first, align_bytes=64)
             nc.vector.quantize_mx(
-                out=h_codes[:].bitcast(FP8X4), scales=h_scales[:], in_=h_bf[first][:].rearrange("p h n t -> p (h n t)"),
+                out=h_codes[:].bitcast(FP8X4), scales=h_scales[:],
+                in_=h_rounded[first][:].rearrange("p h n t -> p (h n t)"),
             )
-            packed[first] = (h_codes, h_scales)
+            h_packed[first] = (h_codes, h_scales)
 
         def score(first, count):
             width = count * TILE
-            h_codes, h_scales = packed[first]
+            h_codes, h_scales = h_packed[first]
             per_bank = min(2, CHUNK // width)
             span = CHUNK if width == CHUNK else TILE
             for n in range(2 // per_bank):
                 acc = bank("for_scalar")[:, : per_bank * width].rearrange("p (h w) -> p h w", h=per_bank)
-                for slot in range(per_bank):
-                    half = n * per_bank + slot
+                for place in range(per_bank):
+                    half = n * per_bank + place
                     for begin in range(0, width, span):
                         for part, w in enumerate((nr, ni)):
-                            cols = slice(part * width + begin, part * width + begin + span)
+                            tokens = slice(part * width + begin, part * width + begin + span)
                             nc.tensor.matmul_mx(
-                                out=acc[:, slot, begin : begin + span],
-                                lhsT=w[0][:, 2 * P * half : 2 * P * (half + 1)].bitcast(FP4X4),
-                                lhsT_scale=w[1][:, P * half : P * (half + 1)],
-                                rhs=h_codes[:, cols].bitcast(FP8X4), rhs_scale=h_scales[:, cols],
+                                out=acc[:, place, begin : begin + span],
+                                lhsT=w["codes"][:, 2 * P * half : 2 * P * (half + 1)].bitcast(FP4X4),
+                                lhsT_scale=w["plane"][:, P * half : P * (half + 1)],
+                                rhs=h_codes[:, tokens].bitcast(FP8X4), rhs_scale=h_scales[:, tokens],
                                 start=(part == 0), stop=(part == 1),
                             )
                 result = keep.tile([P, per_bank, width], F32, name="result_%d_%d" % (first, n))
@@ -273,37 +269,33 @@ def tile_list_ckg_sig_kernel(
                 nc.sync.dma_start(out=rows.rearrange("(h p) n -> p h n", p=P), in_=result[:])
 
         gather("scales_r", 0, CHUNKS)
-        gather("codes_r", 0)
-        gather("codes_r", 1)
-        gather("codes_r", 2)
-        rels = {j: relation(j) for j in range(RELATION_AHEAD)}
+        gather("codes_r", 0, 1)
+        gather("codes_r", 1, 1)
+        gather("codes_r", 2, 2)
+        rels = {i: relation(i) for i in range(RELATION_AHEAD)}
         gather("scales_e", 0, CHUNKS)
-        gather("codes_e", 0)
-        gather("codes_e", 1)
+        gather("codes_e", 0, 1)
+        gather("codes_e", 1, 1)
         ents = {0: entity(0)}
         prods = {}
-        for step in range(TILES + SCORE_LAG + 1):
-            due = [
-                i for i in range(TILES)
-                if i not in channel_major and i + (POOL_LAG if i in POOL_TILES else TURN_LAG) == step
-            ]
-            for i in due:
-                turn(i, prods[i], 0)
+        for step in range(QUANTISE_STEPS[-1] + 2):
+            turns = 1 <= step <= TILES and step - 1 not in POOL_SUM_TILES
+            if turns:
+                turn(step - 1, prods[step - 1], 0)
             if step + 1 < TILES:
                 ents[step + 1] = entity(step + 1)
             if step + RELATION_AHEAD < TILES:
                 rels[step + RELATION_AHEAD] = relation(step + RELATION_AHEAD)
-            for first, count in SCORE_GROUPS:
-                if first + count - 1 == step - SCORE_LAG:
-                    score(first, count)
-            for i in due:
-                turn(i, prods[i], 1)
+            if step - 1 in QUANTISE_STEPS:
+                score(*SCORE_GROUPS[QUANTISE_STEPS.index(step - 1)])
+            if turns:
+                turn(step - 1, prods[step - 1], 1)
             if step < TILES:
                 prods[step] = products(step, rels[step], *ents[step])
-            if step in channel_major:
+            if step in POOL_SUM_TILES:
                 add_terms(step, prods[step])
-            for name, c in GATHERS_AT.get(step, ()):
-                gather(name, c)
-            for first, count in SCORE_GROUPS:
-                if first + count - 1 == step - QUANT_LAG:
-                    quantise(first, count)
+            if step in LATE_GATHER_STEPS:
+                chunk = LATE_GATHER_STEPS[step]
+                gather("codes_e", chunk, 1, into=picked["codes_e", chunk - 2])
+            if step in QUANTISE_STEPS:
+                quantise(*SCORE_GROUPS[QUANTISE_STEPS.index(step)])

@@ -28,21 +28,25 @@ CHUNKS = J // CHUNK
 TILES = J // TILE
 TILES_PER_CHUNK = CHUNK // TILE
 
-POOL_PRODUCT_TILES = tuple(range(1, TILES, 3))
-POOL_SUM_TILES = tuple(range(2, TILES, 3))
-
-RELATION_AHEAD = 2
-PRODUCT_DEPTH = 5
-AER_DEPTH = 2
-BANKS = 4
+KINDS = "BCBBCABCBBCABCBA"
+RELATION_AHEAD = 5
+POOL_AHEAD = 2
+POOL_LOADS = ()
+SYNC_LOADS = ("list_r", "wer", "wei", "rows_r", "list_e", "wrr", "wri", "rows_e", "wrr_123", "words_r", "wrr_4", "wri_rows", "wei_1", "words_e", "wei_234", "wer_rows", "nr", "ni", "nr_rows", "ni_rows")
+RELATION_PACE = (0, 2, 1, 1, 1, 1, 1, 1, 1, 1, 1)
+RELATION_DEPTH = 6
+PRODUCT_DEPTH = 6
+AER_DEPTH = 3
+SCALAR_BANKS = 4
+VECTOR_BANKS = 4
 
 SCORE_GROUPS = ((0, 4), (4, 4), (8, 4), (12, 2), (14, 1), (15, 1))
-QUANTISE_STEPS = POOL_SUM_TILES[-3:] + (TILES, TILES + 1, TILES + 2)
-LATE_GATHER_STEPS = {3: 2, 9: 3}
+QUANTISE_STEPS = (6, 10, 13, 16, 17, 18)
+LATE_GATHERS = {2: ("scales_e", 2, 1, "scales_e", 0), 3: ("codes_e", 2, 1, "codes_e", 0), 6: ("scales_e", 3, 1, "scales_e", 1), 7: ("codes_e", 3, 1, "codes_e", 1)}
+HEAD_GATHERS = (("scales_r", 0, 4), ("scales_e", 0, 1), ("scales_e", 1, 1), ("codes_r", 0, 1), ("codes_r", 1, 1), ("codes_r", 2, 2), ("codes_e", 0, 1), ("codes_e", 1, 1))
 
 WRR_ROW = 4
 WRI_ROW = 8
-WER_ROWS_AHEAD = 2
 
 
 def tile_list_ckg_sig_kernel(
@@ -50,6 +54,8 @@ def tile_list_ckg_sig_kernel(
     wrr_words, wrr_scales, wri_words, wri_scales, nr_words, nr_scales, ni_words, ni_scales, offs, offs2, out,
 ):
     nc = tc.nc
+    pool_sum_tiles = [i for i in range(TILES) if KINDS[i] == "C"]
+    pool_product_tiles = [i for i in range(TILES) if KINDS[i] == "B"]
     with ExitStack() as ctx:
         keep = ctx.enter_context(tc.tile_pool(name="keep", bufs=1))
         psum = ctx.enter_context(tc.psum_pool(name="psum", bufs=1))
@@ -67,7 +73,7 @@ def tile_list_ckg_sig_kernel(
             return next_of(name, depth, lambda label: keep.tile(shape, F32, name=label, align_bytes=64))
 
         def bank(name):
-            return next_of(name, BANKS, lambda label: psum.tile([P, CHUNK], F32, name=label))
+            return next_of(name, SCALAR_BANKS if name == "for_scalar" else VECTOR_BANKS, lambda label: psum.tile([P, CHUNK], F32, name=label))
 
         list_e = keep.tile([P, J // 16], U16, name="list_e")
         list_r = keep.tile([P, J // 16], U16, name="list_r")
@@ -78,78 +84,92 @@ def tile_list_ckg_sig_kernel(
         ident = keep.tile([P, P], F32, name="ident", align_bytes=64)
         warm = keep.tile([P, 2], F32, name="warm")
 
-        nc.gpsimd.memset(plane_r[:, : T // 8], 0)
-        nc.gpsimd.memset(warm[:, 0:1], 0.0)
-        nc.vector.memset(plane_r[:, T // 8 :], 0)
+        nc.vector.memset(warm[:, 0:1], 0.0)
         nc.scalar.activation(warm[:, 1:2], warm[:, 0:1], SIGMOID)
 
-        def row_loads(plane, scales, first_row):
+        def row_loads(plane, scales, first_row, first_column=0):
             rows = scales[0].bitcast(I32)
-            return [(plane[first_row + s : P : 32, :], rows[s:16:4, :]) for s in range(4)]
+            columns = slice(first_column // 4, first_column // 4 + rows.shape[1])
+            return [(plane[first_row + s : P : 32, columns], rows[s:16:4, :]) for s in range(4)]
 
         def flat_words(words):
             return words[0].rearrange("p c i -> p (c i)")
 
-        def zeroed_plane(name, columns):
+        def zeroed_plane(name, columns, engine=nc.vector):
             plane = keep.tile([P, columns // 4], I32, name=name + "_plane", align_bytes=64)
-            nc.vector.memset(plane[:], 0)
+            engine.memset(plane[:], 0)
             return plane
 
-        def weight(name, words, scales, plane, first_row):
+        def weight(name, words, scales, plane, first_row, first_column=0):
             codes = keep.tile([P, words.shape[1]], U8, name=name, align_bytes=64)
             return {
                 "codes": codes[:], "plane": plane[:].bitcast(U8),
-                "load": (codes[:].bitcast(I32), words.bitcast(I32)), "rows": row_loads(plane, scales, first_row),
+                "load": (codes[:].bitcast(I32), words.bitcast(I32)), "rows": row_loads(plane, scales, first_row, first_column),
             }
 
-        relation_plane = zeroed_plane("relation", R)
+        nc.vector.memset(plane_r[:], 0)
+        relation_plane = zeroed_plane("relation", R, nc.gpsimd)
         wrr = weight("wrr", flat_words(wrr_words), wrr_scales, relation_plane, WRR_ROW)
         wri = weight("wri", flat_words(wri_words), wri_scales, relation_plane, WRI_ROW)
         nc.vector.memset(plane_e[:], 0)
-        wer = weight("wer", wer_words[0], wer_scales, zeroed_plane("wer", R), 0)
-        wei = weight("wei", wei_words[0], wei_scales, zeroed_plane("wei", R), 0)
+        entity_plane = zeroed_plane("entity", 2 * R)
+        wer = weight("wer", wer_words[0], wer_scales, entity_plane, 0)
+        wei = weight("wei", wei_words[0], wei_scales, entity_plane, 0, R)
         nr = weight("nr", nr_words[0], nr_scales, zeroed_plane("nr", N), 0)
         ni = weight("ni", ni_words[0], ni_scales, zeroed_plane("ni", N), 0)
-        make_identity(nc, ident[:])
 
-        loads = [(list_r[:], offs2), wer["load"], wei["load"]] + row_loads(plane_r, tab2_scales, 0)
-        loads += [(list_e[:], offs)] + row_loads(plane_e, tab_scales, 0) + [wrr["load"], wri["load"]]
-        loads += wrr["rows"] + wri["rows"] + wer["rows"][:WER_ROWS_AHEAD]
-        loads += [(words_r[:], flat_words(tab2_words).bitcast(I32))] + wer["rows"][WER_ROWS_AHEAD:] + wei["rows"]
-        loads += [(words_e[:], flat_words(tab_words).bitcast(I32))]
-        loads += [nr["load"], ni["load"]] + nr["rows"] + ni["rows"]
-        for dst, src in loads:
-            nc.sync.dma_start(out=dst, in_=src)
+        named = {
+            "list_r": [(list_r[:], offs2)], "rows_r": row_loads(plane_r, tab2_scales, 0),
+            "list_e": [(list_e[:], offs)], "rows_e": row_loads(plane_e, tab_scales, 0),
+            "words_r": [(words_r[:], flat_words(tab2_words).bitcast(I32))],
+            "words_e": [(words_e[:], flat_words(tab_words).bitcast(I32))],
+        }
+        for name, w in (("wrr", wrr), ("wri", wri), ("wer", wer), ("wei", wei), ("nr", nr), ("ni", ni)):
+            named[name] = [w["load"]]
+            named[name + "_rows"] = w["rows"]
+            named[name + "_a"] = w["rows"][:2]
+            named[name + "_b"] = w["rows"][2:]
+            named[name + "_1"] = w["rows"][:1]
+            named[name + "_234"] = w["rows"][1:]
+            named[name + "_123"] = w["rows"][:3]
+            named[name + "_4"] = w["rows"][3:]
+        for name in POOL_LOADS:
+            for dst, src in named[name]:
+                nc.gpsimd.dma_start(out=dst, in_=src)
+        for name in SYNC_LOADS:
+            for dst, src in named[name]:
+                nc.sync.dma_start(out=dst, in_=src)
 
-        def reorder(name, source, dtype, size, engine):
+        def reorder(name, source, dtype, size, engine, count=1):
             run = LINE // size
-            ordered = keep.tile([P, PACK, R // PACK], dtype, name=name, align_bytes=64)
+            ordered = keep.tile([P, count, PACK, R // PACK], dtype, name=name, align_bytes=64)
             engine.tensor_copy(
-                ordered[:].rearrange("p t (c i) -> p c t i", i=run),
-                source.bitcast(dtype).rearrange("p (c i t) -> p c t i", i=run, t=PACK),
+                ordered[:].rearrange("p w t (c i) -> p w c t i", i=run),
+                source.bitcast(dtype).rearrange("p (w c i t) -> p w c t i", w=count, i=run, t=PACK),
             )
-            return ordered[:].rearrange("p t m -> p (t m)")
+            return ordered[:].rearrange("p w t m -> p (w t m)")
 
         relation_slots = reorder("relation_slots", wrr["plane"], U8, 1, nc.gpsimd)
         slots_wrr = (reorder("wrr_slots", wrr["codes"], I32, 4, nc.gpsimd), relation_slots[WRR_ROW:P, :])
         slots_wri = (reorder("wri_slots", wri["codes"], I32, 4, nc.gpsimd), relation_slots[WRI_ROW:P, :])
-        slots_wer = (
-            reorder("wer_slots", wer["codes"], U16, 2, nc.vector), reorder("wer_scales", wer["plane"], U8, 1, nc.gpsimd),
-        )
-        slots_wei = (
-            reorder("wei_slots", wei["codes"], U16, 2, nc.vector), reorder("wei_scales", wei["plane"], U8, 1, nc.gpsimd),
-        )
+        entity_slots = reorder("entity_slots", wer["plane"], U8, 1, nc.gpsimd, 2)
+        slots_wer = (reorder("wer_slots", wer["codes"], U16, 2, nc.vector), entity_slots[:, :R])
+        slots_wei = (reorder("wei_slots", wei["codes"], U16, 2, nc.vector), entity_slots[:, R:])
+
+        make_identity(nc, ident[:])
 
         sources = {
             "scales_r": (plane_r, list_r, U8), "codes_r": (words_r, list_r, U32),
             "scales_e": (plane_e, list_e, U8), "codes_e": (words_e, list_e, U32),
         }
         picked = {}
+        whole = {}
 
         def gather(name, chunk, count, into=None):
             window, offsets, dtype = sources[name]
             if into is None:
                 into = keep.tile([P, count * CHUNK], dtype, name="%s_%d" % (name, chunk), align_bytes=64)[:]
+                whole[name, chunk] = into
             columns = slice(chunk * CHUNK // 16, (chunk + count) * CHUNK // 16)
             nc.vector.tensor_copy(into, window[:].bitcast(dtype).indirect(offsets[:, columns]))
             for n in range(count):
@@ -161,7 +181,7 @@ def tile_list_ckg_sig_kernel(
             codes = picked["codes_" + side, chunk][:, tokens].bitcast(FP8X4)
             scales = picked["scales_" + side, chunk][:, tokens]
             acc = bank(ring)
-            if i in POOL_SUM_TILES:
+            if i in pool_sum_tiles:
                 by_slot = acc[:].rearrange("p (t n) -> p t n", t=PACK)
                 for t in range(PACK):
                     nc.tensor.matmul_mx(
@@ -177,37 +197,42 @@ def tile_list_ckg_sig_kernel(
             return acc[:]
 
         def relation(i):
-            rel = ring_tile("rel", [P, 2, R], RELATION_AHEAD + 1)
+            rel = ring_tile("rel", [P, 2, R], RELATION_DEPTH)
             for part, slots in enumerate((slots_wrr, slots_wri)):
                 target = rel[:, part]
-                if i in POOL_SUM_TILES:
+                if i in pool_sum_tiles:
                     target = target.rearrange("p (n t) -> p n t", t=PACK)
                 nc.scalar.copy(target, project("for_scalar", "r", i, slots, FP8X4))
             return rel
 
         def entity(i):
-            return project("entity", "e", i, slots_wer, FP4X4), project("entity", "e", i, slots_wei, FP4X4)
+            aer = None if i in pool_product_tiles else project("entity", "e", i, slots_wer, FP4X4)
+            return aer, project("entity", "e", i, slots_wei, FP4X4)
 
-        def products(i, rel, aer, aei):
-            prod = ring_tile("prod", [P, 4, R], PRODUCT_DEPTH)
-            if i in POOL_SUM_TILES:
-                for pair, acc in enumerate((aer, aei)):
+        def pool_products(i, rel):
+            aer_copy = ring_tile("aer_copy", [P, R], AER_DEPTH)
+            nc.scalar.copy(aer_copy[:], project("for_scalar", "e", i, slots_wer, FP4X4))
+            real = ring_tile("real", [P, 2, R], PRODUCT_DEPTH)
+            nc.gpsimd.tensor_tensor(real[:], aer_copy[:].unsqueeze(1).broadcast_to([P, 2, R]), rel[:], MULT)
+            return real
+
+        def products(i, rel, aer, aei, real):
+            if real is None:
+                real = ring_tile("real", [P, 2, R], PRODUCT_DEPTH)
+            imag = ring_tile("imag", [P, 2, R], PRODUCT_DEPTH)
+            if i in pool_sum_tiles:
+                for prod, acc in ((real, aer), (imag, aei)):
                     nc.vector.tensor_tensor(
-                        prod[:, 2 * pair : 2 * pair + 2].rearrange("p h (n t) -> p h n t", t=PACK),
+                        prod[:].rearrange("p h (n t) -> p h n t", t=PACK),
                         acc.unsqueeze(1).broadcast_to([P, 2, TILE, PACK]),
                         rel[:].rearrange("p h (n t) -> p h n t", t=PACK), MULT,
                     )
-                return prod
-            if i in POOL_PRODUCT_TILES:
-                aer_copy = ring_tile("aer_copy", [P, R], AER_DEPTH)
-                nc.scalar.copy(aer_copy[:], aer)
-                nc.gpsimd.tensor_tensor(prod[:, 0], aer_copy[:], rel[:, 0], MULT)
-                nc.gpsimd.tensor_tensor(prod[:, 1], aer_copy[:], rel[:, 1], MULT)
-            else:
-                nc.vector.tensor_tensor(prod[:, 0:2], aer.unsqueeze(1).broadcast_to([P, 2, R]), rel[:], MULT)
-            nc.vector.scalar_tensor_tensor(prod[:, 2], aei, -1.0, rel[:, 1], MULT, MULT)
-            nc.vector.tensor_tensor(prod[:, 3], aei, rel[:, 0], MULT)
-            return prod
+                return real, imag
+            if aer is not None:
+                nc.vector.tensor_tensor(real[:], aer.unsqueeze(1).broadcast_to([P, 2, R]), rel[:], MULT)
+            nc.vector.scalar_tensor_tensor(imag[:, 0], aei, -1.0, rel[:, 1], MULT, MULT)
+            nc.vector.tensor_tensor(imag[:, 1], aei, rel[:, 0], MULT)
+            return real, imag
 
         h_rounded = {}
 
@@ -219,15 +244,15 @@ def tile_list_ckg_sig_kernel(
 
         def add_terms(i, prod):
             flat = rounded(i).rearrange("p h n t -> p h (n t)")
-            nc.gpsimd.tensor_tensor(flat[:, 0], prod[:, 0], prod[:, 3], SUBTRACT)
-            nc.gpsimd.tensor_tensor(flat[:, 1], prod[:, 1], prod[:, 2], ADD)
+            nc.gpsimd.tensor_tensor(flat[:, 0], prod[0][:, 0], prod[1][:, 1], SUBTRACT)
+            nc.gpsimd.tensor_tensor(flat[:, 1], prod[0][:, 1], prod[1][:, 0], ADD)
 
         def turn(i, prod, part):
             acc = bank("for_scalar")[:].rearrange("p (t n) -> p t n", t=PACK)
             for term in range(2):
                 for t in range(PACK):
                     nc.tensor.matmul(
-                        acc[:, t, :], lhsT=prod[:, part + 2 * term, t * P : (t + 1) * P], rhs=ident[:],
+                        acc[:, t, :], lhsT=prod[1 - term][:, part, t * P : (t + 1) * P], rhs=ident[:],
                         start=(term == 0 and t == 0), stop=(term == 1 and t == PACK - 1), is_transpose=True,
                     )
             nc.scalar.copy(rounded(i)[:, part], acc.rearrange("p t n -> p n t"))
@@ -268,34 +293,34 @@ def tile_list_ckg_sig_kernel(
                 rows = out[P * n * per_bank : P * (n + 1) * per_bank, first * TILE : first * TILE + width]
                 nc.sync.dma_start(out=rows.rearrange("(h p) n -> p h n", p=P), in_=result[:])
 
-        gather("scales_r", 0, CHUNKS)
-        gather("codes_r", 0, 1)
-        gather("codes_r", 1, 1)
-        gather("codes_r", 2, 2)
+        for name, chunk, count in HEAD_GATHERS:
+            gather(name, chunk, count)
         rels = {i: relation(i) for i in range(RELATION_AHEAD)}
-        gather("scales_e", 0, CHUNKS)
-        gather("codes_e", 0, 1)
-        gather("codes_e", 1, 1)
+        next_relation = RELATION_AHEAD
+        reals = {i: pool_products(i, rels[i]) for i in range(POOL_AHEAD + 1) if i in pool_product_tiles}
         ents = {0: entity(0)}
         prods = {}
         for step in range(QUANTISE_STEPS[-1] + 2):
-            turns = 1 <= step <= TILES and step - 1 not in POOL_SUM_TILES
+            turns = 1 <= step <= TILES and step - 1 not in pool_sum_tiles
             if turns:
                 turn(step - 1, prods[step - 1], 0)
             if step + 1 < TILES:
                 ents[step + 1] = entity(step + 1)
-            if step + RELATION_AHEAD < TILES:
-                rels[step + RELATION_AHEAD] = relation(step + RELATION_AHEAD)
+            for n in range(RELATION_PACE[step] if step < len(RELATION_PACE) else 0):
+                rels[next_relation] = relation(next_relation)
+                next_relation = next_relation + 1
+            if step + 1 + POOL_AHEAD in pool_product_tiles:
+                reals[step + 1 + POOL_AHEAD] = pool_products(step + 1 + POOL_AHEAD, rels[step + 1 + POOL_AHEAD])
             if step - 1 in QUANTISE_STEPS:
                 score(*SCORE_GROUPS[QUANTISE_STEPS.index(step - 1)])
             if turns:
                 turn(step - 1, prods[step - 1], 1)
             if step < TILES:
-                prods[step] = products(step, rels[step], *ents[step])
-            if step in POOL_SUM_TILES:
+                prods[step] = products(step, rels[step], ents[step][0], ents[step][1], reals.get(step))
+            if step in pool_sum_tiles:
                 add_terms(step, prods[step])
-            if step in LATE_GATHER_STEPS:
-                chunk = LATE_GATHER_STEPS[step]
-                gather("codes_e", chunk, 1, into=picked["codes_e", chunk - 2])
+            if step in LATE_GATHERS:
+                name, chunk, count, old_name, old_chunk = LATE_GATHERS[step]
+                gather(name, chunk, count, into=whole[old_name, old_chunk])
             if step in QUANTISE_STEPS:
                 quantise(*SCORE_GROUPS[QUANTISE_STEPS.index(step)])

@@ -28,12 +28,16 @@ CHUNKS = J // CHUNK
 TILES = J // TILE
 TILES_PER_CHUNK = CHUNK // TILE
 
-KINDS = "BCBBCABCBBCABCBA"
+KINDS = "BCBBCABCBBCABCAW"
 RELATION_AHEAD = 5
 POOL_AHEAD = 2
+SCORE_FIRST = True
+SCORE_STEPS = (7, 11, 16, 17, 18, 19)
+TURN_FIRST = False
+SPREAD = False
 POOL_LOADS = ()
 SYNC_LOADS = ("list_r", "wer", "wei", "rows_r", "list_e", "wrr", "wri", "rows_e", "wrr_123", "words_r", "wrr_4", "wri_rows", "wei_1", "words_e", "wei_234", "wer_rows", "nr", "ni", "nr_rows", "ni_rows")
-RELATION_PACE = (0, 2, 1, 1, 1, 1, 1, 1, 1, 1, 1)
+RELATION_PACE = (0, 0, 2, 1, 1, 1, 1, 1, 1, 1, 1, 1)
 RELATION_DEPTH = 6
 PRODUCT_DEPTH = 6
 AER_DEPTH = 3
@@ -54,8 +58,8 @@ def tile_list_ckg_sig_kernel(
     wrr_words, wrr_scales, wri_words, wri_scales, nr_words, nr_scales, ni_words, ni_scales, offs, offs2, out,
 ):
     nc = tc.nc
-    pool_sum_tiles = [i for i in range(TILES) if KINDS[i] == "C"]
-    pool_product_tiles = [i for i in range(TILES) if KINDS[i] == "B"]
+    pool_sum_tiles = [i for i in range(TILES) if KINDS[i] in "CVWE"]
+    pool_product_tiles = [i for i in range(TILES) if KINDS[i] in "BWE"]
     with ExitStack() as ctx:
         keep = ctx.enter_context(tc.tile_pool(name="keep", bufs=1))
         psum = ctx.enter_context(tc.psum_pool(name="psum", bufs=1))
@@ -113,6 +117,8 @@ def tile_list_ckg_sig_kernel(
         wri = weight("wri", flat_words(wri_words), wri_scales, relation_plane, WRI_ROW)
         nc.vector.memset(plane_e[:], 0)
         entity_plane = zeroed_plane("entity", 2 * R)
+        if SPREAD:
+            moved_r = zeroed_plane("moved_r", J)
         wer = weight("wer", wer_words[0], wer_scales, entity_plane, 0)
         wei = weight("wei", wei_words[0], wei_scales, entity_plane, 0, R)
         nr = weight("nr", nr_words[0], nr_scales, zeroed_plane("nr", N), 0)
@@ -136,7 +142,9 @@ def tile_list_ckg_sig_kernel(
         for name in POOL_LOADS:
             for dst, src in named[name]:
                 nc.gpsimd.dma_start(out=dst, in_=src)
-        for name in SYNC_LOADS:
+        named["spread_r"] = [(plane_r[0:P:8, :], tab2_scales[0].bitcast(I32))]
+        split = SYNC_LOADS.index("moves_r") if SPREAD else len(SYNC_LOADS)
+        for name in SYNC_LOADS[:split]:
             for dst, src in named[name]:
                 nc.sync.dma_start(out=dst, in_=src)
 
@@ -211,7 +219,10 @@ def tile_list_ckg_sig_kernel(
 
         def pool_products(i, rel):
             aer_copy = ring_tile("aer_copy", [P, R], AER_DEPTH)
-            nc.scalar.copy(aer_copy[:], project("for_scalar", "e", i, slots_wer, FP4X4))
+            target = aer_copy[:]
+            if i in pool_sum_tiles:
+                target = target.rearrange("p (n t) -> p n t", t=PACK)
+            nc.scalar.copy(target, project("for_scalar", "e", i, slots_wer, FP4X4))
             real = ring_tile("real", [P, 2, R], PRODUCT_DEPTH)
             nc.gpsimd.tensor_tensor(real[:], aer_copy[:].unsqueeze(1).broadcast_to([P, 2, R]), rel[:], MULT)
             return real
@@ -222,6 +233,8 @@ def tile_list_ckg_sig_kernel(
             imag = ring_tile("imag", [P, 2, R], PRODUCT_DEPTH)
             if i in pool_sum_tiles:
                 for prod, acc in ((real, aer), (imag, aei)):
+                    if acc is None:
+                        continue
                     nc.vector.tensor_tensor(
                         prod[:].rearrange("p h (n t) -> p h n t", t=PACK),
                         acc.unsqueeze(1).broadcast_to([P, 2, TILE, PACK]),
@@ -244,8 +257,9 @@ def tile_list_ckg_sig_kernel(
 
         def add_terms(i, prod):
             flat = rounded(i).rearrange("p h n t -> p h (n t)")
-            nc.gpsimd.tensor_tensor(flat[:, 0], prod[0][:, 0], prod[1][:, 1], SUBTRACT)
-            nc.gpsimd.tensor_tensor(flat[:, 1], prod[0][:, 1], prod[1][:, 0], ADD)
+            engine = nc.vector if KINDS[i] in "VW" else nc.gpsimd
+            engine.tensor_tensor(flat[:, 0], prod[0][:, 0], prod[1][:, 1], SUBTRACT)
+            engine.tensor_tensor(flat[:, 1], prod[0][:, 1], prod[1][:, 0], ADD)
 
         def turn(i, prod, part):
             acc = bank("for_scalar")[:].rearrange("p (t n) -> p t n", t=PACK)
@@ -295,14 +309,22 @@ def tile_list_ckg_sig_kernel(
 
         for name, chunk, count in HEAD_GATHERS:
             gather(name, chunk, count)
+            if SPREAD and name == "scales_r":
+                for s in range(4):
+                    nc.sync.dma_start(out=moved_r[s:P:32, :], in_=whole["scales_r", 0].bitcast(I32)[8 * s : P : 32, :])
+                for n in range(CHUNKS):
+                    picked["scales_r", n] = moved_r[:].bitcast(U8)[:, n * CHUNK : (n + 1) * CHUNK]
+                for later in SYNC_LOADS[split + 1 :]:
+                    for dst, src in named[later]:
+                        nc.sync.dma_start(out=dst, in_=src)
         rels = {i: relation(i) for i in range(RELATION_AHEAD)}
         next_relation = RELATION_AHEAD
         reals = {i: pool_products(i, rels[i]) for i in range(POOL_AHEAD + 1) if i in pool_product_tiles}
         ents = {0: entity(0)}
         prods = {}
-        for step in range(QUANTISE_STEPS[-1] + 2):
+        for step in range(SCORE_STEPS[-1] + 1):
             turns = 1 <= step <= TILES and step - 1 not in pool_sum_tiles
-            if turns:
+            if turns and TURN_FIRST:
                 turn(step - 1, prods[step - 1], 0)
             if step + 1 < TILES:
                 ents[step + 1] = entity(step + 1)
@@ -311,10 +333,14 @@ def tile_list_ckg_sig_kernel(
                 next_relation = next_relation + 1
             if step + 1 + POOL_AHEAD in pool_product_tiles:
                 reals[step + 1 + POOL_AHEAD] = pool_products(step + 1 + POOL_AHEAD, rels[step + 1 + POOL_AHEAD])
-            if step - 1 in QUANTISE_STEPS:
-                score(*SCORE_GROUPS[QUANTISE_STEPS.index(step - 1)])
+            if step in SCORE_STEPS and SCORE_FIRST:
+                score(*SCORE_GROUPS[SCORE_STEPS.index(step)])
+            if turns and not TURN_FIRST:
+                turn(step - 1, prods[step - 1], 0)
             if turns:
                 turn(step - 1, prods[step - 1], 1)
+            if step in SCORE_STEPS and not SCORE_FIRST:
+                score(*SCORE_GROUPS[SCORE_STEPS.index(step)])
             if step < TILES:
                 prods[step] = products(step, rels[step], ents[step][0], ents[step][1], reals.get(step))
             if step in pool_sum_tiles:

@@ -16,41 +16,42 @@ FP8X4 = mybir.dt.float8_e4m3fn_x4
 FP4X4 = mybir.dt.float4_e2m1fn_x4
 MULT = mybir.AluOpType.mult
 ADD = mybir.AluOpType.add
-SUBTRACT = mybir.AluOpType.subtract
 SIGMOID = mybir.ActivationFunctionType.Sigmoid
 
 P = 128
 PACK = 4
 LINE = 16
+QUADRANT = 32
+SCALE_ROWS = 16
 CHUNK = 512
 TILE = 128
 CHUNKS = J // CHUNK
 TILES = J // TILE
 TILES_PER_CHUNK = CHUNK // TILE
 
-KINDS = "BCBBCABCBBCABCAW"
-RELATION_AHEAD = 5
-POOL_AHEAD = 2
-SCORE_FIRST = True
-SCORE_STEPS = (7, 11, 16, 17, 18, 19)
-TURN_FIRST = False
-SPREAD = False
-POOL_LOADS = ()
-SYNC_LOADS = ("list_r", "wer", "wei", "rows_r", "list_e", "wrr", "wri", "rows_e", "wrr_123", "words_r", "wrr_4", "wri_rows", "wei_1", "words_e", "wei_234", "wer_rows", "nr", "ni", "nr_rows", "ni_rows")
-RELATION_PACE = (0, 0, 2, 1, 1, 1, 1, 1, 1, 1, 1, 1)
-RELATION_DEPTH = 6
-PRODUCT_DEPTH = 6
+LAST = TILES - 1
+CHANNEL_TILES = tuple(range(1, LAST, 3)) + (LAST,)
+PLAIN_TILES = tuple(range(5, LAST, 6)) + (LAST - 1,)
+HELPED_TILES = tuple(i for i in range(LAST) if i not in CHANNEL_TILES + PLAIN_TILES) + (LAST,)
+
+RELATION_HEAD = 5
+RELATION_RESUMES = 2
+RELATION_AHEAD = RELATION_HEAD - 1
+RELATION_DEPTH = RELATION_AHEAD + 2
+HELP_AHEAD = 3
 AER_DEPTH = 3
-SCALAR_BANKS = 4
-VECTOR_BANKS = 4
+PRODUCT_DEPTH = 6
+BANKS = 4
 
 SCORE_GROUPS = ((0, 4), (4, 4), (8, 4), (12, 2), (14, 1), (15, 1))
-QUANTISE_STEPS = (6, 10, 13, 16, 17, 18)
-LATE_GATHERS = {2: ("scales_e", 2, 1, "scales_e", 0), 3: ("codes_e", 2, 1, "codes_e", 0), 6: ("scales_e", 3, 1, "scales_e", 1), 7: ("codes_e", 3, 1, "codes_e", 1)}
-HEAD_GATHERS = (("scales_r", 0, 4), ("scales_e", 0, 1), ("scales_e", 1, 1), ("codes_r", 0, 1), ("codes_r", 1, 1), ("codes_r", 2, 2), ("codes_e", 0, 1), ("codes_e", 1, 1))
+QUANTISE_STEPS = (7, 11, LAST - 1, TILES, TILES + 1, TILES + 2)
+SCORE_STEPS = (8, 12, TILES, TILES + 1, TILES + 2, TILES + 3)
+LATE_GATHERS = {2: ("scales_e", 2), 3: ("codes_e", 2), 6: ("scales_e", 3), 7: ("codes_e", 3)}
 
 WRR_ROW = 4
 WRI_ROW = 8
+WRI_ROWS_AHEAD = 3
+WEI_ROWS_AHEAD = 1
 
 
 def tile_list_ckg_sig_kernel(
@@ -58,8 +59,6 @@ def tile_list_ckg_sig_kernel(
     wrr_words, wrr_scales, wri_words, wri_scales, nr_words, nr_scales, ni_words, ni_scales, offs, offs2, out,
 ):
     nc = tc.nc
-    pool_sum_tiles = [i for i in range(TILES) if KINDS[i] in "CVWE"]
-    pool_product_tiles = [i for i in range(TILES) if KINDS[i] in "BWE"]
     with ExitStack() as ctx:
         keep = ctx.enter_context(tc.tile_pool(name="keep", bufs=1))
         psum = ctx.enter_context(tc.psum_pool(name="psum", bufs=1))
@@ -77,76 +76,61 @@ def tile_list_ckg_sig_kernel(
             return next_of(name, depth, lambda label: keep.tile(shape, F32, name=label, align_bytes=64))
 
         def bank(name):
-            return next_of(name, SCALAR_BANKS if name == "for_scalar" else VECTOR_BANKS, lambda label: psum.tile([P, CHUNK], F32, name=label))
+            return next_of(name, BANKS, lambda label: psum.tile([P, CHUNK], F32, name=label))
 
         list_e = keep.tile([P, J // 16], U16, name="list_e")
         list_r = keep.tile([P, J // 16], U16, name="list_r")
         words_e = keep.tile([P, T], I32, name="words_e", align_bytes=64)
         words_r = keep.tile([P, T], I32, name="words_r", align_bytes=64)
         plane_e = keep.tile([P, T // 4], I32, name="plane_e", align_bytes=64)
-        plane_r = keep.tile([P, T // 4], I32, name="plane_r", align_bytes=64)
+        spread_r = keep.tile([P, T // 4], I32, name="plane_r", align_bytes=64)
         ident = keep.tile([P, P], F32, name="ident", align_bytes=64)
-        warm = keep.tile([P, 2], F32, name="warm")
-
-        nc.vector.memset(warm[:, 0:1], 0.0)
-        nc.scalar.activation(warm[:, 1:2], warm[:, 0:1], SIGMOID)
 
         def row_loads(plane, scales, first_row, first_column=0):
             rows = scales[0].bitcast(I32)
             columns = slice(first_column // 4, first_column // 4 + rows.shape[1])
-            return [(plane[first_row + s : P : 32, columns], rows[s:16:4, :]) for s in range(4)]
+            return [(plane[first_row + s : P : QUADRANT, columns], rows[s:SCALE_ROWS:4, :]) for s in range(4)]
 
         def flat_words(words):
             return words[0].rearrange("p c i -> p (c i)")
-
-        def zeroed_plane(name, columns, engine=nc.vector):
-            plane = keep.tile([P, columns // 4], I32, name=name + "_plane", align_bytes=64)
-            engine.memset(plane[:], 0)
-            return plane
 
         def weight(name, words, scales, plane, first_row, first_column=0):
             codes = keep.tile([P, words.shape[1]], U8, name=name, align_bytes=64)
             return {
                 "codes": codes[:], "plane": plane[:].bitcast(U8),
-                "load": (codes[:].bitcast(I32), words.bitcast(I32)), "rows": row_loads(plane, scales, first_row, first_column),
+                "load": (codes[:].bitcast(I32), words.bitcast(I32)),
+                "rows": row_loads(plane, scales, first_row, first_column),
             }
 
-        nc.vector.memset(plane_r[:], 0)
-        relation_plane = zeroed_plane("relation", R, nc.gpsimd)
+        nc.vector.memset(spread_r[:], 0)
+        relation_plane = keep.tile([P, R // 4], I32, name="relation_plane", align_bytes=64)
+        nc.vector.memset(relation_plane[:], 0)
         wrr = weight("wrr", flat_words(wrr_words), wrr_scales, relation_plane, WRR_ROW)
         wri = weight("wri", flat_words(wri_words), wri_scales, relation_plane, WRI_ROW)
         nc.vector.memset(plane_e[:], 0)
-        entity_plane = zeroed_plane("entity", 2 * R)
-        if SPREAD:
-            moved_r = zeroed_plane("moved_r", J)
+        gathered_plane_r = wrr["codes"].bitcast(I32)
+        late_planes = wri["codes"].bitcast(I32)[:, : (2 * R + 2 * N) // 4]
+        entity_plane = late_planes[:, : 2 * R // 4]
         wer = weight("wer", wer_words[0], wer_scales, entity_plane, 0)
         wei = weight("wei", wei_words[0], wei_scales, entity_plane, 0, R)
-        nr = weight("nr", nr_words[0], nr_scales, zeroed_plane("nr", N), 0)
-        ni = weight("ni", ni_words[0], ni_scales, zeroed_plane("ni", N), 0)
+        nr = weight("nr", nr_words[0], nr_scales, late_planes[:, 2 * R // 4 : (2 * R + N) // 4], 0)
+        ni = weight("ni", ni_words[0], ni_scales, late_planes[:, (2 * R + N) // 4 :], 0)
 
-        named = {
-            "list_r": [(list_r[:], offs2)], "rows_r": row_loads(plane_r, tab2_scales, 0),
-            "list_e": [(list_e[:], offs)], "rows_e": row_loads(plane_e, tab_scales, 0),
-            "words_r": [(words_r[:], flat_words(tab2_words).bitcast(I32))],
-            "words_e": [(words_e[:], flat_words(tab_words).bitcast(I32))],
+        sources = {
+            "scales_r": (spread_r, list_r, U8), "codes_r": (words_r, list_r, U32),
+            "scales_e": (plane_e, list_e, U8), "codes_e": (words_e, list_e, U32),
         }
-        for name, w in (("wrr", wrr), ("wri", wri), ("wer", wer), ("wei", wei), ("nr", nr), ("ni", ni)):
-            named[name] = [w["load"]]
-            named[name + "_rows"] = w["rows"]
-            named[name + "_a"] = w["rows"][:2]
-            named[name + "_b"] = w["rows"][2:]
-            named[name + "_1"] = w["rows"][:1]
-            named[name + "_234"] = w["rows"][1:]
-            named[name + "_123"] = w["rows"][:3]
-            named[name + "_4"] = w["rows"][3:]
-        for name in POOL_LOADS:
-            for dst, src in named[name]:
-                nc.gpsimd.dma_start(out=dst, in_=src)
-        named["spread_r"] = [(plane_r[0:P:8, :], tab2_scales[0].bitcast(I32))]
-        split = SYNC_LOADS.index("moves_r") if SPREAD else len(SYNC_LOADS)
-        for name in SYNC_LOADS[:split]:
-            for dst, src in named[name]:
-                nc.sync.dma_start(out=dst, in_=src)
+        picked = {}
+
+        def gather(name, chunk, count, into=None):
+            window, offsets, dtype = sources[name]
+            if into is None:
+                into = keep.tile([P, count * CHUNK], dtype, name="%s_%d" % (name, chunk), align_bytes=64)[:]
+            columns = slice(chunk * CHUNK // 16, (chunk + count) * CHUNK // 16)
+            nc.vector.tensor_copy(into, window[:].bitcast(dtype).indirect(offsets[:, columns]))
+            for n in range(count):
+                picked[name, chunk + n] = into[:, n * CHUNK : (n + 1) * CHUNK]
+            return into
 
         def reorder(name, source, dtype, size, engine, count=1):
             run = LINE // size
@@ -157,31 +141,35 @@ def tile_list_ckg_sig_kernel(
             )
             return ordered[:].rearrange("p w t m -> p (w t m)")
 
-        relation_slots = reorder("relation_slots", wrr["plane"], U8, 1, nc.gpsimd)
-        slots_wrr = (reorder("wrr_slots", wrr["codes"], I32, 4, nc.gpsimd), relation_slots[WRR_ROW:P, :])
-        slots_wri = (reorder("wri_slots", wri["codes"], I32, 4, nc.gpsimd), relation_slots[WRI_ROW:P, :])
-        entity_slots = reorder("entity_slots", wer["plane"], U8, 1, nc.gpsimd, 2)
-        slots_wer = (reorder("wer_slots", wer["codes"], U16, 2, nc.vector), entity_slots[:, :R])
-        slots_wei = (reorder("wei_slots", wei["codes"], U16, 2, nc.vector), entity_slots[:, R:])
+        def load(pairs, queue=nc.sync):
+            for dst, src in pairs:
+                queue.dma_start(out=dst, in_=src)
 
+        load(wrr["rows"], nc.gpsimd)
+        step_r = P // SCALE_ROWS
+        load([(list_r[:], offs2), wer["load"], wei["load"], (spread_r[0:P:step_r, :], tab2_scales[0].bitcast(I32))])
+        load([(list_e[:], offs), wrr["load"], wri["load"]])
+        wrr_ordered = reorder("wrr_slots", wrr["codes"], I32, 4, nc.gpsimd)
+        wri_ordered = reorder("wri_slots", wri["codes"], I32, 4, nc.gpsimd)
+        nc.gpsimd.memset(late_planes, 0)
+        nc.gpsimd.memset(gathered_plane_r, 0)
+        load(row_loads(plane_e, tab_scales, 0) + wri["rows"][:WRI_ROWS_AHEAD])
+        load([(words_r[:], flat_words(tab2_words).bitcast(I32))] + wri["rows"][WRI_ROWS_AHEAD:])
+        load(wei["rows"][:WEI_ROWS_AHEAD])
+        spread_picked = gather("scales_r", 0, CHUNKS).bitcast(I32)
+        load([(gathered_plane_r[s:P:QUADRANT, :], spread_picked[step_r * s : P : QUADRANT, :]) for s in range(4)])
+        for chunk in range(CHUNKS):
+            picked["scales_r", chunk] = gathered_plane_r.bitcast(U8)[:, chunk * CHUNK : (chunk + 1) * CHUNK]
+        load([(words_e[:], flat_words(tab_words).bitcast(I32))] + wei["rows"][WEI_ROWS_AHEAD:] + wer["rows"])
+        load([nr["load"], ni["load"]] + nr["rows"] + ni["rows"])
+
+        relation_scales = reorder("relation_slots", wrr["plane"], U8, 1, nc.gpsimd)
+        slots_wrr = (wrr_ordered, relation_scales[WRR_ROW:P, :])
+        slots_wri = (wri_ordered, relation_scales[WRI_ROW:P, :])
+        entity_scales = reorder("entity_slots", wei["plane"], U8, 1, nc.gpsimd, 2)
+        slots_wer = (reorder("wer_slots", wer["codes"], U16, 2, nc.vector), entity_scales[:, :R])
+        slots_wei = (reorder("wei_slots", wei["codes"], U16, 2, nc.vector), entity_scales[:, R:])
         make_identity(nc, ident[:])
-
-        sources = {
-            "scales_r": (plane_r, list_r, U8), "codes_r": (words_r, list_r, U32),
-            "scales_e": (plane_e, list_e, U8), "codes_e": (words_e, list_e, U32),
-        }
-        picked = {}
-        whole = {}
-
-        def gather(name, chunk, count, into=None):
-            window, offsets, dtype = sources[name]
-            if into is None:
-                into = keep.tile([P, count * CHUNK], dtype, name="%s_%d" % (name, chunk), align_bytes=64)[:]
-                whole[name, chunk] = into
-            columns = slice(chunk * CHUNK // 16, (chunk + count) * CHUNK // 16)
-            nc.vector.tensor_copy(into, window[:].bitcast(dtype).indirect(offsets[:, columns]))
-            for n in range(count):
-                picked[name, chunk + n] = into[:, n * CHUNK : (n + 1) * CHUNK]
 
         def project(ring, side, i, slots, fmt):
             chunk, place = divmod(i, TILES_PER_CHUNK)
@@ -189,7 +177,7 @@ def tile_list_ckg_sig_kernel(
             codes = picked["codes_" + side, chunk][:, tokens].bitcast(FP8X4)
             scales = picked["scales_" + side, chunk][:, tokens]
             acc = bank(ring)
-            if i in pool_sum_tiles:
+            if i in CHANNEL_TILES:
                 by_slot = acc[:].rearrange("p (t n) -> p t n", t=PACK)
                 for t in range(PACK):
                     nc.tensor.matmul_mx(
@@ -204,48 +192,42 @@ def tile_list_ckg_sig_kernel(
             )
             return acc[:]
 
+        def like_sums(i, columns):
+            return columns.rearrange("p (n t) -> p n t", t=PACK) if i in CHANNEL_TILES else columns
+
         def relation(i):
             rel = ring_tile("rel", [P, 2, R], RELATION_DEPTH)
-            for part, slots in enumerate((slots_wrr, slots_wri)):
-                target = rel[:, part]
-                if i in pool_sum_tiles:
-                    target = target.rearrange("p (n t) -> p n t", t=PACK)
-                nc.scalar.copy(target, project("for_scalar", "r", i, slots, FP8X4))
+            sums = [project("for_scalar", "r", i, slots, FP8X4) for slots in (slots_wrr, slots_wri)]
+            for part in range(2):
+                nc.scalar.copy(like_sums(i, rel[:, part]), sums[part])
             return rel
 
         def entity(i):
-            aer = None if i in pool_product_tiles else project("entity", "e", i, slots_wer, FP4X4)
+            aer = None if i in HELPED_TILES else project("entity", "e", i, slots_wer, FP4X4)
             return aer, project("entity", "e", i, slots_wei, FP4X4)
 
-        def pool_products(i, rel):
+        def help_with(i, rel):
             aer_copy = ring_tile("aer_copy", [P, R], AER_DEPTH)
-            target = aer_copy[:]
-            if i in pool_sum_tiles:
-                target = target.rearrange("p (n t) -> p n t", t=PACK)
-            nc.scalar.copy(target, project("for_scalar", "e", i, slots_wer, FP4X4))
-            real = ring_tile("real", [P, 2, R], PRODUCT_DEPTH)
-            nc.gpsimd.tensor_tensor(real[:], aer_copy[:].unsqueeze(1).broadcast_to([P, 2, R]), rel[:], MULT)
-            return real
+            nc.scalar.copy(like_sums(i, aer_copy[:]), project("for_scalar", "e", i, slots_wer, FP4X4))
+            by_aer = ring_tile("real", [P, 2, R], PRODUCT_DEPTH)
+            nc.gpsimd.tensor_tensor(by_aer[:], aer_copy[:].unsqueeze(1).broadcast_to([P, 2, R]), rel[:], MULT)
+            return by_aer
 
-        def products(i, rel, aer, aei, real):
-            if real is None:
-                real = ring_tile("real", [P, 2, R], PRODUCT_DEPTH)
-            imag = ring_tile("imag", [P, 2, R], PRODUCT_DEPTH)
-            if i in pool_sum_tiles:
-                for prod, acc in ((real, aer), (imag, aei)):
-                    if acc is None:
-                        continue
-                    nc.vector.tensor_tensor(
-                        prod[:].rearrange("p h (n t) -> p h n t", t=PACK),
-                        acc.unsqueeze(1).broadcast_to([P, 2, TILE, PACK]),
-                        rel[:].rearrange("p h (n t) -> p h n t", t=PACK), MULT,
-                    )
-                return real, imag
-            if aer is not None:
-                nc.vector.tensor_tensor(real[:], aer.unsqueeze(1).broadcast_to([P, 2, R]), rel[:], MULT)
-            nc.vector.scalar_tensor_tensor(imag[:, 0], aei, -1.0, rel[:, 1], MULT, MULT)
-            nc.vector.tensor_tensor(imag[:, 1], aei, rel[:, 0], MULT)
-            return real, imag
+        def products(i, rel, aer, aei, by_aer):
+            if by_aer is None:
+                by_aer = ring_tile("real", [P, 2, R], PRODUCT_DEPTH)
+            by_aei = ring_tile("imag", [P, 2, R], PRODUCT_DEPTH)
+            nc.vector.scalar_tensor_tensor(like_sums(i, by_aei[:, 0]), aei, -1.0, like_sums(i, rel[:, 1]), MULT, MULT)
+            nc.vector.tensor_tensor(like_sums(i, by_aei[:, 1]), aei, like_sums(i, rel[:, 0]), MULT)
+            if i in PLAIN_TILES:
+                nc.vector.tensor_tensor(by_aer[:], aer.unsqueeze(1).broadcast_to([P, 2, R]), rel[:], MULT)
+            elif i not in HELPED_TILES:
+                nc.vector.tensor_tensor(
+                    by_aer[:].rearrange("p h (n t) -> p h n t", t=PACK),
+                    aer.unsqueeze(1).broadcast_to([P, 2, TILE, PACK]),
+                    rel[:].rearrange("p h (n t) -> p h n t", t=PACK), MULT,
+                )
+            return by_aer, by_aei
 
         h_rounded = {}
 
@@ -255,18 +237,16 @@ def tile_list_ckg_sig_kernel(
                 h_rounded[first] = keep.tile([P, 2, count * TILE, PACK], BF16, name="h_%d" % first, align_bytes=64)
             return h_rounded[first][:, :, (i - first) * TILE : (i - first + 1) * TILE, :]
 
-        def add_terms(i, prod):
-            flat = rounded(i).rearrange("p h n t -> p h (n t)")
-            engine = nc.vector if KINDS[i] in "VW" else nc.gpsimd
-            engine.tensor_tensor(flat[:, 0], prod[0][:, 0], prod[1][:, 1], SUBTRACT)
-            engine.tensor_tensor(flat[:, 1], prod[0][:, 1], prod[1][:, 0], ADD)
+        def add_terms(i, by_aer, by_aei):
+            engine = nc.vector if i == LAST else nc.gpsimd
+            engine.tensor_tensor(rounded(i).rearrange("p h n t -> p h (n t)"), by_aer[:], by_aei[:], ADD)
 
-        def turn(i, prod, part):
+        def turn(i, by_aer, by_aei, part):
             acc = bank("for_scalar")[:].rearrange("p (t n) -> p t n", t=PACK)
-            for term in range(2):
+            for term, prod in enumerate((by_aei, by_aer)):
                 for t in range(PACK):
                     nc.tensor.matmul(
-                        acc[:, t, :], lhsT=prod[1 - term][:, part, t * P : (t + 1) * P], rhs=ident[:],
+                        acc[:, t, :], lhsT=prod[:, part, t * P : (t + 1) * P], rhs=ident[:],
                         start=(term == 0 and t == 0), stop=(term == 1 and t == PACK - 1), is_transpose=True,
                     )
             nc.scalar.copy(rounded(i)[:, part], acc.rearrange("p t n -> p n t"))
@@ -307,46 +287,36 @@ def tile_list_ckg_sig_kernel(
                 rows = out[P * n * per_bank : P * (n + 1) * per_bank, first * TILE : first * TILE + width]
                 nc.sync.dma_start(out=rows.rearrange("(h p) n -> p h n", p=P), in_=result[:])
 
-        for name, chunk, count in HEAD_GATHERS:
-            gather(name, chunk, count)
-            if SPREAD and name == "scales_r":
-                for s in range(4):
-                    nc.sync.dma_start(out=moved_r[s:P:32, :], in_=whole["scales_r", 0].bitcast(I32)[8 * s : P : 32, :])
-                for n in range(CHUNKS):
-                    picked["scales_r", n] = moved_r[:].bitcast(U8)[:, n * CHUNK : (n + 1) * CHUNK]
-                for later in SYNC_LOADS[split + 1 :]:
-                    for dst, src in named[later]:
-                        nc.sync.dma_start(out=dst, in_=src)
-        rels = {i: relation(i) for i in range(RELATION_AHEAD)}
-        next_relation = RELATION_AHEAD
-        reals = {i: pool_products(i, rels[i]) for i in range(POOL_AHEAD + 1) if i in pool_product_tiles}
+        gather("scales_e", 0, 1)
+        gather("scales_e", 1, 1)
+        gather("codes_r", 0, 1)
+        gather("codes_r", 1, 1)
+        gather("codes_r", 2, 2)
+        gather("codes_e", 0, 1)
+        gather("codes_e", 1, 1)
+        rels = {i: relation(i) for i in range(RELATION_HEAD)}
+        helped = {i: help_with(i, rels[i]) for i in range(HELP_AHEAD) if i in HELPED_TILES}
         ents = {0: entity(0)}
         prods = {}
         for step in range(SCORE_STEPS[-1] + 1):
-            turns = 1 <= step <= TILES and step - 1 not in pool_sum_tiles
-            if turns and TURN_FIRST:
-                turn(step - 1, prods[step - 1], 0)
             if step + 1 < TILES:
                 ents[step + 1] = entity(step + 1)
-            for n in range(RELATION_PACE[step] if step < len(RELATION_PACE) else 0):
-                rels[next_relation] = relation(next_relation)
-                next_relation = next_relation + 1
-            if step + 1 + POOL_AHEAD in pool_product_tiles:
-                reals[step + 1 + POOL_AHEAD] = pool_products(step + 1 + POOL_AHEAD, rels[step + 1 + POOL_AHEAD])
-            if step in SCORE_STEPS and SCORE_FIRST:
+            if step >= RELATION_RESUMES:
+                for i in range(len(rels), min(step + RELATION_AHEAD, LAST) + 1):
+                    rels[i] = relation(i)
+            if step + HELP_AHEAD in HELPED_TILES:
+                helped[step + HELP_AHEAD] = help_with(step + HELP_AHEAD, rels[step + HELP_AHEAD])
+            if step in SCORE_STEPS:
                 score(*SCORE_GROUPS[SCORE_STEPS.index(step)])
-            if turns and not TURN_FIRST:
-                turn(step - 1, prods[step - 1], 0)
-            if turns:
-                turn(step - 1, prods[step - 1], 1)
-            if step in SCORE_STEPS and not SCORE_FIRST:
-                score(*SCORE_GROUPS[SCORE_STEPS.index(step)])
+            if 1 <= step <= TILES and step - 1 not in CHANNEL_TILES:
+                turn(step - 1, *prods[step - 1], 0)
+                turn(step - 1, *prods[step - 1], 1)
             if step < TILES:
-                prods[step] = products(step, rels[step], ents[step][0], ents[step][1], reals.get(step))
-            if step in pool_sum_tiles:
-                add_terms(step, prods[step])
+                prods[step] = products(step, rels[step], *ents[step], helped.get(step))
+            if step in CHANNEL_TILES:
+                add_terms(step, *prods[step])
             if step in LATE_GATHERS:
-                name, chunk, count, old_name, old_chunk = LATE_GATHERS[step]
-                gather(name, chunk, count, into=whole[old_name, old_chunk])
+                name, chunk = LATE_GATHERS[step]
+                gather(name, chunk, 1, into=picked[name, chunk - 2])
             if step in QUANTISE_STEPS:
                 quantise(*SCORE_GROUPS[QUANTISE_STEPS.index(step)])

@@ -16,42 +16,46 @@ FP8X4 = mybir.dt.float8_e4m3fn_x4
 FP4X4 = mybir.dt.float4_e2m1fn_x4
 MULT = mybir.AluOpType.mult
 ADD = mybir.AluOpType.add
+SUBTRACT = mybir.AluOpType.subtract
 SIGMOID = mybir.ActivationFunctionType.Sigmoid
 
 P = 128
 PACK = 4
 LINE = 16
-QUADRANT = 32
-SCALE_ROWS = 16
 CHUNK = 512
 TILE = 128
 CHUNKS = J // CHUNK
 TILES = J // TILE
 TILES_PER_CHUNK = CHUNK // TILE
 
-LAST = TILES - 1
-CHANNEL_TILES = tuple(range(1, LAST, 3)) + (LAST,)
-PLAIN_TILES = tuple(range(5, LAST, 6)) + (LAST - 1,)
-HELPED_TILES = tuple(i for i in range(LAST) if i not in CHANNEL_TILES + PLAIN_TILES) + (LAST,)
-
-RELATION_HEAD = 5
-RELATION_RESUMES = 2
-RELATION_AHEAD = RELATION_HEAD - 1
-RELATION_DEPTH = RELATION_AHEAD + 2
+KINDS = "BBCBCABCABCABCAW"
+RELATION_HEAD = 4
+RELATION_DEPTH = 5
 HELP_AHEAD = 3
-AER_DEPTH = 3
-PRODUCT_DEPTH = 6
-BANKS = 4
-
+TURN_LAG = 1
+SUM_LAG = 0
+STEP_ORDER = "pers10"
+REAL_DEPTH = 8
+IMAG_DEPTH = 4
+AER_DEPTH = 4
+SCALAR_BANKS = 4
+VECTOR_BANKS = 4
+TWO_SUMS = True
+HOLD = {}
 SCORE_GROUPS = ((0, 4), (4, 4), (8, 4), (12, 2), (14, 1), (15, 1))
-QUANTISE_STEPS = (7, 11, LAST - 1, TILES, TILES + 1, TILES + 2)
-SCORE_STEPS = (8, 12, TILES, TILES + 1, TILES + 2, TILES + 3)
-LATE_GATHERS = {2: ("scales_e", 2), 3: ("codes_e", 2), 6: ("scales_e", 3), 7: ("codes_e", 3)}
-
+QUANTISE_STEPS = (9, 12, 14, 14, 15, 17)
+SCORE_STEPS = (13, 14, 16, 17, 18, 19)
+RELATION_FROM = 0
+LATE_STEPS = (2,8)
+LATE = (("codes_e", 2, 1, "codes_e", 0), ("codes_e", 3, 1, "codes_e", 1))
+SYNC_LOADS = ("list_r", "wrr", "spread_r", "wri", "wrr_rows", "wri_rows", "list_e", "spread_e", "spread_w", "wer", "words_r", "wei", "moves_w_1", "moves_r", "words_e", "moves_w_234", "moves_e", "nr", "ni", "nr_rows", "ni_rows")
+HALVES_ON = "S"
+POOL_LOADS = ()
+DIRECT_E = False
+HELP_FIRST = True
+ENTITY_AHEAD = 1
 WRR_ROW = 4
 WRI_ROW = 8
-WRI_ROWS_AHEAD = 3
-WEI_ROWS_AHEAD = 1
 
 
 def tile_list_ckg_sig_kernel(
@@ -59,6 +63,8 @@ def tile_list_ckg_sig_kernel(
     wrr_words, wrr_scales, wri_words, wri_scales, nr_words, nr_scales, ni_words, ni_scales, offs, offs2, out,
 ):
     nc = tc.nc
+    channel_tiles = [i for i in range(TILES) if KINDS[i] in "CVWE"]
+    helped_tiles = [i for i in range(TILES) if KINDS[i] in "BWE"]
     with ExitStack() as ctx:
         keep = ctx.enter_context(tc.tile_pool(name="keep", bufs=1))
         psum = ctx.enter_context(tc.psum_pool(name="psum", bufs=1))
@@ -76,177 +82,273 @@ def tile_list_ckg_sig_kernel(
             return next_of(name, depth, lambda label: keep.tile(shape, F32, name=label, align_bytes=64))
 
         def bank(name):
-            return next_of(name, BANKS, lambda label: psum.tile([P, CHUNK], F32, name=label))
+            depth = SCALAR_BANKS if name == "for_scalar" else VECTOR_BANKS
+            return next_of(name, depth, lambda label: psum.tile([P, CHUNK], F32, name=label))
 
         list_e = keep.tile([P, J // 16], U16, name="list_e")
         list_r = keep.tile([P, J // 16], U16, name="list_r")
         words_e = keep.tile([P, T], I32, name="words_e", align_bytes=64)
         words_r = keep.tile([P, T], I32, name="words_r", align_bytes=64)
-        plane_e = keep.tile([P, T // 4], I32, name="plane_e", align_bytes=64)
-        spread_r = keep.tile([P, T // 4], I32, name="plane_r", align_bytes=64)
         ident = keep.tile([P, P], F32, name="ident", align_bytes=64)
+        warm = keep.tile([P, 2], F32, name="warm")
 
-        def row_loads(plane, scales, first_row, first_column=0):
+        def zeroed_plane(name, columns):
+            plane = keep.tile([P, columns // 4], I32, name=name, align_bytes=64)
+            nc.vector.memset(plane[:], 0)
+            return plane
+
+        if not POOL_LOADS:
+            shared_plane = zeroed_plane("shared_plane", R)
+        plane_r = zeroed_plane("plane_r", T)
+        plane_e = zeroed_plane("plane_e", T)
+        if not DIRECT_E:
+            spread_w = zeroed_plane("spread_w", 2 * R)
+        nc.vector.memset(warm[:, 0:1], 0.0)
+        nc.scalar.activation(warm[:, 1:2], warm[:, 0:1], SIGMOID)
+        moved_r = zeroed_plane("moved_r", J)
+        moved_e = zeroed_plane("moved_e", J)
+        entity_planes = zeroed_plane("entity_planes", 2 * R)
+        score_planes = zeroed_plane("score_planes", 2 * N)
+        if POOL_LOADS:
+            shared_plane = zeroed_plane("shared_plane", R)
+
+        def row_loads(plane, scales, first_row=0, first_column=0):
             rows = scales[0].bitcast(I32)
             columns = slice(first_column // 4, first_column // 4 + rows.shape[1])
-            return [(plane[first_row + s : P : QUADRANT, columns], rows[s:SCALE_ROWS:4, :]) for s in range(4)]
+            return [(plane[first_row + s : P : 32, columns], rows[s:16:4, :]) for s in range(4)]
 
         def flat_words(words):
             return words[0].rearrange("p c i -> p (c i)")
 
-        def weight(name, words, scales, plane, first_row, first_column=0):
-            codes = keep.tile([P, words.shape[1]], U8, name=name, align_bytes=64)
-            return {
-                "codes": codes[:], "plane": plane[:].bitcast(U8),
-                "load": (codes[:].bitcast(I32), words.bitcast(I32)),
-                "rows": row_loads(plane, scales, first_row, first_column),
-            }
-
-        nc.vector.memset(spread_r[:], 0)
-        relation_plane = keep.tile([P, R // 4], I32, name="relation_plane", align_bytes=64)
-        nc.vector.memset(relation_plane[:], 0)
-        wrr = weight("wrr", flat_words(wrr_words), wrr_scales, relation_plane, WRR_ROW)
-        wri = weight("wri", flat_words(wri_words), wri_scales, relation_plane, WRI_ROW)
-        nc.vector.memset(plane_e[:], 0)
-        gathered_plane_r = wrr["codes"].bitcast(I32)
-        late_planes = wri["codes"].bitcast(I32)[:, : (2 * R + 2 * N) // 4]
-        entity_plane = late_planes[:, : 2 * R // 4]
-        wer = weight("wer", wer_words[0], wer_scales, entity_plane, 0)
-        wei = weight("wei", wei_words[0], wei_scales, entity_plane, 0, R)
-        nr = weight("nr", nr_words[0], nr_scales, late_planes[:, 2 * R // 4 : (2 * R + N) // 4], 0)
-        ni = weight("ni", ni_words[0], ni_scales, late_planes[:, (2 * R + N) // 4 :], 0)
+        raw = {}
+        named = {
+            "list_r": [(list_r[:], offs2)], "list_e": [(list_e[:], offs)],
+            "spread_r": [(plane_r[0:P:8, :], tab2_scales[0].bitcast(I32))],
+            "spread_e": [(plane_e[0:P:8, :], tab_scales[0].bitcast(I32))],
+            "words_r": [(words_r[:], flat_words(tab2_words).bitcast(I32))],
+            "words_e": [(words_e[:], flat_words(tab_words).bitcast(I32))],
+            "wrr_rows": row_loads(shared_plane, wrr_scales, WRR_ROW),
+            "wri_rows": row_loads(shared_plane, wri_scales, WRI_ROW),
+            "wer_rows": row_loads(entity_planes, wer_scales),
+            "wei_rows": row_loads(entity_planes, wei_scales, 0, R),
+            "wei_1": row_loads(entity_planes, wei_scales, 0, R)[:1],
+            "wei_234": row_loads(entity_planes, wei_scales, 0, R)[1:],
+            "spread_w": [] if DIRECT_E else [
+                (spread_w[0:P:8, n * R // 4 : (n + 1) * R // 4], scales[0].bitcast(I32))
+                for n, scales in enumerate((wer_scales, wei_scales))
+            ],
+            "nr_rows": row_loads(score_planes, nr_scales),
+            "ni_rows": row_loads(score_planes, ni_scales, 0, N),
+        }
+        for name, words in (
+            ("wrr", flat_words(wrr_words)), ("wri", flat_words(wri_words)), ("wer", wer_words[0]),
+            ("wei", wei_words[0]), ("nr", nr_words[0]), ("ni", ni_words[0]),
+        ):
+            raw[name] = keep.tile([P, words.shape[1]], U8, name=name, align_bytes=64)
+            named[name] = [(raw[name][:].bitcast(I32), words.bitcast(I32))]
 
         sources = {
-            "scales_r": (spread_r, list_r, U8), "codes_r": (words_r, list_r, U32),
+            "scales_r": (plane_r, list_r, U8), "codes_r": (words_r, list_r, U32),
             "scales_e": (plane_e, list_e, U8), "codes_e": (words_e, list_e, U32),
         }
         picked = {}
+        whole = {}
+        room_a = keep.tile([P, J], U8, name="room_a", align_bytes=64)
+        room_b = keep.tile([P, CHUNK], U32, name="room_b", align_bytes=64)
+        spread = {}
+        moved = {"scales_r": moved_r, "scales_e": moved_e}
 
         def gather(name, chunk, count, into=None):
             window, offsets, dtype = sources[name]
+            spread[name, chunk] = into
             if into is None:
                 into = keep.tile([P, count * CHUNK], dtype, name="%s_%d" % (name, chunk), align_bytes=64)[:]
+                whole[name, chunk] = into
             columns = slice(chunk * CHUNK // 16, (chunk + count) * CHUNK // 16)
             nc.vector.tensor_copy(into, window[:].bitcast(dtype).indirect(offsets[:, columns]))
             for n in range(count):
                 picked[name, chunk + n] = into[:, n * CHUNK : (n + 1) * CHUNK]
-            return into
 
-        def reorder(name, source, dtype, size, engine, count=1):
-            run = LINE // size
-            ordered = keep.tile([P, count, PACK, R // PACK], dtype, name=name, align_bytes=64)
-            engine.tensor_copy(
-                ordered[:].rearrange("p w t (c i) -> p w c t i", i=run),
-                source.bitcast(dtype).rearrange("p (w c i t) -> p w c t i", w=count, i=run, t=PACK),
+        def move_rows(name, chunk, count):
+            columns = slice(chunk * CHUNK // 4, (chunk + count) * CHUNK // 4)
+            for s in range(4):
+                nc.sync.dma_start(out=moved[name][s:P:32, columns], in_=spread[name, chunk][8 * s : P : 32, :].bitcast(I32))
+            for n in range(chunk, chunk + count):
+                picked[name, n] = moved[name][:].bitcast(U8)[:, n * CHUNK : (n + 1) * CHUNK]
+
+        slots = {}
+
+        def reorder_words(name):
+            ordered = keep.tile([P, PACK, R // PACK], U32, name=name + "_slots", align_bytes=64)
+            nc.scalar.copy(
+                ordered[:].rearrange("p t (c i) -> p c t i", i=PACK),
+                raw[name][:].bitcast(U32).rearrange("p (c i t) -> p c t i", i=PACK, t=PACK),
+            )
+            slots[name] = ordered[:].rearrange("p t m -> p (t m)").bitcast(FP8X4)
+
+        def reorder_halves(name):
+            ordered = keep.tile([P, PACK, R // PACK, 2], U8, name=name + "_slots", align_bytes=64)
+            if HALVES_ON == "G":
+                nc.gpsimd.tensor_copy(ordered[:], raw[name][:].rearrange("p (m t b) -> p t m b", t=PACK, b=2))
+            else:
+                engine = nc.scalar.copy if HALVES_ON == "S" else nc.vector.tensor_copy
+                engine(
+                    ordered[:].rearrange("p t m b -> p (t m b)").bitcast(U16).rearrange("p (t c i) -> p c t i", t=PACK, i=8),
+                    raw[name][:].bitcast(U16).rearrange("p (c i t) -> p c t i", i=8, t=PACK),
+                )
+            slots[name] = ordered[:].rearrange("p t m b -> p (t m b)")
+
+        def reorder_scales(name, plane, count):
+            ordered = keep.tile([P, count, PACK, R // PACK], U8, name=name, align_bytes=64)
+            nc.gpsimd.tensor_copy(
+                ordered[:].rearrange("p w t (c i) -> p w c t i", i=LINE),
+                plane[:].bitcast(U8).rearrange("p (w c i t) -> p w c t i", w=count, i=LINE, t=PACK),
             )
             return ordered[:].rearrange("p w t m -> p (w t m)")
 
-        def load(pairs, queue=nc.sync):
-            for dst, src in pairs:
-                queue.dma_start(out=dst, in_=src)
-
-        load(wrr["rows"], nc.gpsimd)
-        step_r = P // SCALE_ROWS
-        load([(list_r[:], offs2), wer["load"], wei["load"], (spread_r[0:P:step_r, :], tab2_scales[0].bitcast(I32))])
-        load([(list_e[:], offs), wrr["load"], wri["load"]])
-        wrr_ordered = reorder("wrr_slots", wrr["codes"], I32, 4, nc.gpsimd)
-        wri_ordered = reorder("wri_slots", wri["codes"], I32, 4, nc.gpsimd)
-        nc.gpsimd.memset(late_planes, 0)
-        nc.gpsimd.memset(gathered_plane_r, 0)
-        load(row_loads(plane_e, tab_scales, 0) + wri["rows"][:WRI_ROWS_AHEAD])
-        load([(words_r[:], flat_words(tab2_words).bitcast(I32))] + wri["rows"][WRI_ROWS_AHEAD:])
-        load(wei["rows"][:WEI_ROWS_AHEAD])
-        spread_picked = gather("scales_r", 0, CHUNKS).bitcast(I32)
-        load([(gathered_plane_r[s:P:QUADRANT, :], spread_picked[step_r * s : P : QUADRANT, :]) for s in range(4)])
-        for chunk in range(CHUNKS):
-            picked["scales_r", chunk] = gathered_plane_r.bitcast(U8)[:, chunk * CHUNK : (chunk + 1) * CHUNK]
-        load([(words_e[:], flat_words(tab_words).bitcast(I32))] + wei["rows"][WEI_ROWS_AHEAD:] + wer["rows"])
-        load([nr["load"], ni["load"]] + nr["rows"] + ni["rows"])
-
-        relation_scales = reorder("relation_slots", wrr["plane"], U8, 1, nc.gpsimd)
-        slots_wrr = (wrr_ordered, relation_scales[WRR_ROW:P, :])
-        slots_wri = (wri_ordered, relation_scales[WRI_ROW:P, :])
-        entity_scales = reorder("entity_slots", wei["plane"], U8, 1, nc.gpsimd, 2)
-        slots_wer = (reorder("wer_slots", wer["codes"], U16, 2, nc.vector), entity_scales[:, :R])
-        slots_wei = (reorder("wei_slots", wei["codes"], U16, 2, nc.vector), entity_scales[:, R:])
+        for name in POOL_LOADS:
+            for dst, src in named[name]:
+                nc.gpsimd.dma_start(out=dst, in_=src)
         make_identity(nc, ident[:])
+        for name in SYNC_LOADS:
+            if name == "moves_r":
+                gather("scales_r", 0, CHUNKS, room_a[:])
+                move_rows("scales_r", 0, CHUNKS)
+            elif name == "moves_w_1":
+                spread_slots = reorder_scales("spread_slots", spread_w, 2).bitcast(I32)
+                nc.sync.dma_start(out=entity_planes[0:P:32, :], in_=spread_slots[0:P:32, :])
+            elif name == "moves_w_234":
+                for s in range(1, 4):
+                    nc.sync.dma_start(out=entity_planes[s:P:32, :], in_=spread_slots[8 * s : P : 32, :])
+            elif name == "moves_e":
+                gather("scales_e", 0, 2, room_b[:].bitcast(U8)[:, : 2 * CHUNK])
+                gather("codes_r", 0, 1)
+                gather("codes_r", 2, 2)
+                gather("scales_e", 2, 2, room_a[:, : 2 * CHUNK])
+                gather("codes_e", 0, 1)
+                move_rows("scales_e", 0, 2)
+                move_rows("scales_e", 2, 2)
+                gather("codes_r", 1, 1, room_b[:])
+                gather("codes_e", 1, 1)
+            else:
+                for dst, src in named[name]:
+                    nc.sync.dma_start(out=dst, in_=src)
+                if name in ("wrr", "wri"):
+                    reorder_words(name)
+                if name in ("wer", "wei"):
+                    reorder_halves(name)
+        shared_slots = reorder_scales("shared_slots", shared_plane, 1)
+        plane_of = {
+            "wrr": shared_slots[WRR_ROW:P, :], "wri": shared_slots[WRI_ROW:P, :],
+            "wer": entity_planes[:].bitcast(U8)[:, :R], "wei": entity_planes[:].bitcast(U8)[:, R:],
+            "nr": score_planes[:].bitcast(U8)[:, :N], "ni": score_planes[:].bitcast(U8)[:, N:],
+        }
 
-        def project(ring, side, i, slots, fmt):
+        if DIRECT_E:
+            plane_of["wer"] = reorder_scales("wer_scale_slots", entity_planes[:, : R // 4], 1)
+            plane_of["wei"] = reorder_scales("wei_scale_slots", entity_planes[:, R // 4 :], 1)
+
+        def columns_of(name, first, count):
+            if name in ("wrr", "wri"):
+                return slots[name][:, first : first + count]
+            return slots[name][:, 2 * first : 2 * (first + count)].bitcast(FP4X4)
+
+        def project(ring, side, i, name):
             chunk, place = divmod(i, TILES_PER_CHUNK)
             tokens = slice(place * TILE, (place + 1) * TILE)
             codes = picked["codes_" + side, chunk][:, tokens].bitcast(FP8X4)
             scales = picked["scales_" + side, chunk][:, tokens]
             acc = bank(ring)
-            if i in CHANNEL_TILES:
+            if i in channel_tiles:
                 by_slot = acc[:].rearrange("p (t n) -> p t n", t=PACK)
                 for t in range(PACK):
                     nc.tensor.matmul_mx(
-                        out=by_slot[:, t, :], lhsT=slots[0][:, t * P : (t + 1) * P].bitcast(fmt),
-                        lhsT_scale=slots[1][:, t * P : (t + 1) * P],
+                        out=by_slot[:, t, :], lhsT=columns_of(name, t * P, P),
+                        lhsT_scale=plane_of[name][:, t * P : (t + 1) * P],
                         rhs=codes, rhs_scale=scales, start=True, stop=True,
                     )
                 return by_slot.rearrange("p t n -> p n t")
             nc.tensor.matmul_mx(
                 out=acc[:], lhsT=codes, lhsT_scale=scales,
-                rhs=slots[0].bitcast(fmt), rhs_scale=slots[1], start=True, stop=True,
+                rhs=columns_of(name, 0, R), rhs_scale=plane_of[name], start=True, stop=True,
             )
             return acc[:]
 
-        def like_sums(i, columns):
-            return columns.rearrange("p (n t) -> p n t", t=PACK) if i in CHANNEL_TILES else columns
+        def as_sums(i, flat):
+            if i in channel_tiles:
+                return flat.rearrange("p (n t) -> p n t", t=PACK)
+            return flat
 
         def relation(i):
             rel = ring_tile("rel", [P, 2, R], RELATION_DEPTH)
-            sums = [project("for_scalar", "r", i, slots, FP8X4) for slots in (slots_wrr, slots_wri)]
+            sums = [project("for_scalar", "r", i, name) for name in ("wrr", "wri")]
             for part in range(2):
-                nc.scalar.copy(like_sums(i, rel[:, part]), sums[part])
+                nc.scalar.copy(as_sums(i, rel[:, part]), sums[part])
             return rel
 
         def entity(i):
-            aer = None if i in HELPED_TILES else project("entity", "e", i, slots_wer, FP4X4)
-            return aer, project("entity", "e", i, slots_wei, FP4X4)
+            aer = None if i in helped_tiles else project("entity", "e", i, "wer")
+            return aer, project("entity", "e", i, "wei")
 
-        def help_with(i, rel):
-            aer_copy = ring_tile("aer_copy", [P, R], AER_DEPTH)
-            nc.scalar.copy(like_sums(i, aer_copy[:]), project("for_scalar", "e", i, slots_wer, FP4X4))
-            by_aer = ring_tile("real", [P, 2, R], PRODUCT_DEPTH)
-            nc.gpsimd.tensor_tensor(by_aer[:], aer_copy[:].unsqueeze(1).broadcast_to([P, 2, R]), rel[:], MULT)
-            return by_aer
-
-        def products(i, rel, aer, aei, by_aer):
-            if by_aer is None:
-                by_aer = ring_tile("real", [P, 2, R], PRODUCT_DEPTH)
-            by_aei = ring_tile("imag", [P, 2, R], PRODUCT_DEPTH)
-            nc.vector.scalar_tensor_tensor(like_sums(i, by_aei[:, 0]), aei, -1.0, like_sums(i, rel[:, 1]), MULT, MULT)
-            nc.vector.tensor_tensor(like_sums(i, by_aei[:, 1]), aei, like_sums(i, rel[:, 0]), MULT)
-            if i in PLAIN_TILES:
-                nc.vector.tensor_tensor(by_aer[:], aer.unsqueeze(1).broadcast_to([P, 2, R]), rel[:], MULT)
-            elif i not in HELPED_TILES:
-                nc.vector.tensor_tensor(
-                    by_aer[:].rearrange("p h (n t) -> p h n t", t=PACK),
-                    aer.unsqueeze(1).broadcast_to([P, 2, TILE, PACK]),
-                    rel[:].rearrange("p h (n t) -> p h n t", t=PACK), MULT,
-                )
-            return by_aer, by_aei
-
-        h_rounded = {}
+        h_tiles = {}
+        for first, count in SCORE_GROUPS:
+            h_tiles[first] = keep.tile([P, count * TILE * PACK], F32, name="h_%d" % first, align_bytes=64)
 
         def rounded(i):
             first, count = [group for group in SCORE_GROUPS if group[0] <= i][-1]
-            if first not in h_rounded:
-                h_rounded[first] = keep.tile([P, 2, count * TILE, PACK], BF16, name="h_%d" % first, align_bytes=64)
-            return h_rounded[first][:, :, (i - first) * TILE : (i - first + 1) * TILE, :]
+            view = h_tiles[first][:].bitcast(BF16).rearrange("p (h n t) -> p h n t", h=2, t=PACK)
+            return view[:, :, (i - first) * TILE : (i - first + 1) * TILE, :]
 
-        def add_terms(i, by_aer, by_aei):
-            engine = nc.vector if i == LAST else nc.gpsimd
-            engine.tensor_tensor(rounded(i).rearrange("p h n t -> p h (n t)"), by_aer[:], by_aei[:], ADD)
+        def real_room(i):
+            if i in HOLD:
+                first, half = HOLD[i]
+                return h_tiles[first][:, half * 2 * R : (half + 1) * 2 * R].rearrange("p (h r) -> p h r", h=2)
+            return ring_tile("real", [P, 2, R], REAL_DEPTH)[:]
 
-        def turn(i, by_aer, by_aei, part):
+        def help_products(i, rel):
+            aer_copy = ring_tile("aer_copy", [P, R], AER_DEPTH)
+            nc.scalar.copy(as_sums(i, aer_copy[:]), project("for_scalar", "e", i, "wer"))
+            real = real_room(i)
+            nc.gpsimd.tensor_tensor(real, aer_copy[:].unsqueeze(1).broadcast_to([P, 2, R]), rel[:], MULT)
+            return real
+
+        def both(i, target, acc, rel):
+            if i in channel_tiles:
+                nc.vector.tensor_tensor(
+                    target.rearrange("p h (n t) -> p h n t", t=PACK),
+                    acc.unsqueeze(1).broadcast_to([P, 2, TILE, PACK]),
+                    rel[:].rearrange("p h (n t) -> p h n t", t=PACK), MULT,
+                )
+            else:
+                nc.vector.tensor_tensor(target, acc.unsqueeze(1).broadcast_to([P, 2, R]), rel[:], MULT)
+
+        def products(i, rel, aer, aei, real):
+            imag = ring_tile("imag", [P, 2, R], IMAG_DEPTH)[:]
+            if aer is not None:
+                real = real_room(i)
+                both(i, real, aer, rel)
+            if TWO_SUMS and i in channel_tiles:
+                both(i, imag, aei, rel)
+            else:
+                nc.vector.scalar_tensor_tensor(as_sums(i, imag[:, 0]), aei, -1.0, as_sums(i, rel[:, 1]), MULT, MULT)
+                nc.vector.tensor_tensor(as_sums(i, imag[:, 1]), aei, as_sums(i, rel[:, 0]), MULT)
+            return real, imag
+
+        def add_terms(i, prod):
+            flat = rounded(i).rearrange("p h n t -> p h (n t)")
+            engine = nc.vector if KINDS[i] in "VW" else nc.gpsimd
+            if TWO_SUMS:
+                engine.tensor_tensor(flat[:, 0], prod[0][:, 0], prod[1][:, 1], SUBTRACT)
+                engine.tensor_tensor(flat[:, 1], prod[0][:, 1], prod[1][:, 0], ADD)
+            else:
+                engine.tensor_tensor(flat, prod[0], prod[1], ADD)
+
+        def turn(i, prod, part):
             acc = bank("for_scalar")[:].rearrange("p (t n) -> p t n", t=PACK)
-            for term, prod in enumerate((by_aei, by_aer)):
+            for term in range(2):
                 for t in range(PACK):
                     nc.tensor.matmul(
-                        acc[:, t, :], lhsT=prod[:, part, t * P : (t + 1) * P], rhs=ident[:],
+                        acc[:, t, :], lhsT=prod[term][:, part, t * P : (t + 1) * P], rhs=ident[:],
                         start=(term == 0 and t == 0), stop=(term == 1 and t == PACK - 1), is_transpose=True,
                     )
             nc.scalar.copy(rounded(i)[:, part], acc.rearrange("p t n -> p n t"))
@@ -257,10 +359,7 @@ def tile_list_ckg_sig_kernel(
             width = count * TILE
             h_codes = keep.tile([P, 2 * width], U32, name="h_codes_%d" % first, align_bytes=64)
             h_scales = keep.tile([P, 2 * width], U8, name="h_scales_%d" % first, align_bytes=64)
-            nc.vector.quantize_mx(
-                out=h_codes[:].bitcast(FP8X4), scales=h_scales[:],
-                in_=h_rounded[first][:].rearrange("p h n t -> p (h n t)"),
-            )
+            nc.vector.quantize_mx(out=h_codes[:].bitcast(FP8X4), scales=h_scales[:], in_=h_tiles[first][:].bitcast(BF16))
             h_packed[first] = (h_codes, h_scales)
 
         def score(first, count):
@@ -273,12 +372,12 @@ def tile_list_ckg_sig_kernel(
                 for place in range(per_bank):
                     half = n * per_bank + place
                     for begin in range(0, width, span):
-                        for part, w in enumerate((nr, ni)):
+                        for part, name in enumerate(("nr", "ni")):
                             tokens = slice(part * width + begin, part * width + begin + span)
                             nc.tensor.matmul_mx(
                                 out=acc[:, place, begin : begin + span],
-                                lhsT=w["codes"][:, 2 * P * half : 2 * P * (half + 1)].bitcast(FP4X4),
-                                lhsT_scale=w["plane"][:, P * half : P * (half + 1)],
+                                lhsT=raw[name][:, 2 * P * half : 2 * P * (half + 1)].bitcast(FP4X4),
+                                lhsT_scale=plane_of[name][:, P * half : P * (half + 1)],
                                 rhs=h_codes[:, tokens].bitcast(FP8X4), rhs_scale=h_scales[:, tokens],
                                 start=(part == 0), stop=(part == 1),
                             )
@@ -287,36 +386,37 @@ def tile_list_ckg_sig_kernel(
                 rows = out[P * n * per_bank : P * (n + 1) * per_bank, first * TILE : first * TILE + width]
                 nc.sync.dma_start(out=rows.rearrange("(h p) n -> p h n", p=P), in_=result[:])
 
-        gather("scales_e", 0, 1)
-        gather("scales_e", 1, 1)
-        gather("codes_r", 0, 1)
-        gather("codes_r", 1, 1)
-        gather("codes_r", 2, 2)
-        gather("codes_e", 0, 1)
-        gather("codes_e", 1, 1)
         rels = {i: relation(i) for i in range(RELATION_HEAD)}
-        helped = {i: help_with(i, rels[i]) for i in range(HELP_AHEAD) if i in HELPED_TILES}
-        ents = {0: entity(0)}
+        next_relation = RELATION_HEAD
+        reals = {i: help_products(i, rels[i]) for i in range(HELP_AHEAD) if i in helped_tiles and HELP_FIRST}
+        ents = {i: entity(i) for i in range(ENTITY_AHEAD)}
+        if not HELP_FIRST:
+            reals = {i: help_products(i, rels[i]) for i in range(HELP_AHEAD) if i in helped_tiles}
         prods = {}
-        for step in range(SCORE_STEPS[-1] + 1):
-            if step + 1 < TILES:
-                ents[step + 1] = entity(step + 1)
-            if step >= RELATION_RESUMES:
-                for i in range(len(rels), min(step + RELATION_AHEAD, LAST) + 1):
-                    rels[i] = relation(i)
-            if step + HELP_AHEAD in HELPED_TILES:
-                helped[step + HELP_AHEAD] = help_with(step + HELP_AHEAD, rels[step + HELP_AHEAD])
-            if step in SCORE_STEPS:
-                score(*SCORE_GROUPS[SCORE_STEPS.index(step)])
-            if 1 <= step <= TILES and step - 1 not in CHANNEL_TILES:
-                turn(step - 1, *prods[step - 1], 0)
-                turn(step - 1, *prods[step - 1], 1)
+        for step in range(max(SCORE_STEPS) + 1):
+            turned = step - TURN_LAG
+            for part in STEP_ORDER:
+                if part in "01" and 0 <= turned < TILES and turned not in channel_tiles:
+                    turn(turned, prods[turned], int(part))
+                if part == "e" and step + ENTITY_AHEAD < TILES:
+                    ents[step + ENTITY_AHEAD] = entity(step + ENTITY_AHEAD)
+                if part == "r" and step >= RELATION_FROM and next_relation < TILES:
+                    rels[next_relation] = relation(next_relation)
+                    next_relation = next_relation + 1
+                if part == "p" and step + HELP_AHEAD in helped_tiles:
+                    reals[step + HELP_AHEAD] = help_products(step + HELP_AHEAD, rels[step + HELP_AHEAD])
+                if part == "s":
+                    for n, group in enumerate(SCORE_GROUPS):
+                        if SCORE_STEPS[n] == step:
+                            score(*group)
             if step < TILES:
-                prods[step] = products(step, rels[step], *ents[step], helped.get(step))
-            if step in CHANNEL_TILES:
-                add_terms(step, *prods[step])
-            if step in LATE_GATHERS:
-                name, chunk = LATE_GATHERS[step]
-                gather(name, chunk, 1, into=picked[name, chunk - 2])
-            if step in QUANTISE_STEPS:
-                quantise(*SCORE_GROUPS[QUANTISE_STEPS.index(step)])
+                prods[step] = products(step, rels[step], ents[step][0], ents[step][1], reals.get(step))
+            if step < TILES and KINDS[step] in "VW":
+                add_terms(step, prods[step])
+            if step - SUM_LAG in channel_tiles and KINDS[step - SUM_LAG] in "CE":
+                add_terms(step - SUM_LAG, prods[step - SUM_LAG])
+            for name, chunk, count, old_name, old_chunk in [LATE[n] for n in range(len(LATE)) if LATE_STEPS[n] == step]:
+                gather(name, chunk, count, None if old_name is None else whole[old_name, old_chunk])
+            for n, group in enumerate(SCORE_GROUPS):
+                if QUANTISE_STEPS[n] == step:
+                    quantise(*group)

@@ -28,31 +28,35 @@ CHUNKS = J // CHUNK
 TILES = J // TILE
 TILES_PER_CHUNK = CHUNK // TILE
 
-KINDS = "BBCBCABCABCABCAW"
-RELATION_HEAD = 4
-RELATION_DEPTH = 5
+KINDS = "BCBBCABCBBCABCAW"
+RELATION_HEAD = 5
+RELATION_DEPTH = 6
 HELP_AHEAD = 3
 TURN_LAG = 1
 SUM_LAG = 0
-STEP_ORDER = "pers10"
-REAL_DEPTH = 8
-IMAG_DEPTH = 4
-AER_DEPTH = 4
+STEP_ORDER = "erps01"
+REAL_DEPTH = 6
+IMAG_DEPTH = 6
+AER_DEPTH = 3
 SCALAR_BANKS = 4
 VECTOR_BANKS = 4
-TWO_SUMS = True
+TWO_SUMS = False
 HOLD = {}
 SCORE_GROUPS = ((0, 4), (4, 4), (8, 4), (12, 2), (14, 1), (15, 1))
-QUANTISE_STEPS = (9, 12, 14, 14, 15, 17)
-SCORE_STEPS = (13, 14, 16, 17, 18, 19)
-RELATION_FROM = 0
-LATE_STEPS = (2,8)
-LATE = (("codes_e", 2, 1, "codes_e", 0), ("codes_e", 3, 1, "codes_e", 1))
-SYNC_LOADS = ("list_r", "wrr", "spread_r", "wri", "wrr_rows", "wri_rows", "list_e", "spread_e", "spread_w", "wer", "words_r", "wei", "moves_w_1", "moves_r", "words_e", "moves_w_234", "moves_e", "nr", "ni", "nr_rows", "ni_rows")
-HALVES_ON = "S"
+QUANTISE_STEPS = (7, 11, 14, 16, 17, 18)
+SCORE_STEPS = (8, 12, 16, 17, 18, 19)
+RELATION_FROM = 1
+LATE_STEPS = (1,3,7)
+LATE = (("scales_e", 2, 2, "scales_e", 0), ("codes_e", 2, 1, "codes_e", 0), ("codes_e", 3, 1, "codes_e", 1))
+SYNC_LOADS = ("list_r", "list_e", "spread_r", "spread_e", "spread_w", "first_rows", "words_r", "wrr", "wri", "moves_r", "words_e", "wer", "wei", "moves_e", "nr", "ni", "nr_rows", "ni_rows")
+HALVES_ON = "G"
 POOL_LOADS = ()
+JOINT = 2
+SYNC_ROWS = 1
+FOURTH = True
 DIRECT_E = False
 HELP_FIRST = True
+IMAG_FIRST = True
 ENTITY_AHEAD = 1
 WRR_ROW = 4
 WRI_ROW = 8
@@ -97,20 +101,17 @@ def tile_list_ckg_sig_kernel(
             nc.vector.memset(plane[:], 0)
             return plane
 
-        if not POOL_LOADS:
-            shared_plane = zeroed_plane("shared_plane", R)
         plane_r = zeroed_plane("plane_r", T)
         plane_e = zeroed_plane("plane_e", T)
-        if not DIRECT_E:
-            spread_w = zeroed_plane("spread_w", 2 * R)
+        spread_w = zeroed_plane("spread_w", 2 * R)
+        shared_plane = zeroed_plane("shared_plane", R)
         nc.vector.memset(warm[:, 0:1], 0.0)
         nc.scalar.activation(warm[:, 1:2], warm[:, 0:1], SIGMOID)
-        moved_r = zeroed_plane("moved_r", J)
-        moved_e = zeroed_plane("moved_e", J)
-        entity_planes = zeroed_plane("entity_planes", 2 * R)
-        score_planes = zeroed_plane("score_planes", 2 * N)
-        if POOL_LOADS:
-            shared_plane = zeroed_plane("shared_plane", R)
+        planes = zeroed_plane("planes", 2 * J + 2 * N)
+        moved_r = planes[:, : J // 4]
+        moved_e = planes[:, J // 4 : J // 2]
+        score_planes = planes[:, J // 2 :]
+        nc.vector.memset(ident[:], 0.0)
 
         def row_loads(plane, scales, first_row=0, first_column=0):
             rows = scales[0].bitcast(I32)
@@ -120,6 +121,7 @@ def tile_list_ckg_sig_kernel(
         def flat_words(words):
             return words[0].rearrange("p c i -> p (c i)")
 
+        relation_rows = row_loads(shared_plane, wri_scales, WRI_ROW) + row_loads(shared_plane, wrr_scales, WRR_ROW)
         raw = {}
         named = {
             "list_r": [(list_r[:], offs2)], "list_e": [(list_e[:], offs)],
@@ -127,16 +129,11 @@ def tile_list_ckg_sig_kernel(
             "spread_e": [(plane_e[0:P:8, :], tab_scales[0].bitcast(I32))],
             "words_r": [(words_r[:], flat_words(tab2_words).bitcast(I32))],
             "words_e": [(words_e[:], flat_words(tab_words).bitcast(I32))],
-            "wrr_rows": row_loads(shared_plane, wrr_scales, WRR_ROW),
-            "wri_rows": row_loads(shared_plane, wri_scales, WRI_ROW),
-            "wer_rows": row_loads(entity_planes, wer_scales),
-            "wei_rows": row_loads(entity_planes, wei_scales, 0, R),
-            "wei_1": row_loads(entity_planes, wei_scales, 0, R)[:1],
-            "wei_234": row_loads(entity_planes, wei_scales, 0, R)[1:],
-            "spread_w": [] if DIRECT_E else [
+            "spread_w": [
                 (spread_w[0:P:8, n * R // 4 : (n + 1) * R // 4], scales[0].bitcast(I32))
                 for n, scales in enumerate((wer_scales, wei_scales))
             ],
+            "first_rows": relation_rows[:SYNC_ROWS],
             "nr_rows": row_loads(score_planes, nr_scales),
             "ni_rows": row_loads(score_planes, ni_scales, 0, N),
         }
@@ -153,8 +150,8 @@ def tile_list_ckg_sig_kernel(
         }
         picked = {}
         whole = {}
-        room_a = keep.tile([P, J], U8, name="room_a", align_bytes=64)
-        room_b = keep.tile([P, CHUNK], U32, name="room_b", align_bytes=64)
+        room_a = keep.tile([P, 3 * CHUNK], U8, name="room_a", align_bytes=64)
+        room_b = keep.tile([P, J // 2], U8, name="room_b", align_bytes=64)
         spread = {}
         moved = {"scales_r": moved_r, "scales_e": moved_e}
 
@@ -198,6 +195,8 @@ def tile_list_ckg_sig_kernel(
                 )
             slots[name] = ordered[:].rearrange("p t m b -> p (t m b)")
 
+        plane_of = {"nr": score_planes[:].bitcast(U8)[:, :N], "ni": score_planes[:].bitcast(U8)[:, N:]}
+
         def reorder_scales(name, plane, count):
             ordered = keep.tile([P, count, PACK, R // PACK], U8, name=name, align_bytes=64)
             nc.gpsimd.tensor_copy(
@@ -206,47 +205,43 @@ def tile_list_ckg_sig_kernel(
             )
             return ordered[:].rearrange("p w t m -> p (w t m)")
 
-        for name in POOL_LOADS:
-            for dst, src in named[name]:
-                nc.gpsimd.dma_start(out=dst, in_=src)
-        make_identity(nc, ident[:])
+        for dst, src in relation_rows[SYNC_ROWS:]:
+            nc.gpsimd.dma_start(out=dst, in_=src)
         for name in SYNC_LOADS:
             if name == "moves_r":
-                gather("scales_r", 0, CHUNKS, room_a[:])
-                move_rows("scales_r", 0, CHUNKS)
-            elif name == "moves_w_1":
-                spread_slots = reorder_scales("spread_slots", spread_w, 2).bitcast(I32)
-                nc.sync.dma_start(out=entity_planes[0:P:32, :], in_=spread_slots[0:P:32, :])
-            elif name == "moves_w_234":
-                for s in range(1, 4):
-                    nc.sync.dma_start(out=entity_planes[s:P:32, :], in_=spread_slots[8 * s : P : 32, :])
+                gather("scales_r", 0, 2, room_a[:, CHUNK:])
+                gather("scales_e", 0, 2, room_b[:])
+                gather("scales_r", 2, 1, room_a[:, :CHUNK])
+                move_rows("scales_r", 0, 2)
             elif name == "moves_e":
-                gather("scales_e", 0, 2, room_b[:].bitcast(U8)[:, : 2 * CHUNK])
-                gather("codes_r", 0, 1)
-                gather("codes_r", 2, 2)
-                gather("scales_e", 2, 2, room_a[:, : 2 * CHUNK])
-                gather("codes_e", 0, 1)
                 move_rows("scales_e", 0, 2)
-                move_rows("scales_e", 2, 2)
-                gather("codes_r", 1, 1, room_b[:])
+                gather("codes_r", 0, 1)
+                gather("codes_r", 1, 1)
+                gather("scales_r", 3, 1, room_a[:, CHUNK : 2 * CHUNK])
+                gather("codes_r", 2, 2)
+                gather("codes_e", 0, 1)
                 gather("codes_e", 1, 1)
+                spread["scales_r", 2] = room_a[:, : 2 * CHUNK]
+                move_rows("scales_r", 2, 2)
             else:
                 for dst, src in named[name]:
                     nc.sync.dma_start(out=dst, in_=src)
                 if name in ("wrr", "wri"):
                     reorder_words(name)
+                if name == "first_rows":
+                    shared_slots = reorder_scales("shared_slots", shared_plane, 1)
+                    plane_of["wrr"] = shared_slots[WRR_ROW:P, :]
+                    plane_of["wri"] = shared_slots[WRI_ROW:P, :]
+                    entity_slots = reorder_scales("entity_slots", spread_w, 2)
+                    for s in range(1, 4):
+                        rows = entity_slots.bitcast(I32)
+                        nc.gpsimd.dma_start(out=rows[s:P:32, :], in_=rows[8 * s : P : 32, :])
+                    plane_of["wer"] = entity_slots[:, :R]
+                    plane_of["wei"] = entity_slots[:, R:]
+                    make_identity(nc, ident[:], nomemset=True)
                 if name in ("wer", "wei"):
                     reorder_halves(name)
-        shared_slots = reorder_scales("shared_slots", shared_plane, 1)
-        plane_of = {
-            "wrr": shared_slots[WRR_ROW:P, :], "wri": shared_slots[WRI_ROW:P, :],
-            "wer": entity_planes[:].bitcast(U8)[:, :R], "wei": entity_planes[:].bitcast(U8)[:, R:],
-            "nr": score_planes[:].bitcast(U8)[:, :N], "ni": score_planes[:].bitcast(U8)[:, N:],
-        }
-
-        if DIRECT_E:
-            plane_of["wer"] = reorder_scales("wer_scale_slots", entity_planes[:, : R // 4], 1)
-            plane_of["wei"] = reorder_scales("wei_scale_slots", entity_planes[:, R // 4 :], 1)
+        whole["scales_e", 0] = room_b[:]
 
         def columns_of(name, first, count):
             if name in ("wrr", "wri"):
@@ -286,18 +281,17 @@ def tile_list_ckg_sig_kernel(
                 nc.scalar.copy(as_sums(i, rel[:, part]), sums[part])
             return rel
 
-        def entity(i):
-            aer = None if i in helped_tiles else project("entity", "e", i, "wer")
-            return aer, project("entity", "e", i, "wei")
+        def entity(i, ring="entity"):
+            aer = None if i in helped_tiles else project(ring, "e", i, "wer")
+            return aer, project(ring, "e", i, "wei")
 
         h_tiles = {}
         for first, count in SCORE_GROUPS:
-            h_tiles[first] = keep.tile([P, count * TILE * PACK], F32, name="h_%d" % first, align_bytes=64)
+            h_tiles[first] = keep.tile([P, 2, count * TILE, PACK], BF16, name="h_%d" % first, align_bytes=64)
 
         def rounded(i):
             first, count = [group for group in SCORE_GROUPS if group[0] <= i][-1]
-            view = h_tiles[first][:].bitcast(BF16).rearrange("p (h n t) -> p h n t", h=2, t=PACK)
-            return view[:, :, (i - first) * TILE : (i - first + 1) * TILE, :]
+            return h_tiles[first][:, :, (i - first) * TILE : (i - first + 1) * TILE, :]
 
         def real_room(i):
             if i in HOLD:
@@ -326,12 +320,15 @@ def tile_list_ckg_sig_kernel(
             imag = ring_tile("imag", [P, 2, R], IMAG_DEPTH)[:]
             if aer is not None:
                 real = real_room(i)
+            if aer is not None and not IMAG_FIRST:
                 both(i, real, aer, rel)
             if TWO_SUMS and i in channel_tiles:
                 both(i, imag, aei, rel)
             else:
                 nc.vector.scalar_tensor_tensor(as_sums(i, imag[:, 0]), aei, -1.0, as_sums(i, rel[:, 1]), MULT, MULT)
                 nc.vector.tensor_tensor(as_sums(i, imag[:, 1]), aei, as_sums(i, rel[:, 0]), MULT)
+            if aer is not None and IMAG_FIRST:
+                both(i, real, aer, rel)
             return real, imag
 
         def add_terms(i, prod):
@@ -359,7 +356,7 @@ def tile_list_ckg_sig_kernel(
             width = count * TILE
             h_codes = keep.tile([P, 2 * width], U32, name="h_codes_%d" % first, align_bytes=64)
             h_scales = keep.tile([P, 2 * width], U8, name="h_scales_%d" % first, align_bytes=64)
-            nc.vector.quantize_mx(out=h_codes[:].bitcast(FP8X4), scales=h_scales[:], in_=h_tiles[first][:].bitcast(BF16))
+            nc.vector.quantize_mx(out=h_codes[:].bitcast(FP8X4), scales=h_scales[:], in_=h_tiles[first][:].rearrange("p h n t -> p (h n t)"))
             h_packed[first] = (h_codes, h_scales)
 
         def score(first, count):
@@ -389,7 +386,7 @@ def tile_list_ckg_sig_kernel(
         rels = {i: relation(i) for i in range(RELATION_HEAD)}
         next_relation = RELATION_HEAD
         reals = {i: help_products(i, rels[i]) for i in range(HELP_AHEAD) if i in helped_tiles and HELP_FIRST}
-        ents = {i: entity(i) for i in range(ENTITY_AHEAD)}
+        ents = {i: entity(i, "for_scalar" if FOURTH and i == 0 else "entity") for i in range(ENTITY_AHEAD)}
         if not HELP_FIRST:
             reals = {i: help_products(i, rels[i]) for i in range(HELP_AHEAD) if i in helped_tiles}
         prods = {}
@@ -416,7 +413,9 @@ def tile_list_ckg_sig_kernel(
             if step - SUM_LAG in channel_tiles and KINDS[step - SUM_LAG] in "CE":
                 add_terms(step - SUM_LAG, prods[step - SUM_LAG])
             for name, chunk, count, old_name, old_chunk in [LATE[n] for n in range(len(LATE)) if LATE_STEPS[n] == step]:
-                gather(name, chunk, count, None if old_name is None else whole[old_name, old_chunk])
+                gather(name, chunk, count, whole[old_name, old_chunk])
+                if name in moved:
+                    move_rows(name, chunk, count)
             for n, group in enumerate(SCORE_GROUPS):
                 if QUANTISE_STEPS[n] == step:
                     quantise(*group)

@@ -46,16 +46,18 @@ SCORE_GROUPS = ((0, 4), (4, 4), (8, 4), (12, 2), (14, 1), (15, 1))
 QUANTISE_STEPS = (7, 11, 14, 16, 17, 18)
 SCORE_STEPS = (8, 12, 16, 17, 18, 19)
 RELATION_FROM = 1
-LATE_STEPS = (1,3,7)
-LATE = (("scales_e", 2, 2, "scales_e", 0), ("codes_e", 2, 1, "codes_e", 0), ("codes_e", 3, 1, "codes_e", 1))
-SYNC_LOADS = ("list_r", "list_e", "spread_r", "spread_e", "spread_w", "first_rows", "words_r", "wrr", "wri", "moves_r", "words_e", "wer", "wei", "moves_e", "nr", "ni", "nr_rows", "ni_rows")
-HALVES_ON = "G"
+LATE_STEPS = (5, 4)
+LATE = (("codes_r", 3, 1, "codes_r", 1), ("codes_e", 3, 1, "codes_e", 0))
+SYNC_LOADS = ("list_r", "list_e", "wer", "spread_r", "wei", "spread_e", "first_rows", "spread_w", "more_rows", "words_r", "wrr", "wri", "moves_r", "words_e", "moves_w", "moves_e", "nr", "ni", "nr_rows", "ni_rows")
+HALVES_ON = "S"
 POOL_LOADS = ()
 JOINT = 2
-SYNC_ROWS = 1
+SYNC_ROWS = 5
 FOURTH = True
 DIRECT_E = False
 HELP_FIRST = True
+LAST_IN_HEAD = False
+MOVES = (("scales_r", 0, 2), ("scales_e", 0, 4), ("scales_r", 2, 2))
 IMAG_FIRST = True
 ENTITY_AHEAD = 1
 WRR_ROW = 4
@@ -101,16 +103,14 @@ def tile_list_ckg_sig_kernel(
             nc.vector.memset(plane[:], 0)
             return plane
 
+        wrr_plane = zeroed_plane("wrr_plane", R)
         plane_r = zeroed_plane("plane_r", T)
         plane_e = zeroed_plane("plane_e", T)
+        wri_plane = zeroed_plane("wri_plane", R)
         spread_w = zeroed_plane("spread_w", 2 * R)
-        shared_plane = zeroed_plane("shared_plane", R)
         nc.vector.memset(warm[:, 0:1], 0.0)
         nc.scalar.activation(warm[:, 1:2], warm[:, 0:1], SIGMOID)
-        planes = zeroed_plane("planes", 2 * J + 2 * N)
-        moved_r = planes[:, : J // 4]
-        moved_e = planes[:, J // 4 : J // 2]
-        score_planes = planes[:, J // 2 :]
+        moved = {batch: zeroed_plane("moved_%s_%d" % batch[:2], batch[2] * CHUNK) for batch in MOVES}
         nc.vector.memset(ident[:], 0.0)
 
         def row_loads(plane, scales, first_row=0, first_column=0):
@@ -121,7 +121,7 @@ def tile_list_ckg_sig_kernel(
         def flat_words(words):
             return words[0].rearrange("p c i -> p (c i)")
 
-        relation_rows = row_loads(shared_plane, wri_scales, WRI_ROW) + row_loads(shared_plane, wrr_scales, WRR_ROW)
+        relation_rows = row_loads(wri_plane, wri_scales) + row_loads(wrr_plane, wrr_scales)
         raw = {}
         named = {
             "list_r": [(list_r[:], offs2)], "list_e": [(list_e[:], offs)],
@@ -133,16 +133,22 @@ def tile_list_ckg_sig_kernel(
                 (spread_w[0:P:8, n * R // 4 : (n + 1) * R // 4], scales[0].bitcast(I32))
                 for n, scales in enumerate((wer_scales, wei_scales))
             ],
-            "first_rows": relation_rows[:SYNC_ROWS],
-            "nr_rows": row_loads(score_planes, nr_scales),
-            "ni_rows": row_loads(score_planes, ni_scales, 0, N),
+            "first_rows": relation_rows[:4],
+            "more_rows": relation_rows[4:SYNC_ROWS],
         }
         for name, words in (
             ("wrr", flat_words(wrr_words)), ("wri", flat_words(wri_words)), ("wer", wer_words[0]),
-            ("wei", wei_words[0]), ("nr", nr_words[0]), ("ni", ni_words[0]),
+            ("wei", wei_words[0]),
         ):
             raw[name] = keep.tile([P, words.shape[1]], U8, name=name, align_bytes=64)
             named[name] = [(raw[name][:].bitcast(I32), words.bitcast(I32))]
+        raw["nr"] = raw["wri"][:, : 2 * N]
+        raw["ni"] = raw["wri"][:, 2 * N : 4 * N]
+        score_planes = raw["wri"][:, 4 * N : 6 * N].bitcast(I32)
+        named["nr"] = [(raw["nr"].bitcast(I32), nr_words[0].bitcast(I32))]
+        named["ni"] = [(raw["ni"].bitcast(I32), ni_words[0].bitcast(I32))]
+        named["nr_rows"] = row_loads(score_planes, nr_scales)
+        named["ni_rows"] = row_loads(score_planes, ni_scales, 0, N)
 
         sources = {
             "scales_r": (plane_r, list_r, U8), "codes_r": (words_r, list_r, U32),
@@ -150,10 +156,9 @@ def tile_list_ckg_sig_kernel(
         }
         picked = {}
         whole = {}
-        room_a = keep.tile([P, 3 * CHUNK], U8, name="room_a", align_bytes=64)
-        room_b = keep.tile([P, J // 2], U8, name="room_b", align_bytes=64)
+        room_a = keep.tile([P, J // 2], U8, name="room_a", align_bytes=64)
+        room_b = keep.tile([P, J], U8, name="room_b", align_bytes=64)
         spread = {}
-        moved = {"scales_r": moved_r, "scales_e": moved_e}
 
         def gather(name, chunk, count, into=None):
             window, offsets, dtype = sources[name]
@@ -167,11 +172,11 @@ def tile_list_ckg_sig_kernel(
                 picked[name, chunk + n] = into[:, n * CHUNK : (n + 1) * CHUNK]
 
         def move_rows(name, chunk, count):
-            columns = slice(chunk * CHUNK // 4, (chunk + count) * CHUNK // 4)
+            plane = moved[name, chunk, count]
             for s in range(4):
-                nc.sync.dma_start(out=moved[name][s:P:32, columns], in_=spread[name, chunk][8 * s : P : 32, :].bitcast(I32))
-            for n in range(chunk, chunk + count):
-                picked[name, n] = moved[name][:].bitcast(U8)[:, n * CHUNK : (n + 1) * CHUNK]
+                nc.sync.dma_start(out=plane[s:P:32, :], in_=spread[name, chunk][8 * s : P : 32, :].bitcast(I32))
+            for n in range(count):
+                picked[name, chunk + n] = plane[:].bitcast(U8)[:, n * CHUNK : (n + 1) * CHUNK]
 
         slots = {}
 
@@ -209,39 +214,40 @@ def tile_list_ckg_sig_kernel(
             nc.gpsimd.dma_start(out=dst, in_=src)
         for name in SYNC_LOADS:
             if name == "moves_r":
-                gather("scales_r", 0, 2, room_a[:, CHUNK:])
-                gather("scales_e", 0, 2, room_b[:])
-                gather("scales_r", 2, 1, room_a[:, :CHUNK])
+                gather("scales_r", 0, 2, room_a[:])
+                gather("scales_e", 0, CHUNKS, room_b[:])
                 move_rows("scales_r", 0, 2)
+            elif name == "moves_w":
+                rows = entity_slots.bitcast(I32)
+                for s in range(1, 4):
+                    nc.sync.dma_start(out=rows[s:P:32, :], in_=rows[8 * s : P : 32, :])
             elif name == "moves_e":
-                move_rows("scales_e", 0, 2)
+                move_rows("scales_e", 0, CHUNKS)
                 gather("codes_r", 0, 1)
                 gather("codes_r", 1, 1)
-                gather("scales_r", 3, 1, room_a[:, CHUNK : 2 * CHUNK])
-                gather("codes_r", 2, 2)
+                gather("scales_r", 2, 2, room_a[:])
+                gather("codes_r", 2, 1)
                 gather("codes_e", 0, 1)
-                gather("codes_e", 1, 1)
-                spread["scales_r", 2] = room_a[:, : 2 * CHUNK]
+                gather("codes_e", 1, 2)
+                if LAST_IN_HEAD:
+                    gather("codes_r", 3, 1, whole["codes_r", 0])
                 move_rows("scales_r", 2, 2)
             else:
                 for dst, src in named[name]:
                     nc.sync.dma_start(out=dst, in_=src)
                 if name in ("wrr", "wri"):
                     reorder_words(name)
-                if name == "first_rows":
-                    shared_slots = reorder_scales("shared_slots", shared_plane, 1)
-                    plane_of["wrr"] = shared_slots[WRR_ROW:P, :]
-                    plane_of["wri"] = shared_slots[WRI_ROW:P, :]
+                if name == "more_rows":
+                    plane_of["wrr"] = reorder_scales("wrr_scale_slots", wrr_plane, 1)
+                    plane_of["wri"] = reorder_scales("wri_scale_slots", wri_plane, 1)
                     entity_slots = reorder_scales("entity_slots", spread_w, 2)
-                    for s in range(1, 4):
-                        rows = entity_slots.bitcast(I32)
-                        nc.gpsimd.dma_start(out=rows[s:P:32, :], in_=rows[8 * s : P : 32, :])
                     plane_of["wer"] = entity_slots[:, :R]
                     plane_of["wei"] = entity_slots[:, R:]
                     make_identity(nc, ident[:], nomemset=True)
+                if name == "wri":
+                    nc.gpsimd.memset(score_planes, 0)
                 if name in ("wer", "wei"):
                     reorder_halves(name)
-        whole["scales_e", 0] = room_b[:]
 
         def columns_of(name, first, count):
             if name in ("wrr", "wri"):
@@ -414,7 +420,7 @@ def tile_list_ckg_sig_kernel(
                 add_terms(step - SUM_LAG, prods[step - SUM_LAG])
             for name, chunk, count, old_name, old_chunk in [LATE[n] for n in range(len(LATE)) if LATE_STEPS[n] == step]:
                 gather(name, chunk, count, whole[old_name, old_chunk])
-                if name in moved:
+                if name.startswith("scales"):
                     move_rows(name, chunk, count)
             for n, group in enumerate(SCORE_GROUPS):
                 if QUANTISE_STEPS[n] == step:

@@ -16,7 +16,6 @@ FP8X4 = mybir.dt.float8_e4m3fn_x4
 FP4X4 = mybir.dt.float4_e2m1fn_x4
 MULT = mybir.AluOpType.mult
 ADD = mybir.AluOpType.add
-SUBTRACT = mybir.AluOpType.subtract
 SIGMOID = mybir.ActivationFunctionType.Sigmoid
 
 P = 128
@@ -24,44 +23,25 @@ PACK = 4
 LINE = 16
 CHUNK = 512
 TILE = 128
-CHUNKS = J // CHUNK
 TILES = J // TILE
 TILES_PER_CHUNK = CHUNK // TILE
 
 KINDS = "BCBBCABCBBCABCAW"
-RELATION_HEAD = 5
+RELATION_AHEAD = 4
 RELATION_DEPTH = 6
 HELP_AHEAD = 3
-TURN_LAG = 1
-SUM_LAG = 0
-STEP_ORDER = "erps01"
+AER_DEPTH = 3
 REAL_DEPTH = 6
 IMAG_DEPTH = 6
-AER_DEPTH = 3
 SCALAR_BANKS = 4
 VECTOR_BANKS = 4
-TWO_SUMS = False
-HOLD = {}
-SCORE_GROUPS = ((0, 4), (4, 4), (8, 4), (12, 2), (14, 1), (15, 1))
+SUM_LAG = 0
+STEP_ORDER = "erpst"
+GROUPS = ((0, 4), (4, 4), (8, 4), (12, 2), (14, 1), (15, 1))
 QUANTISE_STEPS = (7, 11, 14, 16, 17, 18)
 SCORE_STEPS = (8, 12, 16, 17, 18, 19)
-RELATION_FROM = 1
-LATE_STEPS = (5, 4)
-LATE = (("codes_r", 3, 1, "codes_r", 1), ("codes_e", 3, 1, "codes_e", 0))
-SYNC_LOADS = ("list_r", "list_e", "wer", "spread_r", "wei", "spread_e", "first_rows", "spread_w", "more_rows", "words_r", "wrr", "wri", "moves_r", "words_e", "moves_w", "moves_e", "nr", "ni", "nr_rows", "ni_rows")
-HALVES_ON = "S"
-POOL_LOADS = ()
-JOINT = 2
-SYNC_ROWS = 5
-FOURTH = True
-DIRECT_E = False
-HELP_FIRST = True
-LAST_IN_HEAD = False
-MOVES = (("scales_r", 0, 2), ("scales_e", 0, 4), ("scales_r", 2, 2))
-IMAG_FIRST = True
-ENTITY_AHEAD = 1
-WRR_ROW = 4
-WRI_ROW = 8
+EARLY_ENTITY = 2
+LATE = ((2, ("r", 2, "e", 0)), (3, ("e", 2, "r", 1)), (6, ("r", 3, "e", 1)), (7, ("e", 3, "r", 2)))
 
 
 def tile_list_ckg_sig_kernel(
@@ -69,359 +49,331 @@ def tile_list_ckg_sig_kernel(
     wrr_words, wrr_scales, wri_words, wri_scales, nr_words, nr_scales, ni_words, ni_scales, offs, offs2, out,
 ):
     nc = tc.nc
-    channel_tiles = [i for i in range(TILES) if KINDS[i] in "CVWE"]
-    helped_tiles = [i for i in range(TILES) if KINDS[i] in "BWE"]
     with ExitStack() as ctx:
         keep = ctx.enter_context(tc.tile_pool(name="keep", bufs=1))
         psum = ctx.enter_context(tc.psum_pool(name="psum", bufs=1))
 
+        def sbuf(name, shape, dtype):
+            return keep.tile(shape, dtype, name=name, align_bytes=64)
+
         rings = {}
         uses = {}
 
-        def next_of(name, depth, make):
+        def ring(name, depth, make):
             if name not in rings:
                 rings[name] = [make("%s_%d" % (name, n)) for n in range(depth)]
             uses[name] = uses.get(name, -1) + 1
             return rings[name][uses[name] % depth]
 
-        def ring_tile(name, shape, depth):
-            return next_of(name, depth, lambda label: keep.tile(shape, F32, name=label, align_bytes=64))
+        def float_room(name, shape, depth):
+            return ring(name, depth, lambda label: sbuf(label, shape, F32))[:]
 
-        def bank(name):
-            depth = SCALAR_BANKS if name == "for_scalar" else VECTOR_BANKS
-            return next_of(name, depth, lambda label: psum.tile([P, CHUNK], F32, name=label))
+        def bank(reader):
+            depth = SCALAR_BANKS if reader == "scalar" else VECTOR_BANKS
+            return ring(reader, depth, lambda label: psum.tile([P, CHUNK], F32, name=label))[:]
 
-        list_e = keep.tile([P, J // 16], U16, name="list_e")
-        list_r = keep.tile([P, J // 16], U16, name="list_r")
-        words_e = keep.tile([P, T], I32, name="words_e", align_bytes=64)
-        words_r = keep.tile([P, T], I32, name="words_r", align_bytes=64)
-        ident = keep.tile([P, P], F32, name="ident", align_bytes=64)
-        warm = keep.tile([P, 2], F32, name="warm")
-
-        def zeroed_plane(name, columns):
-            plane = keep.tile([P, columns // 4], I32, name=name, align_bytes=64)
-            nc.vector.memset(plane[:], 0)
+        def zeroed(engine, name, columns):
+            plane = sbuf(name, [P, columns // 4], I32)
+            engine.memset(plane[:], 0)
             return plane
-
-        wrr_plane = zeroed_plane("wrr_plane", R)
-        plane_r = zeroed_plane("plane_r", T)
-        plane_e = zeroed_plane("plane_e", T)
-        wri_plane = zeroed_plane("wri_plane", R)
-        spread_w = zeroed_plane("spread_w", 2 * R)
-        nc.vector.memset(warm[:, 0:1], 0.0)
-        nc.scalar.activation(warm[:, 1:2], warm[:, 0:1], SIGMOID)
-        moved = {batch: zeroed_plane("moved_%s_%d" % batch[:2], batch[2] * CHUNK) for batch in MOVES}
-        nc.vector.memset(ident[:], 0.0)
-
-        def row_loads(plane, scales, first_row=0, first_column=0):
-            rows = scales[0].bitcast(I32)
-            columns = slice(first_column // 4, first_column // 4 + rows.shape[1])
-            return [(plane[first_row + s : P : 32, columns], rows[s:16:4, :]) for s in range(4)]
 
         def flat_words(words):
             return words[0].rearrange("p c i -> p (c i)")
 
-        relation_rows = row_loads(wri_plane, wri_scales) + row_loads(wrr_plane, wrr_scales)
+        def load_bytes(queue, name, source):
+            tile = sbuf(name, [P, source.shape[1]], U8)
+            queue.dma_start(out=tile[:].bitcast(I32), in_=source.bitcast(I32))
+            return tile[:]
+
+        def load_spread(queue, plane, first_column, scales):
+            rows = scales[0].bitcast(I32)
+            queue.dma_start(out=plane[0:P:8, first_column // 4 : first_column // 4 + rows.shape[1]], in_=rows)
+
+        def move_rows(queue, plane, spread, first_row):
+            for s in range(first_row, 4):
+                queue.dma_start(out=plane[s:P:32, :], in_=spread[8 * s : P : 32, :])
+
+        list_r = keep.tile([P, J // 16], U16, name="list_r")
+        list_e = keep.tile([P, J // 16], U16, name="list_e")
+        table_r = sbuf("table_r", [P, T], I32)
+        ident = sbuf("ident", [P, P], F32)
+        warm = keep.tile([P, 2], F32, name="warm")
+
+        plane_r = sbuf("plane_r", [P, T // 4], I32)
+        rows_e = sbuf("rows_e", [P, T // 4], I32)
+        for window in (rows_e, plane_r):
+            nc.gpsimd.memset(window[:, : T // 8], 0)
+            nc.vector.memset(window[:, T // 8 :], 0)
+        rows_we = zeroed(nc.vector, "rows_we", 2 * R)
+        rows_wri = keep.tile([P, R // 4], I32, name="rows_wri", tag="entity_table", align_bytes=64)
+        nc.vector.memset(rows_wri[:], 0)
+        nc.vector.memset(warm[:, 0:1], 0.0)
+
         raw = {}
-        named = {
-            "list_r": [(list_r[:], offs2)], "list_e": [(list_e[:], offs)],
-            "spread_r": [(plane_r[0:P:8, :], tab2_scales[0].bitcast(I32))],
-            "spread_e": [(plane_e[0:P:8, :], tab_scales[0].bitcast(I32))],
-            "words_r": [(words_r[:], flat_words(tab2_words).bitcast(I32))],
-            "words_e": [(words_e[:], flat_words(tab_words).bitcast(I32))],
-            "spread_w": [
-                (spread_w[0:P:8, n * R // 4 : (n + 1) * R // 4], scales[0].bitcast(I32))
-                for n, scales in enumerate((wer_scales, wei_scales))
-            ],
-            "first_rows": relation_rows[:4],
-            "more_rows": relation_rows[4:SYNC_ROWS],
-        }
-        for name, words in (
-            ("wrr", flat_words(wrr_words)), ("wri", flat_words(wri_words)), ("wer", wer_words[0]),
-            ("wei", wei_words[0]),
-        ):
-            raw[name] = keep.tile([P, words.shape[1]], U8, name=name, align_bytes=64)
-            named[name] = [(raw[name][:].bitcast(I32), words.bitcast(I32))]
-        raw["nr"] = raw["wri"][:, : 2 * N]
-        raw["ni"] = raw["wri"][:, 2 * N : 4 * N]
-        score_planes = raw["wri"][:, 4 * N : 6 * N].bitcast(I32)
-        named["nr"] = [(raw["nr"].bitcast(I32), nr_words[0].bitcast(I32))]
-        named["ni"] = [(raw["ni"].bitcast(I32), ni_words[0].bitcast(I32))]
-        named["nr_rows"] = row_loads(score_planes, nr_scales)
-        named["ni_rows"] = row_loads(score_planes, ni_scales, 0, N)
-
-        sources = {
-            "scales_r": (plane_r, list_r, U8), "codes_r": (words_r, list_r, U32),
-            "scales_e": (plane_e, list_e, U8), "codes_e": (words_e, list_e, U32),
-        }
-        picked = {}
-        whole = {}
-        room_a = keep.tile([P, J // 2], U8, name="room_a", align_bytes=64)
-        room_b = keep.tile([P, J], U8, name="room_b", align_bytes=64)
-        spread = {}
-
-        def gather(name, chunk, count, into=None):
-            window, offsets, dtype = sources[name]
-            spread[name, chunk] = into
-            if into is None:
-                into = keep.tile([P, count * CHUNK], dtype, name="%s_%d" % (name, chunk), align_bytes=64)[:]
-                whole[name, chunk] = into
-            columns = slice(chunk * CHUNK // 16, (chunk + count) * CHUNK // 16)
-            nc.vector.tensor_copy(into, window[:].bitcast(dtype).indirect(offsets[:, columns]))
-            for n in range(count):
-                picked[name, chunk + n] = into[:, n * CHUNK : (n + 1) * CHUNK]
-
-        def move_rows(name, chunk, count):
-            plane = moved[name, chunk, count]
-            for s in range(4):
-                nc.sync.dma_start(out=plane[s:P:32, :], in_=spread[name, chunk][8 * s : P : 32, :].bitcast(I32))
-            for n in range(count):
-                picked[name, chunk + n] = plane[:].bitcast(U8)[:, n * CHUNK : (n + 1) * CHUNK]
+        nc.sync.dma_start(out=list_r[:], in_=offs2)
+        nc.sync.dma_start(out=list_e[:], in_=offs)
+        raw["wrr"] = load_bytes(nc.scalar, "wrr", flat_words(wrr_words))
+        load_spread(nc.scalar, rows_we, 0, wrr_scales)
+        load_spread(nc.scalar, rows_wri, 0, wri_scales)
+        load_spread(nc.sync, rows_e, 0, tab_scales)
+        for s in range(4):
+            nc.sync.dma_start(out=plane_r[s:P:32, :], in_=tab2_scales[0].bitcast(I32)[s:16:4, :])
+        nc.sync.dma_start(out=table_r[:], in_=flat_words(tab2_words).bitcast(I32))
+        nc.scalar.activation(warm[:, 1:2], warm[:, 0:1], SIGMOID)
 
         slots = {}
+        plane_of = {}
 
-        def reorder_words(name):
-            ordered = keep.tile([P, PACK, R // PACK], U32, name=name + "_slots", align_bytes=64)
+        def reorder_words(name, dtype, run):
+            ordered = sbuf(name + "_slots", [P, R], dtype)
             nc.scalar.copy(
-                ordered[:].rearrange("p t (c i) -> p c t i", i=PACK),
-                raw[name][:].bitcast(U32).rearrange("p (c i t) -> p c t i", i=PACK, t=PACK),
+                ordered[:].rearrange("p (t c i) -> p c t i", t=PACK, i=run),
+                raw[name].bitcast(dtype).rearrange("p (c i t) -> p c t i", i=run, t=PACK),
             )
-            slots[name] = ordered[:].rearrange("p t m -> p (t m)").bitcast(FP8X4)
+            slots[name] = ordered[:].bitcast(U8)
 
-        def reorder_halves(name):
-            ordered = keep.tile([P, PACK, R // PACK, 2], U8, name=name + "_slots", align_bytes=64)
-            if HALVES_ON == "G":
-                nc.gpsimd.tensor_copy(ordered[:], raw[name][:].rearrange("p (m t b) -> p t m b", t=PACK, b=2))
-            else:
-                engine = nc.scalar.copy if HALVES_ON == "S" else nc.vector.tensor_copy
-                engine(
-                    ordered[:].rearrange("p t m b -> p (t m b)").bitcast(U16).rearrange("p (t c i) -> p c t i", t=PACK, i=8),
-                    raw[name][:].bitcast(U16).rearrange("p (c i t) -> p c t i", i=8, t=PACK),
-                )
-            slots[name] = ordered[:].rearrange("p t m b -> p (t m b)")
-
-        plane_of = {"nr": score_planes[:].bitcast(U8)[:, :N], "ni": score_planes[:].bitcast(U8)[:, N:]}
-
-        def reorder_scales(name, plane, count):
-            ordered = keep.tile([P, count, PACK, R // PACK], U8, name=name, align_bytes=64)
+        def reorder_scales(planes, rows, names):
             nc.gpsimd.tensor_copy(
-                ordered[:].rearrange("p w t (c i) -> p w c t i", i=LINE),
-                plane[:].bitcast(U8).rearrange("p (w c i t) -> p w c t i", w=count, i=LINE, t=PACK),
+                planes.rearrange("p (w t c i) -> p w c t i", w=len(names), t=PACK, i=LINE),
+                rows.bitcast(U8).rearrange("p (w c i t) -> p w c t i", w=len(names), i=LINE, t=PACK),
             )
-            return ordered[:].rearrange("p w t m -> p (w t m)")
+            for n, name in enumerate(names):
+                plane_of[name] = planes[:, n * R : (n + 1) * R]
 
-        for dst, src in relation_rows[SYNC_ROWS:]:
-            nc.gpsimd.dma_start(out=dst, in_=src)
-        for name in SYNC_LOADS:
-            if name == "moves_r":
-                gather("scales_r", 0, 2, room_a[:])
-                gather("scales_e", 0, CHUNKS, room_b[:])
-                move_rows("scales_r", 0, 2)
-            elif name == "moves_w":
-                rows = entity_slots.bitcast(I32)
-                for s in range(1, 4):
-                    nc.sync.dma_start(out=rows[s:P:32, :], in_=rows[8 * s : P : 32, :])
-            elif name == "moves_e":
-                move_rows("scales_e", 0, CHUNKS)
-                gather("codes_r", 0, 1)
-                gather("codes_r", 1, 1)
-                gather("scales_r", 2, 2, room_a[:])
-                gather("codes_r", 2, 1)
-                gather("codes_e", 0, 1)
-                gather("codes_e", 1, 2)
-                if LAST_IN_HEAD:
-                    gather("codes_r", 3, 1, whole["codes_r", 0])
-                move_rows("scales_r", 2, 2)
-            else:
-                for dst, src in named[name]:
-                    nc.sync.dma_start(out=dst, in_=src)
-                if name in ("wrr", "wri"):
-                    reorder_words(name)
-                if name == "more_rows":
-                    plane_of["wrr"] = reorder_scales("wrr_scale_slots", wrr_plane, 1)
-                    plane_of["wri"] = reorder_scales("wri_scale_slots", wri_plane, 1)
-                    entity_slots = reorder_scales("entity_slots", spread_w, 2)
-                    plane_of["wer"] = entity_slots[:, :R]
-                    plane_of["wei"] = entity_slots[:, R:]
-                    make_identity(nc, ident[:], nomemset=True)
-                if name == "wri":
-                    nc.gpsimd.memset(score_planes, 0)
-                if name in ("wer", "wei"):
-                    reorder_halves(name)
+        reorder_words("wrr", U32, 4)
+        planes_wr = sbuf("planes_wr", [P, 2 * R], U8)
+        planes_we = sbuf("planes_we", [P, 2 * R], U8)
+        reorder_scales(planes_wr[:, :R], rows_we[:, : R // 4], ("wrr",))
+        reorder_scales(planes_wr[:, R:], rows_wri[:], ("wri",))
+        load_spread(nc.gpsimd, rows_we, R, wei_scales)
+        load_spread(nc.gpsimd, rows_we, 0, wer_scales)
+        reorder_scales(planes_we[:], rows_we[:], ("wer", "wei"))
+        plane_e01 = zeroed(nc.gpsimd, "plane_e01", 2 * CHUNK)
+        plane_e23 = zeroed(nc.gpsimd, "plane_e23", 2 * CHUNK)
+        plane_n = zeroed(nc.gpsimd, "plane_n", 2 * N)
+        make_identity(nc, ident[:])
+        plane_of["nr"] = plane_n[:].bitcast(U8)[:, :N]
+        plane_of["ni"] = plane_n[:].bitcast(U8)[:, N:]
+
+        def gather(into, window, offsets, chunk, count):
+            columns = slice(chunk * CHUNK // 16, (chunk + count) * CHUNK // 16)
+            nc.vector.tensor_copy(into, window[:].bitcast(into.dtype).indirect(offsets[:, columns]))
+
+        codes = {}
+        scales = {}
+
+        def gather_words(side, chunk, into):
+            gather(into, table_r if side == "r" else table_e, list_r if side == "r" else list_e, chunk, 1)
+            codes[side, chunk] = into
+
+        def name_scales(plane, side, first, count):
+            for n in range(count):
+                scales[side, first + n] = plane[:].bitcast(U8)[:, n * CHUNK : (n + 1) * CHUNK]
+
+        def word_room(name):
+            return sbuf(name, [P, CHUNK], U32)[:]
+
+        move_rows(nc.sync, planes_wr[:].bitcast(I32), planes_wr[:].bitcast(I32), 1)
+        raw["wri"] = keep.tile([P, 4 * R], U8, name="wri", tag="wri", align_bytes=64)[:]
+        nc.sync.dma_start(out=raw["wri"].bitcast(I32), in_=flat_words(wri_words).bitcast(I32))
+        raw["wer"] = load_bytes(nc.sync, "wer", wer_words[0])
+        raw["wei"] = load_bytes(nc.sync, "wei", wei_words[0])
+        table_e = keep.tile([P, T], I32, name="table_e", tag="entity_table", align_bytes=64)
+        nc.sync.dma_start(out=table_e[:], in_=flat_words(tab_words).bitcast(I32))
+        move_rows(nc.sync, planes_we[:].bitcast(I32), planes_we[:].bitcast(I32), 1)
+        reorder_words("wri", U32, 4)
+
+        room_e = keep.tile([P, 2 * CHUNK], U8, name="room_e", tag="room_e", align_bytes=64)
+        gather(room_e[:], rows_e, list_e, 0, 2)
+        picked_r = sbuf("picked_r", [P, 3 * CHUNK], U8)
+        gather(picked_r[:], plane_r, list_r, 0, 3)
+        name_scales(picked_r, "r", 0, 3)
+        gather_words("r", 0, word_room("codes_r0"))
+        move_rows(nc.sync, plane_e01, room_e[:].bitcast(I32), 0)
+        name_scales(plane_e01, "e", 0, 2)
+        room_late = keep.tile([P, 3 * CHUNK], U8, name="room_late", tag="wri", align_bytes=64)
+        gather(room_late[:, : 2 * CHUNK], rows_e, list_e, 2, 2)
+        gather(room_late[:, 2 * CHUNK :], plane_r, list_r, 3, 1)
+        scales["r", 3] = room_late[:, 2 * CHUNK :]
+        move_rows(nc.sync, plane_e23, room_late[:, : 2 * CHUNK].bitcast(I32), 0)
+        name_scales(plane_e23, "e", 2, 2)
+        for name in ("wer", "wei"):
+            ordered = sbuf(name + "_slots", [P, PACK, R // PACK, 2], U8)
+            nc.gpsimd.tensor_copy(ordered[:], raw[name].rearrange("p (m t b) -> p t m b", t=PACK, b=2))
+            slots[name] = ordered[:].rearrange("p t m b -> p (t m b)")
+        for chunk in range(EARLY_ENTITY):
+            gather_words("e", chunk, word_room("codes_e%d" % chunk))
+        gather_words("r", 1, keep.tile([P, CHUNK], U32, name="codes_r1", tag="room_e", align_bytes=64)[:])
+        raw["nr"] = load_bytes(nc.sync, "nr", nr_words[0])
+        raw["ni"] = load_bytes(nc.sync, "ni", ni_words[0])
+        for n, source in enumerate((nr_scales, ni_scales)):
+            for s in range(4):
+                nc.sync.dma_start(
+                    out=plane_n[s:P:32, n * N // 4 : (n + 1) * N // 4], in_=source[0].bitcast(I32)[s:16:4, :]
+                )
+
+        def late_gather(what):
+            side, chunk, old_side, old_chunk = what
+            gather_words(side, chunk, codes[old_side, old_chunk])
 
         def columns_of(name, first, count):
             if name in ("wrr", "wri"):
-                return slots[name][:, first : first + count]
+                return slots[name][:, 4 * first : 4 * (first + count)].bitcast(FP8X4)
             return slots[name][:, 2 * first : 2 * (first + count)].bitcast(FP4X4)
 
-        def project(ring, side, i, name):
+        def by_channel(i):
+            return KINDS[i] in "CVW"
+
+        def helped(i):
+            return KINDS[i] in "BW"
+
+        def project(reader, name, i):
+            side = name[1]
             chunk, place = divmod(i, TILES_PER_CHUNK)
             tokens = slice(place * TILE, (place + 1) * TILE)
-            codes = picked["codes_" + side, chunk][:, tokens].bitcast(FP8X4)
-            scales = picked["scales_" + side, chunk][:, tokens]
-            acc = bank(ring)
-            if i in channel_tiles:
-                by_slot = acc[:].rearrange("p (t n) -> p t n", t=PACK)
+            words = codes[side, chunk][:, tokens].bitcast(FP8X4)
+            plane = scales[side, chunk][:, tokens]
+            acc = bank(reader)
+            if by_channel(i):
+                by_slot = acc.rearrange("p (t n) -> p t n", t=PACK)
                 for t in range(PACK):
                     nc.tensor.matmul_mx(
                         out=by_slot[:, t, :], lhsT=columns_of(name, t * P, P),
                         lhsT_scale=plane_of[name][:, t * P : (t + 1) * P],
-                        rhs=codes, rhs_scale=scales, start=True, stop=True,
+                        rhs=words, rhs_scale=plane, start=True, stop=True,
                     )
                 return by_slot.rearrange("p t n -> p n t")
             nc.tensor.matmul_mx(
-                out=acc[:], lhsT=codes, lhsT_scale=scales,
+                out=acc, lhsT=words, lhsT_scale=plane,
                 rhs=columns_of(name, 0, R), rhs_scale=plane_of[name], start=True, stop=True,
             )
-            return acc[:]
+            return acc
 
-        def as_sums(i, flat):
-            if i in channel_tiles:
-                return flat.rearrange("p (n t) -> p n t", t=PACK)
-            return flat
+        def like_sums(i, flat):
+            return flat.rearrange("p (n t) -> p n t", t=PACK) if by_channel(i) else flat
+
+        rel = {}
+        real = {}
+        imag = {}
+        sums = {}
 
         def relation(i):
-            rel = ring_tile("rel", [P, 2, R], RELATION_DEPTH)
-            sums = [project("for_scalar", "r", i, name) for name in ("wrr", "wri")]
-            for part in range(2):
-                nc.scalar.copy(as_sums(i, rel[:, part]), sums[part])
-            return rel
+            rel[i] = float_room("rel", [P, 2, R], RELATION_DEPTH)
+            for part, name in enumerate(("wrr", "wri")):
+                nc.scalar.copy(like_sums(i, rel[i][:, part]), project("scalar", name, i))
 
-        def entity(i, ring="entity"):
-            aer = None if i in helped_tiles else project(ring, "e", i, "wer")
-            return aer, project(ring, "e", i, "wei")
+        def help_real(i):
+            aer = float_room("aer", [P, R], AER_DEPTH)
+            nc.scalar.copy(like_sums(i, aer), project("scalar", "wer", i))
+            real[i] = float_room("real", [P, 2, R], REAL_DEPTH)
+            nc.gpsimd.tensor_tensor(real[i], aer.unsqueeze(1).broadcast_to([P, 2, R]), rel[i], MULT)
 
-        h_tiles = {}
-        for first, count in SCORE_GROUPS:
-            h_tiles[first] = keep.tile([P, 2, count * TILE, PACK], BF16, name="h_%d" % first, align_bytes=64)
+        def entity(i):
+            sums[i, "wei"] = project("vector", "wei", i)
+            if not helped(i):
+                sums[i, "wer"] = project("vector", "wer", i)
 
-        def rounded(i):
-            first, count = [group for group in SCORE_GROUPS if group[0] <= i][-1]
-            return h_tiles[first][:, :, (i - first) * TILE : (i - first + 1) * TILE, :]
-
-        def real_room(i):
-            if i in HOLD:
-                first, half = HOLD[i]
-                return h_tiles[first][:, half * 2 * R : (half + 1) * 2 * R].rearrange("p (h r) -> p h r", h=2)
-            return ring_tile("real", [P, 2, R], REAL_DEPTH)[:]
-
-        def help_products(i, rel):
-            aer_copy = ring_tile("aer_copy", [P, R], AER_DEPTH)
-            nc.scalar.copy(as_sums(i, aer_copy[:]), project("for_scalar", "e", i, "wer"))
-            real = real_room(i)
-            nc.gpsimd.tensor_tensor(real, aer_copy[:].unsqueeze(1).broadcast_to([P, 2, R]), rel[:], MULT)
-            return real
-
-        def both(i, target, acc, rel):
-            if i in channel_tiles:
+        def products(i):
+            imag[i] = float_room("imag", [P, 2, R], IMAG_DEPTH)
+            aei = sums[i, "wei"]
+            nc.vector.scalar_tensor_tensor(like_sums(i, imag[i][:, 0]), aei, -1.0, like_sums(i, rel[i][:, 1]), MULT, MULT)
+            nc.vector.tensor_tensor(like_sums(i, imag[i][:, 1]), aei, like_sums(i, rel[i][:, 0]), MULT)
+            if helped(i):
+                return
+            real[i] = float_room("real", [P, 2, R], REAL_DEPTH)
+            aer = sums[i, "wer"]
+            if by_channel(i):
                 nc.vector.tensor_tensor(
-                    target.rearrange("p h (n t) -> p h n t", t=PACK),
-                    acc.unsqueeze(1).broadcast_to([P, 2, TILE, PACK]),
-                    rel[:].rearrange("p h (n t) -> p h n t", t=PACK), MULT,
+                    real[i].rearrange("p h (n t) -> p h n t", t=PACK),
+                    aer.unsqueeze(1).broadcast_to([P, 2, TILE, PACK]),
+                    rel[i].rearrange("p h (n t) -> p h n t", t=PACK), MULT,
                 )
             else:
-                nc.vector.tensor_tensor(target, acc.unsqueeze(1).broadcast_to([P, 2, R]), rel[:], MULT)
+                nc.vector.tensor_tensor(real[i], aer.unsqueeze(1).broadcast_to([P, 2, R]), rel[i], MULT)
 
-        def products(i, rel, aer, aei, real):
-            imag = ring_tile("imag", [P, 2, R], IMAG_DEPTH)[:]
-            if aer is not None:
-                real = real_room(i)
-            if aer is not None and not IMAG_FIRST:
-                both(i, real, aer, rel)
-            if TWO_SUMS and i in channel_tiles:
-                both(i, imag, aei, rel)
-            else:
-                nc.vector.scalar_tensor_tensor(as_sums(i, imag[:, 0]), aei, -1.0, as_sums(i, rel[:, 1]), MULT, MULT)
-                nc.vector.tensor_tensor(as_sums(i, imag[:, 1]), aei, as_sums(i, rel[:, 0]), MULT)
-            if aer is not None and IMAG_FIRST:
-                both(i, real, aer, rel)
-            return real, imag
+        rounded = {first: sbuf("h_%d" % first, [P, 2, count * TILE, PACK], BF16) for first, count in GROUPS}
 
-        def add_terms(i, prod):
-            flat = rounded(i).rearrange("p h n t -> p h (n t)")
-            engine = nc.vector if KINDS[i] in "VW" else nc.gpsimd
-            if TWO_SUMS:
-                engine.tensor_tensor(flat[:, 0], prod[0][:, 0], prod[1][:, 1], SUBTRACT)
-                engine.tensor_tensor(flat[:, 1], prod[0][:, 1], prod[1][:, 0], ADD)
-            else:
-                engine.tensor_tensor(flat, prod[0], prod[1], ADD)
+        def rounded_of(i):
+            first = [group[0] for group in GROUPS if group[0] <= i][-1]
+            return rounded[first][:, :, (i - first) * TILE : (i - first + 1) * TILE, :]
 
-        def turn(i, prod, part):
-            acc = bank("for_scalar")[:].rearrange("p (t n) -> p t n", t=PACK)
-            for term in range(2):
-                for t in range(PACK):
-                    nc.tensor.matmul(
-                        acc[:, t, :], lhsT=prod[term][:, part, t * P : (t + 1) * P], rhs=ident[:],
-                        start=(term == 0 and t == 0), stop=(term == 1 and t == PACK - 1), is_transpose=True,
-                    )
-            nc.scalar.copy(rounded(i)[:, part], acc.rearrange("p t n -> p n t"))
+        def add_terms(engine, i):
+            engine.tensor_tensor(rounded_of(i).rearrange("p h n t -> p h (n t)"), real[i], imag[i], ADD)
 
-        h_packed = {}
+        def turn(i):
+            for part in range(2):
+                acc = bank("scalar").rearrange("p (t n) -> p t n", t=PACK)
+                for term, prod in enumerate((real[i], imag[i])):
+                    for t in range(PACK):
+                        nc.tensor.matmul(
+                            acc[:, t, :], lhsT=prod[:, part, t * P : (t + 1) * P], rhs=ident[:],
+                            start=(term == 0 and t == 0), stop=(term == 1 and t == PACK - 1), is_transpose=True,
+                        )
+                nc.scalar.copy(rounded_of(i)[:, part], acc.rearrange("p t n -> p n t"))
+
+        packed = {}
 
         def quantise(first, count):
             width = count * TILE
-            h_codes = keep.tile([P, 2 * width], U32, name="h_codes_%d" % first, align_bytes=64)
-            h_scales = keep.tile([P, 2 * width], U8, name="h_scales_%d" % first, align_bytes=64)
-            nc.vector.quantize_mx(out=h_codes[:].bitcast(FP8X4), scales=h_scales[:], in_=h_tiles[first][:].rearrange("p h n t -> p (h n t)"))
-            h_packed[first] = (h_codes, h_scales)
+            h_codes = sbuf("h_codes_%d" % first, [P, 2 * width], U32)
+            h_scales = sbuf("h_scales_%d" % first, [P, 2 * width], U8)
+            nc.vector.quantize_mx(
+                out=h_codes[:].bitcast(FP8X4), scales=h_scales[:],
+                in_=rounded[first][:].rearrange("p h n t -> p (h n t)"),
+            )
+            packed[first] = (h_codes, h_scales)
 
         def score(first, count):
             width = count * TILE
-            h_codes, h_scales = h_packed[first]
+            h_codes, h_scales = packed[first]
             per_bank = min(2, CHUNK // width)
-            span = CHUNK if width == CHUNK else TILE
             for n in range(2 // per_bank):
-                acc = bank("for_scalar")[:, : per_bank * width].rearrange("p (h w) -> p h w", h=per_bank)
+                acc = bank("scalar")[:, : per_bank * width].rearrange("p (h w) -> p h w", h=per_bank)
                 for place in range(per_bank):
                     half = n * per_bank + place
-                    for begin in range(0, width, span):
-                        for part, name in enumerate(("nr", "ni")):
-                            tokens = slice(part * width + begin, part * width + begin + span)
-                            nc.tensor.matmul_mx(
-                                out=acc[:, place, begin : begin + span],
-                                lhsT=raw[name][:, 2 * P * half : 2 * P * (half + 1)].bitcast(FP4X4),
-                                lhsT_scale=plane_of[name][:, P * half : P * (half + 1)],
-                                rhs=h_codes[:, tokens].bitcast(FP8X4), rhs_scale=h_scales[:, tokens],
-                                start=(part == 0), stop=(part == 1),
-                            )
-                result = keep.tile([P, per_bank, width], F32, name="result_%d_%d" % (first, n))
+                    for part, name in enumerate(("nr", "ni")):
+                        tokens = slice(part * width, (part + 1) * width)
+                        nc.tensor.matmul_mx(
+                            out=acc[:, place, :],
+                            lhsT=raw[name][:, 2 * P * half : 2 * P * (half + 1)].bitcast(FP4X4),
+                            lhsT_scale=plane_of[name][:, P * half : P * (half + 1)],
+                            rhs=h_codes[:, tokens].bitcast(FP8X4), rhs_scale=h_scales[:, tokens],
+                            start=(part == 0), stop=(part == 1),
+                        )
+                result = sbuf("result_%d_%d" % (first, n), [P, per_bank, width], F32)
                 nc.scalar.activation(result[:], acc, SIGMOID)
                 rows = out[P * n * per_bank : P * (n + 1) * per_bank, first * TILE : first * TILE + width]
                 nc.sync.dma_start(out=rows.rearrange("(h p) n -> p h n", p=P), in_=result[:])
 
-        rels = {i: relation(i) for i in range(RELATION_HEAD)}
-        next_relation = RELATION_HEAD
-        reals = {i: help_products(i, rels[i]) for i in range(HELP_AHEAD) if i in helped_tiles and HELP_FIRST}
-        ents = {i: entity(i, "for_scalar" if FOURTH and i == 0 else "entity") for i in range(ENTITY_AHEAD)}
-        if not HELP_FIRST:
-            reals = {i: help_products(i, rels[i]) for i in range(HELP_AHEAD) if i in helped_tiles}
-        prods = {}
+        for i in range(RELATION_AHEAD):
+            relation(i)
+        for i in range(HELP_AHEAD):
+            if helped(i):
+                help_real(i)
+        entity(0)
         for step in range(max(SCORE_STEPS) + 1):
-            turned = step - TURN_LAG
             for part in STEP_ORDER:
-                if part in "01" and 0 <= turned < TILES and turned not in channel_tiles:
-                    turn(turned, prods[turned], int(part))
-                if part == "e" and step + ENTITY_AHEAD < TILES:
-                    ents[step + ENTITY_AHEAD] = entity(step + ENTITY_AHEAD)
-                if part == "r" and step >= RELATION_FROM and next_relation < TILES:
-                    rels[next_relation] = relation(next_relation)
-                    next_relation = next_relation + 1
-                if part == "p" and step + HELP_AHEAD in helped_tiles:
-                    reals[step + HELP_AHEAD] = help_products(step + HELP_AHEAD, rels[step + HELP_AHEAD])
+                if part == "e" and step + 1 < TILES:
+                    entity(step + 1)
+                if part == "r" and step + RELATION_AHEAD < TILES:
+                    relation(step + RELATION_AHEAD)
+                if part == "p" and step + HELP_AHEAD < TILES and helped(step + HELP_AHEAD):
+                    help_real(step + HELP_AHEAD)
                 if part == "s":
-                    for n, group in enumerate(SCORE_GROUPS):
+                    for n, group in enumerate(GROUPS):
                         if SCORE_STEPS[n] == step:
                             score(*group)
+                if part == "t" and 1 <= step <= TILES and not by_channel(step - 1):
+                    turn(step - 1)
             if step < TILES:
-                prods[step] = products(step, rels[step], ents[step][0], ents[step][1], reals.get(step))
-            if step < TILES and KINDS[step] in "VW":
-                add_terms(step, prods[step])
-            if step - SUM_LAG in channel_tiles and KINDS[step - SUM_LAG] in "CE":
-                add_terms(step - SUM_LAG, prods[step - SUM_LAG])
-            for name, chunk, count, old_name, old_chunk in [LATE[n] for n in range(len(LATE)) if LATE_STEPS[n] == step]:
-                gather(name, chunk, count, whole[old_name, old_chunk])
-                if name.startswith("scales"):
-                    move_rows(name, chunk, count)
-            for n, group in enumerate(SCORE_GROUPS):
+                products(step)
+                if KINDS[step] in "VW":
+                    add_terms(nc.vector, step)
+            if 0 <= step - SUM_LAG < TILES and KINDS[step - SUM_LAG] == "C":
+                add_terms(nc.gpsimd, step - SUM_LAG)
+            for late_step, what in LATE:
+                if late_step == step:
+                    late_gather(what)
+            for n, group in enumerate(GROUPS):
                 if QUANTISE_STEPS[n] == step:
                     quantise(*group)

@@ -104,16 +104,18 @@ def tile_list_ckg_sig_kernel(
         for window in (rows_e, plane_r):
             nc.gpsimd.memset(window[:, : T // 8], 0)
             nc.vector.memset(window[:, T // 8 :], 0)
-        rows_we = zeroed(nc.vector, "rows_we", 2 * R)
+        rows_wrr = keep.tile([P, R // 4], I32, name="rows_wrr", tag="planes_we", align_bytes=64)
+        nc.vector.memset(rows_wrr[:], 0)
         rows_wri = keep.tile([P, R // 4], I32, name="rows_wri", tag="entity_table", align_bytes=64)
         nc.vector.memset(rows_wri[:], 0)
+        rows_we = zeroed(nc.vector, "rows_we", 2 * R)
         nc.vector.memset(warm[:, 0:1], 0.0)
 
         raw = {}
         nc.sync.dma_start(out=list_r[:], in_=offs2)
         nc.sync.dma_start(out=list_e[:], in_=offs)
         raw["wrr"] = load_bytes(nc.scalar, "wrr", flat_words(wrr_words))
-        load_spread(nc.scalar, rows_we, 0, wrr_scales)
+        load_spread(nc.scalar, rows_wrr, 0, wrr_scales)
         load_spread(nc.scalar, rows_wri, 0, wri_scales)
         load_spread(nc.sync, rows_e, 0, tab_scales)
         for s in range(4):
@@ -142,11 +144,11 @@ def tile_list_ckg_sig_kernel(
 
         reorder_words("wrr", U32, 4)
         planes_wr = sbuf("planes_wr", [P, 2 * R], U8)
-        planes_we = sbuf("planes_we", [P, 2 * R], U8)
-        reorder_scales(planes_wr[:, :R], rows_we[:, : R // 4], ("wrr",))
+        reorder_scales(planes_wr[:, :R], rows_wrr[:], ("wrr",))
         reorder_scales(planes_wr[:, R:], rows_wri[:], ("wri",))
-        load_spread(nc.gpsimd, rows_we, R, wei_scales)
         load_spread(nc.gpsimd, rows_we, 0, wer_scales)
+        load_spread(nc.gpsimd, rows_we, R, wei_scales)
+        planes_we = keep.tile([P, 2 * R], U8, name="planes_we", tag="planes_we", align_bytes=64)
         reorder_scales(planes_we[:], rows_we[:], ("wer", "wei"))
         plane_e01 = zeroed(nc.gpsimd, "plane_e01", 2 * CHUNK)
         plane_e23 = zeroed(nc.gpsimd, "plane_e23", 2 * CHUNK)

@@ -26,7 +26,7 @@ TILE = 128
 TILES = J // TILE
 TILES_PER_CHUNK = CHUNK // TILE
 
-KINDS = "BCBBCABCBBCABCAW"
+KINDS = "BCBBCABCBBCACBAW"
 RELATION_AHEAD = 4
 RELATION_DEPTH = 6
 HELP_AHEAD = 3
@@ -99,16 +99,15 @@ def tile_list_ckg_sig_kernel(
         ident = sbuf("ident", [P, P], F32)
         warm = keep.tile([P, 2], F32, name="warm")
 
-        plane_r = sbuf("plane_r", [P, T // 4], I32)
         rows_e = sbuf("rows_e", [P, T // 4], I32)
-        for window in (rows_e, plane_r):
-            nc.gpsimd.memset(window[:, : T // 8], 0)
-            nc.vector.memset(window[:, T // 8 :], 0)
+        nc.gpsimd.memset(rows_e[:, : 3 * T // 16], 0)
+        nc.vector.memset(rows_e[:, 3 * T // 16 :], 0)
+        plane_r = zeroed(nc.vector, "plane_r", T)
+        rows_we = zeroed(nc.gpsimd, "rows_we", 2 * R)
         rows_wrr = keep.tile([P, R // 4], I32, name="rows_wrr", tag="planes_we", align_bytes=64)
         nc.vector.memset(rows_wrr[:], 0)
         rows_wri = keep.tile([P, R // 4], I32, name="rows_wri", tag="entity_table", align_bytes=64)
         nc.vector.memset(rows_wri[:], 0)
-        rows_we = zeroed(nc.vector, "rows_we", 2 * R)
         nc.vector.memset(warm[:, 0:1], 0.0)
 
         raw = {}
@@ -187,17 +186,15 @@ def tile_list_ckg_sig_kernel(
 
         room_e = keep.tile([P, 2 * CHUNK], U8, name="room_e", tag="room_e", align_bytes=64)
         gather(room_e[:], rows_e, list_e, 0, 2)
-        picked_r = sbuf("picked_r", [P, 3 * CHUNK], U8)
-        gather(picked_r[:], plane_r, list_r, 0, 3)
-        name_scales(picked_r, "r", 0, 3)
+        picked_r = sbuf("picked_r", [P, J], U8)
+        gather(picked_r[:], plane_r, list_r, 0, 4)
+        name_scales(picked_r, "r", 0, 4)
         gather_words("r", 0, word_room("codes_r0"))
         move_rows(nc.sync, plane_e01, room_e[:].bitcast(I32), 0)
         name_scales(plane_e01, "e", 0, 2)
-        room_late = keep.tile([P, 3 * CHUNK], U8, name="room_late", tag="wri", align_bytes=64)
-        gather(room_late[:, : 2 * CHUNK], rows_e, list_e, 2, 2)
-        gather(room_late[:, 2 * CHUNK :], plane_r, list_r, 3, 1)
-        scales["r", 3] = room_late[:, 2 * CHUNK :]
-        move_rows(nc.sync, plane_e23, room_late[:, : 2 * CHUNK].bitcast(I32), 0)
+        room_late = keep.tile([P, 2 * CHUNK], U8, name="room_late", tag="wri", align_bytes=64)
+        gather(room_late[:], rows_e, list_e, 2, 2)
+        move_rows(nc.sync, plane_e23, room_late[:].bitcast(I32), 0)
         name_scales(plane_e23, "e", 2, 2)
         for name in ("wer", "wei"):
             ordered = sbuf(name + "_slots", [P, PACK, R // PACK, 2], U8)

@@ -114,6 +114,8 @@ def tile_list_ckg_sig_kernel(
         nc.sync.dma_start(out=list_r[:], in_=offs2)
         nc.sync.dma_start(out=list_e[:], in_=offs)
         raw["wrr"] = load_bytes(nc.scalar, "wrr", flat_words(wrr_words))
+        raw["wer"] = load_bytes(nc.scalar, "wer", wer_words[0])
+        raw["wei"] = load_bytes(nc.scalar, "wei", wei_words[0])
         load_spread(nc.scalar, rows_wrr, 0, wrr_scales)
         load_spread(nc.scalar, rows_wri, 0, wri_scales)
         load_spread(nc.sync, rows_e, 0, tab_scales)
@@ -142,6 +144,8 @@ def tile_list_ckg_sig_kernel(
                 plane_of[name] = planes[:, n * R : (n + 1) * R]
 
         reorder_words("wrr", U32, 4)
+        reorder_words("wer", U16, 8)
+        reorder_words("wei", U16, 8)
         planes_wr = sbuf("planes_wr", [P, 2 * R], U8)
         reorder_scales(planes_wr[:, :R], rows_wrr[:], ("wrr",))
         reorder_scales(planes_wr[:, R:], rows_wri[:], ("wri",))
@@ -177,8 +181,6 @@ def tile_list_ckg_sig_kernel(
         move_rows(nc.sync, planes_wr[:].bitcast(I32), planes_wr[:].bitcast(I32), 1)
         raw["wri"] = keep.tile([P, 4 * R], U8, name="wri", tag="wri", align_bytes=64)[:]
         nc.sync.dma_start(out=raw["wri"].bitcast(I32), in_=flat_words(wri_words).bitcast(I32))
-        raw["wer"] = load_bytes(nc.sync, "wer", wer_words[0])
-        raw["wei"] = load_bytes(nc.sync, "wei", wei_words[0])
         table_e = keep.tile([P, T], I32, name="table_e", tag="entity_table", align_bytes=64)
         nc.sync.dma_start(out=table_e[:], in_=flat_words(tab_words).bitcast(I32))
         move_rows(nc.sync, planes_we[:].bitcast(I32), planes_we[:].bitcast(I32), 1)
@@ -196,10 +198,6 @@ def tile_list_ckg_sig_kernel(
         gather(room_late[:], rows_e, list_e, 2, 2)
         move_rows(nc.sync, plane_e23, room_late[:].bitcast(I32), 0)
         name_scales(plane_e23, "e", 2, 2)
-        for name in ("wer", "wei"):
-            ordered = sbuf(name + "_slots", [P, PACK, R // PACK, 2], U8)
-            nc.gpsimd.tensor_copy(ordered[:], raw[name].rearrange("p (m t b) -> p t m b", t=PACK, b=2))
-            slots[name] = ordered[:].rearrange("p t m b -> p (t m b)")
         for chunk in range(EARLY_ENTITY):
             gather_words("e", chunk, word_room("codes_e%d" % chunk))
         gather_words("r", 1, keep.tile([P, CHUNK], U32, name="codes_r1", tag="room_e", align_bytes=64)[:])

@@ -26,7 +26,7 @@ TILE = 128
 TILES = J // TILE
 TILES_PER_CHUNK = CHUNK // TILE
 
-KINDS = "BCBBCABCBBCACBAW"
+KINDS = "BCBBCABCBBCACBAV"
 RELATION_AHEAD = 4
 RELATION_DEPTH = 6
 HELP_AHEAD = 3

from contextlib import ExitStack

import concourse.mybir as mybir
from concourse.masks import make_identity

R, N, T, J = 512, 256, 4096, 2048
FLOPS = 5368709120

F32 = mybir.dt.float32
BF16 = mybir.dt.bfloat16
I32 = mybir.dt.int32
U32 = mybir.dt.uint32
U16 = mybir.dt.uint16
U8 = mybir.dt.uint8
FP8X4 = mybir.dt.float8_e4m3fn_x4
FP4X4 = mybir.dt.float4_e2m1fn_x4
MULT = mybir.AluOpType.mult
ADD = mybir.AluOpType.add
SIGMOID = mybir.ActivationFunctionType.Sigmoid

P = 128
PACK = 4
LINE = 16
CHUNK = 512
TILE = 128
TILES = J // TILE
TILES_PER_CHUNK = CHUNK // TILE

KINDS = "BCBBCABCBBCACBAV"
RELATION_AHEAD = 4
RELATION_DEPTH = 6
HELP_AHEAD = 3
AER_DEPTH = 3
REAL_DEPTH = 6
IMAG_DEPTH = 6
SCALAR_BANKS = 4
VECTOR_BANKS = 4
SUM_LAG = 0
STEP_ORDER = "erpst"
GROUPS = ((0, 4), (4, 4), (8, 4), (12, 2), (14, 1), (15, 1))
QUANTISE_STEPS = (7, 11, 14, 16, 17, 18)
SCORE_STEPS = (8, 12, 16, 17, 18, 19)
EARLY_ENTITY = 2
LATE = ((2, ("r", 2, "e", 0)), (3, ("e", 2, "r", 1)), (6, ("r", 3, "e", 1)), (7, ("e", 3, "r", 2)))


def tile_list_ckg_sig_kernel(
    tc, tab_words, tab_scales, tab2_words, tab2_scales, wer_words, wer_scales, wei_words, wei_scales,
    wrr_words, wrr_scales, wri_words, wri_scales, nr_words, nr_scales, ni_words, ni_scales, offs, offs2, out,
):
    nc = tc.nc
    with ExitStack() as ctx:
        keep = ctx.enter_context(tc.tile_pool(name="keep", bufs=1))
        psum = ctx.enter_context(tc.psum_pool(name="psum", bufs=1))

        def sbuf(name, shape, dtype):
            return keep.tile(shape, dtype, name=name, align_bytes=64)

        rings = {}
        uses = {}

        def ring(name, depth, make):
            if name not in rings:
                rings[name] = [make("%s_%d" % (name, n)) for n in range(depth)]
            uses[name] = uses.get(name, -1) + 1
            return rings[name][uses[name] % depth]

        def float_room(name, shape, depth):
            return ring(name, depth, lambda label: sbuf(label, shape, F32))[:]

        def bank(reader):
            depth = SCALAR_BANKS if reader == "scalar" else VECTOR_BANKS
            return ring(reader, depth, lambda label: psum.tile([P, CHUNK], F32, name=label))[:]

        def zeroed(engine, name, columns):
            plane = sbuf(name, [P, columns // 4], I32)
            engine.memset(plane[:], 0)
            return plane

        def flat_words(words):
            return words[0].rearrange("p c i -> p (c i)")

        def load_bytes(queue, name, source):
            tile = sbuf(name, [P, source.shape[1]], U8)
            queue.dma_start(out=tile[:].bitcast(I32), in_=source.bitcast(I32))
            return tile[:]

        def load_spread(queue, plane, first_column, scales):
            rows = scales[0].bitcast(I32)
            queue.dma_start(out=plane[0:P:8, first_column // 4 : first_column // 4 + rows.shape[1]], in_=rows)

        def move_rows(queue, plane, spread, first_row):
            for s in range(first_row, 4):
                queue.dma_start(out=plane[s:P:32, :], in_=spread[8 * s : P : 32, :])

        list_r = keep.tile([P, J // 16], U16, name="list_r")
        list_e = keep.tile([P, J // 16], U16, name="list_e")
        table_r = sbuf("table_r", [P, T], I32)
        ident = sbuf("ident", [P, P], F32)
        warm = keep.tile([P, 2], F32, name="warm")

        rows_e = sbuf("rows_e", [P, T // 4], I32)
        nc.gpsimd.memset(rows_e[:, : 3 * T // 16], 0)
        nc.vector.memset(rows_e[:, 3 * T // 16 :], 0)
        plane_r = zeroed(nc.vector, "plane_r", T)
        rows_we = zeroed(nc.gpsimd, "rows_we", 2 * R)
        rows_wrr = keep.tile([P, R // 4], I32, name="rows_wrr", tag="planes_we", align_bytes=64)
        nc.vector.memset(rows_wrr[:], 0)
        rows_wri = keep.tile([P, R // 4], I32, name="rows_wri", tag="entity_table", align_bytes=64)
        nc.vector.memset(rows_wri[:], 0)
        nc.vector.memset(warm[:, 0:1], 0.0)

        raw = {}
        nc.sync.dma_start(out=list_r[:], in_=offs2)
        nc.sync.dma_start(out=list_e[:], in_=offs)
        raw["wrr"] = load_bytes(nc.scalar, "wrr", flat_words(wrr_words))
        raw["wer"] = load_bytes(nc.scalar, "wer", wer_words[0])
        raw["wei"] = load_bytes(nc.scalar, "wei", wei_words[0])
        load_spread(nc.scalar, rows_wrr, 0, wrr_scales)
        load_spread(nc.scalar, rows_wri, 0, wri_scales)
        load_spread(nc.sync, rows_e, 0, tab_scales)
        for s in range(4):
            nc.sync.dma_start(out=plane_r[s:P:32, :], in_=tab2_scales[0].bitcast(I32)[s:16:4, :])
        nc.sync.dma_start(out=table_r[:], in_=flat_words(tab2_words).bitcast(I32))
        nc.scalar.activation(warm[:, 1:2], warm[:, 0:1], SIGMOID)

        slots = {}
        plane_of = {}

        def reorder_words(name, dtype, run):
            ordered = sbuf(name + "_slots", [P, R], dtype)
            nc.scalar.copy(
                ordered[:].rearrange("p (t c i) -> p c t i", t=PACK, i=run),
                raw[name].bitcast(dtype).rearrange("p (c i t) -> p c t i", i=run, t=PACK),
            )
            slots[name] = ordered[:].bitcast(U8)

        def reorder_scales(planes, rows, names):
            nc.gpsimd.tensor_copy(
                planes.rearrange("p (w t c i) -> p w c t i", w=len(names), t=PACK, i=LINE),
                rows.bitcast(U8).rearrange("p (w c i t) -> p w c t i", w=len(names), i=LINE, t=PACK),
            )
            for n, name in enumerate(names):
                plane_of[name] = planes[:, n * R : (n + 1) * R]

        reorder_words("wrr", U32, 4)
        reorder_words("wer", U16, 8)
        reorder_words("wei", U16, 8)
        planes_wr = sbuf("planes_wr", [P, 2 * R], U8)
        reorder_scales(planes_wr[:, :R], rows_wrr[:], ("wrr",))
        reorder_scales(planes_wr[:, R:], rows_wri[:], ("wri",))
        load_spread(nc.gpsimd, rows_we, 0, wer_scales)
        load_spread(nc.gpsimd, rows_we, R, wei_scales)
        planes_we = keep.tile([P, 2 * R], U8, name="planes_we", tag="planes_we", align_bytes=64)
        reorder_scales(planes_we[:], rows_we[:], ("wer", "wei"))
        plane_e01 = zeroed(nc.gpsimd, "plane_e01", 2 * CHUNK)
        plane_e23 = zeroed(nc.gpsimd, "plane_e23", 2 * CHUNK)
        plane_n = zeroed(nc.gpsimd, "plane_n", 2 * N)
        make_identity(nc, ident[:])
        plane_of["nr"] = plane_n[:].bitcast(U8)[:, :N]
        plane_of["ni"] = plane_n[:].bitcast(U8)[:, N:]

        def gather(into, window, offsets, chunk, count):
            columns = slice(chunk * CHUNK // 16, (chunk + count) * CHUNK // 16)
            nc.vector.tensor_copy(into, window[:].bitcast(into.dtype).indirect(offsets[:, columns]))

        codes = {}
        scales = {}

        def gather_words(side, chunk, into):
            gather(into, table_r if side == "r" else table_e, list_r if side == "r" else list_e, chunk, 1)
            codes[side, chunk] = into

        def name_scales(plane, side, first, count):
            for n in range(count):
                scales[side, first + n] = plane[:].bitcast(U8)[:, n * CHUNK : (n + 1) * CHUNK]

        def word_room(name):
            return sbuf(name, [P, CHUNK], U32)[:]

        move_rows(nc.sync, planes_wr[:].bitcast(I32), planes_wr[:].bitcast(I32), 1)
        raw["wri"] = keep.tile([P, 4 * R], U8, name="wri", tag="wri", align_bytes=64)[:]
        nc.sync.dma_start(out=raw["wri"].bitcast(I32), in_=flat_words(wri_words).bitcast(I32))
        table_e = keep.tile([P, T], I32, name="table_e", tag="entity_table", align_bytes=64)
        nc.sync.dma_start(out=table_e[:], in_=flat_words(tab_words).bitcast(I32))
        move_rows(nc.sync, planes_we[:].bitcast(I32), planes_we[:].bitcast(I32), 1)
        reorder_words("wri", U32, 4)

        room_e = keep.tile([P, 2 * CHUNK], U8, name="room_e", tag="room_e", align_bytes=64)
        gather(room_e[:], rows_e, list_e, 0, 2)
        picked_r = sbuf("picked_r", [P, J], U8)
        gather(picked_r[:], plane_r, list_r, 0, 4)
        name_scales(picked_r, "r", 0, 4)
        gather_words("r", 0, word_room("codes_r0"))
        move_rows(nc.sync, plane_e01, room_e[:].bitcast(I32), 0)
        name_scales(plane_e01, "e", 0, 2)
        room_late = keep.tile([P, 2 * CHUNK], U8, name="room_late", tag="wri", align_bytes=64)
        gather(room_late[:], rows_e, list_e, 2, 2)
        move_rows(nc.sync, plane_e23, room_late[:].bitcast(I32), 0)
        name_scales(plane_e23, "e", 2, 2)
        for chunk in range(EARLY_ENTITY):
            gather_words("e", chunk, word_room("codes_e%d" % chunk))
        gather_words("r", 1, keep.tile([P, CHUNK], U32, name="codes_r1", tag="room_e", align_bytes=64)[:])
        raw["nr"] = load_bytes(nc.sync, "nr", nr_words[0])
        raw["ni"] = load_bytes(nc.sync, "ni", ni_words[0])
        for n, source in enumerate((nr_scales, ni_scales)):
            for s in range(4):
                nc.sync.dma_start(
                    out=plane_n[s:P:32, n * N // 4 : (n + 1) * N // 4], in_=source[0].bitcast(I32)[s:16:4, :]
                )

        def late_gather(what):
            side, chunk, old_side, old_chunk = what
            gather_words(side, chunk, codes[old_side, old_chunk])

        def columns_of(name, first, count):
            if name in ("wrr", "wri"):
                return slots[name][:, 4 * first : 4 * (first + count)].bitcast(FP8X4)
            return slots[name][:, 2 * first : 2 * (first + count)].bitcast(FP4X4)

        def by_channel(i):
            return KINDS[i] in "CVW"

        def helped(i):
            return KINDS[i] in "BW"

        def project(reader, name, i):
            side = name[1]
            chunk, place = divmod(i, TILES_PER_CHUNK)
            tokens = slice(place * TILE, (place + 1) * TILE)
            words = codes[side, chunk][:, tokens].bitcast(FP8X4)
            plane = scales[side, chunk][:, tokens]
            acc = bank(reader)
            if by_channel(i):
                by_slot = acc.rearrange("p (t n) -> p t n", t=PACK)
                for t in range(PACK):
                    nc.tensor.matmul_mx(
                        out=by_slot[:, t, :], lhsT=columns_of(name, t * P, P),
                        lhsT_scale=plane_of[name][:, t * P : (t + 1) * P],
                        rhs=words, rhs_scale=plane, start=True, stop=True,
                    )
                return by_slot.rearrange("p t n -> p n t")
            nc.tensor.matmul_mx(
                out=acc, lhsT=words, lhsT_scale=plane,
                rhs=columns_of(name, 0, R), rhs_scale=plane_of[name], start=True, stop=True,
            )
            return acc

        def like_sums(i, flat):
            return flat.rearrange("p (n t) -> p n t", t=PACK) if by_channel(i) else flat

        rel = {}
        real = {}
        imag = {}
        sums = {}

        def relation(i):
            rel[i] = float_room("rel", [P, 2, R], RELATION_DEPTH)
            for part, name in enumerate(("wrr", "wri")):
                nc.scalar.copy(like_sums(i, rel[i][:, part]), project("scalar", name, i))

        def help_real(i):
            aer = float_room("aer", [P, R], AER_DEPTH)
            nc.scalar.copy(like_sums(i, aer), project("scalar", "wer", i))
            real[i] = float_room("real", [P, 2, R], REAL_DEPTH)
            nc.gpsimd.tensor_tensor(real[i], aer.unsqueeze(1).broadcast_to([P, 2, R]), rel[i], MULT)

        def entity(i):
            sums[i, "wei"] = project("vector", "wei", i)
            if not helped(i):
                sums[i, "wer"] = project("vector", "wer", i)

        def products(i):
            imag[i] = float_room("imag", [P, 2, R], IMAG_DEPTH)
            aei = sums[i, "wei"]
            nc.vector.scalar_tensor_tensor(like_sums(i, imag[i][:, 0]), aei, -1.0, like_sums(i, rel[i][:, 1]), MULT, MULT)
            nc.vector.tensor_tensor(like_sums(i, imag[i][:, 1]), aei, like_sums(i, rel[i][:, 0]), MULT)
            if helped(i):
                return
            real[i] = float_room("real", [P, 2, R], REAL_DEPTH)
            aer = sums[i, "wer"]
            if by_channel(i):
                nc.vector.tensor_tensor(
                    real[i].rearrange("p h (n t) -> p h n t", t=PACK),
                    aer.unsqueeze(1).broadcast_to([P, 2, TILE, PACK]),
                    rel[i].rearrange("p h (n t) -> p h n t", t=PACK), MULT,
                )
            else:
                nc.vector.tensor_tensor(real[i], aer.unsqueeze(1).broadcast_to([P, 2, R]), rel[i], MULT)

        rounded = {first: sbuf("h_%d" % first, [P, 2, count * TILE, PACK], BF16) for first, count in GROUPS}

        def rounded_of(i):
            first = [group[0] for group in GROUPS if group[0] <= i][-1]
            return rounded[first][:, :, (i - first) * TILE : (i - first + 1) * TILE, :]

        def add_terms(engine, i):
            engine.tensor_tensor(rounded_of(i).rearrange("p h n t -> p h (n t)"), real[i], imag[i], ADD)

        def turn(i):
            for part in range(2):
                acc = bank("scalar").rearrange("p (t n) -> p t n", t=PACK)
                for term, prod in enumerate((real[i], imag[i])):
                    for t in range(PACK):
                        nc.tensor.matmul(
                            acc[:, t, :], lhsT=prod[:, part, t * P : (t + 1) * P], rhs=ident[:],
                            start=(term == 0 and t == 0), stop=(term == 1 and t == PACK - 1), is_transpose=True,
                        )
                nc.scalar.copy(rounded_of(i)[:, part], acc.rearrange("p t n -> p n t"))

        packed = {}

        def quantise(first, count):
            width = count * TILE
            h_codes = sbuf("h_codes_%d" % first, [P, 2 * width], U32)
            h_scales = sbuf("h_scales_%d" % first, [P, 2 * width], U8)
            nc.vector.quantize_mx(
                out=h_codes[:].bitcast(FP8X4), scales=h_scales[:],
                in_=rounded[first][:].rearrange("p h n t -> p (h n t)"),
            )
            packed[first] = (h_codes, h_scales)

        def score(first, count):
            width = count * TILE
            h_codes, h_scales = packed[first]
            per_bank = min(2, CHUNK // width)
            for n in range(2 // per_bank):
                acc = bank("scalar")[:, : per_bank * width].rearrange("p (h w) -> p h w", h=per_bank)
                for place in range(per_bank):
                    half = n * per_bank + place
                    for part, name in enumerate(("nr", "ni")):
                        tokens = slice(part * width, (part + 1) * width)
                        nc.tensor.matmul_mx(
                            out=acc[:, place, :],
                            lhsT=raw[name][:, 2 * P * half : 2 * P * (half + 1)].bitcast(FP4X4),
                            lhsT_scale=plane_of[name][:, P * half : P * (half + 1)],
                            rhs=h_codes[:, tokens].bitcast(FP8X4), rhs_scale=h_scales[:, tokens],
                            start=(part == 0), stop=(part == 1),
                        )
                result = sbuf("result_%d_%d" % (first, n), [P, per_bank, width], F32)
                nc.scalar.activation(result[:], acc, SIGMOID)
                rows = out[P * n * per_bank : P * (n + 1) * per_bank, first * TILE : first * TILE + width]
                nc.sync.dma_start(out=rows.rearrange("(h p) n -> p h n", p=P), in_=result[:])

        for i in range(RELATION_AHEAD):
            relation(i)
        for i in range(HELP_AHEAD):
            if helped(i):
                help_real(i)
        entity(0)
        for step in range(max(SCORE_STEPS) + 1):
            for part in STEP_ORDER:
                if part == "e" and step + 1 < TILES:
                    entity(step + 1)
                if part == "r" and step + RELATION_AHEAD < TILES:
                    relation(step + RELATION_AHEAD)
                if part == "p" and step + HELP_AHEAD < TILES and helped(step + HELP_AHEAD):
                    help_real(step + HELP_AHEAD)
                if part == "s":
                    for n, group in enumerate(GROUPS):
                        if SCORE_STEPS[n] == step:
                            score(*group)
                if part == "t" and 1 <= step <= TILES and not by_channel(step - 1):
                    turn(step - 1)
            if step < TILES:
                products(step)
                if KINDS[step] in "VW":
                    add_terms(nc.vector, step)
            if 0 <= step - SUM_LAG < TILES and KINDS[step - SUM_LAG] == "C":
                add_terms(nc.gpsimd, step - SUM_LAG)
            for late_step, what in LATE:
                if late_step == step:
                    late_gather(what)
            for n, group in enumerate(GROUPS):
                if QUANTISE_STEPS[n] == step:
                    quantise(*group)
